import numpy as np
import ml_dtypes


def mxq(x, axis, fmt="e4m3"):
    dtype, down = {"e4m3": (ml_dtypes.float8_e4m3fn, 7), "e5m2": (ml_dtypes.float8_e5m2, 14)}[fmt]
    v = np.moveaxis(np.asarray(x, np.float32).astype(ml_dtypes.bfloat16).astype(np.float64), axis, -1)
    blocks = v.reshape(v.shape[:-1] + (-1, 32))
    amax = np.abs(blocks).max(-1, keepdims=True)
    byte = np.maximum(np.where(amax > 0, np.frexp(amax)[1] - 1 + 127, 0) - down, 1)
    scale = np.exp2(byte - 127.0)
    codes = (blocks / scale).astype(np.float32).astype(dtype).astype(np.float64)
    return np.moveaxis((codes * scale).reshape(v.shape), -1, axis)


WIDE = False


def mx_kscale(k):
    if not WIDE:
        return np.ones(k)
    levels = np.array([10, -10, 5, -5, 0])
    if k % 512:
        return np.exp2(np.random.permutation(np.resize(levels, k // 32))).repeat(32)
    a = np.empty((k // 512, 16))
    for p in range(k // 512):
        a[p, :8] = np.random.permutation(np.resize(levels, 8))
        for g in range(8):
            far = levels[np.abs(levels - a[p, g]) >= 10]
            a[p, g + 8] = far[np.random.randint(len(far))]
    return np.exp2(a.ravel()).repeat(32)


def f64(x):
    return np.asarray(x).astype(np.float64)


def striped(idx):
    return np.tile(idx.reshape(-1, 16).T, (8, 1)).astype(np.uint16)


def unstriped(offs):
    return offs[:16].T.reshape(-1).astype(np.int64)


E2M1 = np.array([0.0, 0.5, 1.0, 1.5, 2.0, 3.0, 4.0, 6.0, -0.0, -0.5, -1.0, -1.5, -2.0, -3.0, -4.0, -6.0])


def pack_weight(w, fmt):
    k, n = w.shape
    w = f64(np.asarray(w, np.float32).astype(ml_dtypes.bfloat16)).reshape(k // 32, 32, n)
    amax = np.abs(w).max(1)
    if fmt == "e4m3":
        byte = np.frexp(amax)[1] - 1 + 127 - 7
    else:
        mant, ex = np.frexp(amax / 6.0)
        byte = np.where(mant > 0.5, ex, ex - 1) + 127
    byte = np.clip(np.where(amax > 0, byte, 1), 1, 254)
    scaled = (w * np.exp2(127.0 - byte)[:, None, :]).reshape(k, n).astype(np.float32)
    by_word = np.ascontiguousarray(scaled.reshape(k // 512, 128, 4, n).transpose(0, 1, 3, 2))
    if fmt == "e4m3":
        words = by_word.astype(ml_dtypes.float8_e4m3fn).view(np.uint8)
    else:
        c = by_word.astype(ml_dtypes.float4_e2m1fn).view(np.uint8) & 0xF
        words = (c[..., 0::2] | (c[..., 1::2] << 4)).reshape(k // 512, 128, 2 * n)
    return np.ascontiguousarray(words), np.ascontiguousarray(byte.astype(np.uint8).reshape(k // 512, 16, n))


def unpack_weight(words, scales, fmt):
    g, _, n = scales.shape
    words = np.ascontiguousarray(words).reshape(g, 128, n, -1)
    if fmt == "e4m3":
        vals = words.view(ml_dtypes.float8_e4m3fn).astype(np.float64)
    else:
        nib = np.empty((g, 128, n, 4), np.uint8)
        nib[..., 0::2] = words & 0xF
        nib[..., 1::2] = words >> 4
        vals = E2M1[nib]
    vals = vals * np.repeat(np.exp2(scales.astype(np.float64) - 127.0), 8, axis=1)[..., None]
    return vals.transpose(0, 1, 3, 2).reshape(g * 512, n)


def gelu(v):
    return 0.5 * v * (1.0 + np.tanh(np.sqrt(2.0 / np.pi) * (v + 0.044715 * v**3)))


K, T, E, C, H, N = 1024, 512, 4, 256, 512, 384


def by_expert(wq, xq):
    return np.concatenate([wq[e].T @ xq[:, e * C:(e + 1) * C] for e in range(E)], axis=1)


def setup_inputs():
    n = np.random.standard_normal
    s = mx_kscale(K)[:, None]
    u = mx_kscale(H)
    first = np.random.permutation(np.repeat(np.arange(E), T // E))
    second = (first + 1 + np.random.permutation(np.repeat(np.arange(E - 1), -(-T // (E - 1)))[:T])) % E
    while np.bincount(second, minlength=E).max() != T // E:
        load = np.bincount(second, minlength=E); hi, lo = int(load.argmax()), int(load.argmin())
        t = np.flatnonzero((second == hi) & (first != lo))[0]; second[t] = lo
    slot_token = np.empty(E * C, np.int64); pos = np.empty((2, T), np.int64); fill = np.zeros(E, np.int64)
    place = np.stack([np.random.permutation(C) for _ in range(E)])
    for r, deal in enumerate((first, second)):
        for t in np.random.permutation(T):
            e = deal[t]; j = e * C + place[e, fill[e]]; fill[e] += 1; slot_token[j] = t; pos[r, t] = j
    g = np.random.uniform(0.2, 0.8, T)
    w1 = [pack_weight(m, "e2m1") for m in n((E, K, H)) / np.sqrt(K) / s[None]]
    w3 = [pack_weight(m, "e2m1") for m in n((E, K, H)) / np.sqrt(K) / s[None] * u[None, None, :]]
    w2 = [pack_weight(m, "e2m1") for m in n((E, H, N)) / np.sqrt(H) / u[None, :, None]]
    w_slot = np.empty(E * C); w_slot[pos[0]] = g; w_slot[pos[1]] = 1.0 - g
    return {
        "xT": (n((K, T)) * s).astype(np.float32),
        "w1_words": np.stack([m[0] for m in w1]),
        "w1_scales": np.stack([m[1] for m in w1]),
        "w3_words": np.stack([m[0] for m in w3]),
        "w3_scales": np.stack([m[1] for m in w3]),
        "w2_words": np.stack([m[0] for m in w2]),
        "w2_scales": np.stack([m[1] for m in w2]),
        "gate": np.tile(w_slot, (K, 1)).astype(np.float32),
        "offs": striped(slot_token),
        "pos1": striped(pos[0]),
        "pos2": striped(pos[1]),
    }


def reference(xT, w1_words, w1_scales, w3_words, w3_scales, w2_words, w2_scales, gate, offs, pos1, pos2):
    idx = unstriped(offs)
    w1 = np.stack([unpack_weight(w1_words[e], w1_scales[e], "e2m1") for e in range(E)])
    w3 = np.stack([unpack_weight(w3_words[e], w3_scales[e], "e2m1") for e in range(E)])
    w2 = np.stack([unpack_weight(w2_words[e], w2_scales[e], "e2m1") for e in range(E)])
    xq = mxq(f64(gate) * f64(xT)[:, idx], 0, "e4m3")
    h = gelu(by_expert(w1, xq))
    h = h * by_expert(w3, xq)
    y = by_expert(w2, mxq(h, 0, "e4m3"))
    return y[:, unstriped(pos1)] + y[:, unstriped(pos2)]

@@ -1,0 +1,287 @@
+from contextlib import ExitStack
+
+import concourse.mybir as mybir
+from concourse.masks import make_identity
+
+K, T, E, C, H, N = 1024, 512, 4, 256, 512, 384
+S = E * C
+P = 128
+PACK = 4
+PASSES = K // (P * PACK)
+TILES = S // P
+NT = N // P
+
+FLOPS = 2 * S * (2 * K * H + H * N)
+BYTES = 4 * K * T + E * (2 * K * H + H * N) // 2 + E * (2 * K * H + H * N) // 32 + 4 * S + 2 * P * (S + 2 * T) // 16 + 4 * N * T
+
+F32 = mybir.dt.float32
+BF16 = mybir.dt.bfloat16
+I32 = mybir.dt.int32
+U32 = mybir.dt.uint32
+U16 = mybir.dt.uint16
+U8 = mybir.dt.uint8
+FP8X4 = mybir.dt.float8_e4m3fn_x4
+FP4X4 = mybir.dt.float4_e2m1fn_x4
+MULT = mybir.AluOpType.mult
+ADD = mybir.AluOpType.add
+GELU = mybir.ActivationFunctionType.Gelu_apprx_tanh
+
+GATHERS = [[(0, 384), (384, 384), (768, 256)], [(0, 384), (384, 384), (768, 128), (896, 128)]]
+
+
+def tile_moe_pre_glu_gelu_kernel(
+    tc, xT, w1_words, w1_scales, w3_words, w3_scales, w2_words, w2_scales, gate, offs, pos1, pos2, out
+):
+    nc = tc.nc
+    with ExitStack() as ctx:
+        keep = ctx.enter_context(tc.tile_pool(name="keep", bufs=1))
+        ring = ctx.enter_context(tc.tile_pool(name="ring", bufs=6))
+        ps_a1 = ctx.enter_context(tc.psum_pool(name="ps_a1", bufs=1))
+        ps_a3 = ctx.enter_context(tc.psum_pool(name="ps_a3", bufs=5))
+        ps_h = ctx.enter_context(tc.psum_pool(name="ps_h", bufs=1))
+        ps_y = ctx.enter_context(tc.psum_pool(name="ps_y", bufs=1))
+
+        offs_sb = keep.tile([P, S // 16], U16, name="offs_sb")
+        pos_sb = [keep.tile([P, T // 16], U16, name=f"pos_sb{r}") for r in range(2)]
+        gate_sb = keep.tile([P, S], F32, name="gate_sb")
+        x_sb = [[keep.tile([P, T], F32, name=f"x_sb{s}{t}") for t in range(PACK)] for s in range(PASSES)]
+        up_words = [[keep.tile([P, PASSES, 2 * H], U8, name=f"up_words{m}{e}", align_bytes=64) for e in range(E)] for m in range(2)]
+        up_scales = [keep.tile([P, E * PASSES, H], U8, name=f"up_scales{m}", align_bytes=64) for m in range(2)]
+        down_words = keep.tile([P, E, 2 * N], U8, name="down_words", align_bytes=64)
+        down_scales = keep.tile([P, E, N], U8, name="down_scales", align_bytes=64)
+        y_sb = keep.tile([P, NT, S], F32, name="y_sb", align_bytes=64)
+        ident = keep.tile([P, P], F32, name="ident")
+
+        zero = keep.tile([P, 1], F32, name="zero")
+        warm = keep.tile([P, 1], F32, name="warm")
+        nc.gpsimd.memset(zero[:], 0.0)
+        nc.scalar.activation(warm[:], zero[:], GELU)
+        for lo, hi in ((0, 4), (4, 8)):
+            for plane in up_scales:
+                nc.gpsimd.memset(plane[:, lo:hi, :].rearrange("p a b -> p (a b)").bitcast(U32), 0)
+        nc.gpsimd.memset(down_scales[:].rearrange("p a b -> p (a b)").bitcast(U32), 0)
+        make_identity(nc, ident[:])
+
+        def load_gate(a, b):
+            nc.sync.dma_start(gate_sb[:, a:b], gate[0:P, a:b])
+
+        def load_x(s, t):
+            rows = xT[s * P * PACK : (s + 1) * P * PACK, :].rearrange("(p t) c -> p t c", t=PACK)
+            nc.sync.dma_start(x_sb[s][t][:], rows[:, t, :])
+
+        def load_scales(plane, scales, lo, hi):
+            rows = scales.rearrange("e s q i -> q (e s) i")
+            for quad in range(4):
+                nc.sync.dma_start(
+                    plane[32 * quad : 32 * quad + 4, lo:hi, :].bitcast(I32),
+                    rows[4 * quad : 4 * quad + 4, lo:hi, :].bitcast(I32),
+                )
+
+        def load_up(e):
+            for m, words in enumerate((w1_words, w3_words)):
+                nc.sync.dma_start(up_words[m][e][:].bitcast(I32), words[e].rearrange("s p b -> p s b").bitcast(I32))
+
+        nc.sync.dma_start(offs_sb[:], offs)
+        load_gate(0, 384)
+        for s in range(PASSES):
+            for t in range(PACK):
+                load_x(s, t)
+        load_gate(384, S)
+        load_scales(up_scales[0], w1_scales, 0, 4)
+        load_scales(up_scales[1], w3_scales, 0, 4)
+        load_up(0)
+        load_up(1)
+        load_scales(down_scales, w2_scales, 0, 4)
+        load_scales(up_scales[0], w1_scales, 4, 8)
+        load_scales(up_scales[1], w3_scales, 4, 8)
+        nc.sync.dma_start(down_words[:].bitcast(I32), w2_words.rearrange("e s p b -> p (e s) b").bitcast(I32))
+        load_up(2)
+        load_up(3)
+        nc.sync.dma_start(pos_sb[0][:], pos1)
+        nc.sync.dma_start(pos_sb[1][:], pos2)
+
+        gathered = [[keep.tile([P, PACK, n], F32, name=f"gathered{s}{c}") for c, (a, n) in enumerate(GATHERS[s])] for s in range(PASSES)]
+        x_bf = [keep.tile([P, S * PACK], BF16, name=f"x_bf{s}", align_bytes=64) for s in range(PASSES)]
+        x_codes = [keep.tile([P, S], U32, name=f"x_codes{s}", align_bytes=64) for s in range(PASSES)]
+        x_scales = [keep.tile([P, S], U8, name=f"x_scales{s}", align_bytes=64) for s in range(PASSES)]
+        a1, a3, act, hid, h_bf, h_codes, h_scales = {}, {}, {}, {}, {}, {}, {}
+
+        def gather(s, c, planes):
+            a, n = GATHERS[s][c]
+            for t in planes:
+                nc.vector.tensor_tensor(
+                    gathered[s][c][:, t, :],
+                    x_sb[s][t][:].indirect(offs_sb[:, a // 16 : (a + n) // 16]),
+                    gate_sb[:, a : a + n],
+                    MULT,
+                )
+
+        def interleave(s, j0, j1, engine_copy):
+            c = max(i for i, (a, n) in enumerate(GATHERS[s]) if a <= j0 * P)
+            a = GATHERS[s][c][0]
+            engine_copy(
+                x_bf[s][:, j0 * P * PACK : j1 * P * PACK].rearrange("p (c i t) -> p c t i", i=4, t=PACK),
+                gathered[s][c][:, :, j0 * P - a : j1 * P - a].rearrange("p t (c i) -> p c t i", i=4),
+            )
+
+        def quantize_x(s, j0, j1):
+            cols = slice(j0 * P, j1 * P)
+            nc.vector.quantize_mx(
+                out=x_codes[s][:, cols].bitcast(FP8X4),
+                scales=x_scales[s][:, cols],
+                in_=x_bf[s][:, j0 * P * PACK : j1 * P * PACK],
+            )
+
+        def up(j, m, s):
+            cols = slice(j * P, (j + 1) * P)
+            e = j * P // C
+            if s == 0 and m == 0:
+                a1[j] = ps_a1.tile([P, H], F32, name="a1")
+            if s == 0 and m == 1:
+                a3[j] = ps_a3.tile([P, H], F32, name="a3")
+            nc.tensor.matmul_mx(
+                out=(a1, a3)[m][j][:],
+                lhsT=x_codes[s][:, cols].bitcast(FP8X4),
+                lhsT_scale=x_scales[s][:, cols],
+                rhs=up_words[m][e][:, s, :].bitcast(FP4X4),
+                rhs_scale=up_scales[m][:, e * PASSES + s, :],
+                start=(s == 0),
+                stop=(s == PASSES - 1),
+            )
+
+        def by_half(bank):
+            return bank[:].rearrange("q (p u v) -> q u p v", u=2, v=2)
+
+        def gelu(j):
+            act[j] = ring.tile([P, H], F32, name="act")
+            nc.scalar.activation(act[j][:].rearrange("q (u p v) -> q u p v", u=2, v=2), by_half(a1[j]), GELU)
+
+        def product(j):
+            hid[j] = ring.tile([P, H], BF16, name="hid", align_bytes=64)
+            nc.vector.tensor_tensor(
+                hid[j][:].rearrange("q (u p v) -> q u p v", u=2, v=2),
+                by_half(a3[j]),
+                act[j][:].rearrange("q (u p v) -> q u p v", u=2, v=2),
+                MULT,
+            )
+
+        def turn(j):
+            turned = ps_h.tile([P, 2, P], F32, name="turned")
+            words = hid[j][:].bitcast(F32)
+            for u in range(2):
+                nc.tensor.transpose(turned[:, u, :], words[:, u * P : (u + 1) * P], ident[:])
+            h_bf[j] = ring.tile([P, P * PACK], BF16, name="h_bf", align_bytes=64)
+            nc.scalar.copy(
+                h_bf[j][:].bitcast(F32).rearrange("p (r u) -> p r u", u=2), turned[:].rearrange("p u r -> p r u")
+            )
+
+        def quantize_h(j):
+            h_codes[j] = ring.tile([P, P], U32, name="h_codes", align_bytes=64)
+            h_scales[j] = ring.tile([P, P], U8, name="h_scales", align_bytes=64)
+            nc.vector.quantize_mx(out=h_codes[j][:].bitcast(FP8X4), scales=h_scales[j][:], in_=h_bf[j][:])
+
+        def down(j):
+            e = j * P // C
+            y_ps = ps_y.tile([P, NT, P], F32, name="y_ps")
+            for m in range(NT):
+                nc.tensor.matmul_mx(
+                    out=y_ps[:, m, :],
+                    lhsT=down_words[:, e, 2 * m * P : 2 * (m + 1) * P].bitcast(FP4X4),
+                    lhsT_scale=down_scales[:, e, m * P : (m + 1) * P],
+                    rhs=h_codes[j][:].bitcast(FP8X4),
+                    rhs_scale=h_scales[j][:],
+                    start=True,
+                    stop=True,
+                )
+            nc.scalar.copy(y_sb[:, :, j * P : (j + 1) * P], y_ps[:])
+
+        def up_and_gelu(j):
+            up(j, 0, 0)
+            up(j, 0, 1)
+            gelu(j)
+            up(j, 1, 0)
+            up(j, 1, 1)
+
+        def product_and_turn(j):
+            product(j)
+            turn(j)
+
+        def finish(j):
+            quantize_h(j)
+            down(j)
+
+        gather(0, 0, range(0, 4))
+        interleave(0, 0, 2, nc.scalar.copy)
+        interleave(0, 2, 3, nc.scalar.copy)
+        gather(1, 0, range(0, 2))
+        quantize_x(0, 0, 2)
+        gather(1, 0, range(2, 3))
+        quantize_x(0, 2, 3)
+        gather(1, 0, range(3, 4))
+        interleave(1, 0, 2, nc.scalar.copy)
+        interleave(1, 2, 3, nc.scalar.copy)
+        gather(0, 1, range(0, 2))
+        quantize_x(1, 0, 2)
+        up_and_gelu(0)
+        up_and_gelu(1)
+        gather(0, 1, range(2, 3))
+        quantize_x(1, 2, 3)
+        up_and_gelu(2)
+        gather(0, 1, range(3, 4))
+        interleave(0, 3, 5, nc.scalar.copy)
+        interleave(0, 5, 6, nc.scalar.copy)
+        gather(1, 1, range(0, 1))
+        product_and_turn(0)
+        gather(1, 1, range(1, 2))
+        quantize_x(0, 3, 5)
+        product_and_turn(1)
+        gather(1, 1, range(2, 3))
+        quantize_x(0, 5, 6)
+        finish(0)
+        gather(1, 1, range(3, 4))
+        interleave(1, 3, 5, nc.scalar.copy)
+        interleave(1, 5, 6, nc.scalar.copy)
+        product_and_turn(2)
+        finish(1)
+        gather(0, 2, range(0, 2))
+        quantize_x(1, 3, 5)
+        up_and_gelu(3)
+        up_and_gelu(4)
+        gather(0, 2, range(2, 3))
+        quantize_x(1, 5, 6)
+        up_and_gelu(5)
+        finish(2)
+        gather(0, 2, range(3, 4))
+        interleave(0, 6, 8, nc.scalar.copy)
+        gather(1, 2, range(0, 4))
+        interleave(1, 6, 7, nc.scalar.copy)
+        quantize_x(0, 6, 8)
+        gather(1, 3, range(0, 4))
+        interleave(1, 7, 8, nc.scalar.copy)
+        quantize_x(1, 6, 7)
+        up_and_gelu(6)
+        up(7, 0, 0)
+        up(7, 1, 0)
+        quantize_x(1, 7, 8)
+        up(7, 0, 1)
+        gelu(7)
+        up(7, 1, 1)
+        product_and_turn(3)
+        product_and_turn(4)
+        finish(3)
+        product_and_turn(5)
+        finish(4)
+        product_and_turn(6)
+        finish(5)
+        product_and_turn(7)
+        finish(6)
+        finish(7)
+
+        for m, lo, hi in ((0, 0, T), (1, 0, T), (2, 0, T // 2), (2, T // 2, T)):
+            first = ring.tile([P, hi - lo], F32, name="first")
+            second = ring.tile([P, hi - lo], F32, name="second")
+            total = ring.tile([P, hi - lo], F32, name="total")
+            nc.vector.tensor_copy(first[:], y_sb[:, m, :].indirect(pos_sb[0][:, lo // 16 : hi // 16]))
+            nc.vector.tensor_copy(second[:], y_sb[:, m, :].indirect(pos_sb[1][:, lo // 16 : hi // 16]))
+            nc.vector.tensor_tensor(total[:], first[:], second[:], ADD)
+            nc.sync.dma_start(out[m * P : (m + 1) * P, lo:hi], total[:])

@@ -10,6 +10,7 @@ PACK = 4
 PASSES = K // (P * PACK)
 TILES = S // P
 NT = N // P
+LAST = TILES - 1
 
 FLOPS = 2 * S * (2 * K * H + H * N)
 BYTES = 4 * K * T + E * (2 * K * H + H * N) // 2 + E * (2 * K * H + H * N) // 32 + 4 * S + 2 * P * (S + 2 * T) // 16 + 4 * N * T
@@ -26,8 +27,6 @@ MULT = mybir.AluOpType.mult
 ADD = mybir.AluOpType.add
 GELU = mybir.ActivationFunctionType.Gelu_apprx_tanh
 
-GATHERS = [[(0, 384), (384, 384), (768, 256)], [(0, 384), (384, 384), (768, 128), (896, 128)]]
-
 
 def tile_moe_pre_glu_gelu_kernel(
     tc, xT, w1_words, w1_scales, w3_words, w3_scales, w2_words, w2_scales, gate, offs, pos1, pos2, out
@@ -35,11 +34,8 @@ def tile_moe_pre_glu_gelu_kernel(
     nc = tc.nc
     with ExitStack() as ctx:
         keep = ctx.enter_context(tc.tile_pool(name="keep", bufs=1))
-        ring = ctx.enter_context(tc.tile_pool(name="ring", bufs=6))
-        ps_a1 = ctx.enter_context(tc.psum_pool(name="ps_a1", bufs=1))
-        ps_a3 = ctx.enter_context(tc.psum_pool(name="ps_a3", bufs=5))
-        ps_h = ctx.enter_context(tc.psum_pool(name="ps_h", bufs=1))
-        ps_y = ctx.enter_context(tc.psum_pool(name="ps_y", bufs=1))
+        stage = ctx.enter_context(tc.tile_pool(name="stage", bufs=2))
+        psum = ctx.enter_context(tc.psum_pool(name="psum", bufs=1))
 
         offs_sb = keep.tile([P, S // 16], U16, name="offs_sb")
         pos_sb = [keep.tile([P, T // 16], U16, name=f"pos_sb{r}") for r in range(2)]
@@ -49,6 +45,14 @@ def tile_moe_pre_glu_gelu_kernel(
         up_scales = [keep.tile([P, E * PASSES, H], U8, name=f"up_scales{m}", align_bytes=64) for m in range(2)]
         down_words = keep.tile([P, E, 2 * N], U8, name="down_words", align_bytes=64)
         down_scales = keep.tile([P, E, N], U8, name="down_scales", align_bytes=64)
+        x_bf = [keep.tile([P, S * PACK], BF16, name=f"x_bf{s}", align_bytes=64) for s in range(PASSES)]
+        x_codes = [keep.tile([P, S], U32, name=f"x_codes{s}", align_bytes=64) for s in range(PASSES)]
+        x_scales = [keep.tile([P, S], U8, name=f"x_scales{s}", align_bytes=64) for s in range(PASSES)]
+        act = [keep.tile([P, 2, P, 2], F32, name=f"act{j}") for j in range(TILES)]
+        hid = [keep.tile([P, 2, P, 2], BF16, name=f"hid{j}") for j in range(TILES)]
+        h_bf = [keep.tile([P, P * PACK], BF16, name=f"h_bf{j}", align_bytes=64) for j in range(TILES)]
+        h_codes = [keep.tile([P, P], U32, name=f"h_codes{j}", align_bytes=64) for j in range(TILES)]
+        h_scales = [keep.tile([P, P], U8, name=f"h_scales{j}", align_bytes=64) for j in range(TILES)]
         y_sb = keep.tile([P, NT, S], F32, name="y_sb", align_bytes=64)
         ident = keep.tile([P, P], F32, name="ident")
 
@@ -62,127 +66,116 @@ def tile_moe_pre_glu_gelu_kernel(
         nc.gpsimd.memset(down_scales[:].rearrange("p a b -> p (a b)").bitcast(U32), 0)
         make_identity(nc, ident[:])
 
-        def load_gate(a, b):
-            nc.sync.dma_start(gate_sb[:, a:b], gate[0:P, a:b])
+        def load_gate(queue, a, b):
+            queue.dma_start(gate_sb[:, a:b], gate[0:P, a:b])
 
-        def load_x(s, t):
+        def load_x(queue, s, t):
             rows = xT[s * P * PACK : (s + 1) * P * PACK, :].rearrange("(p t) c -> p t c", t=PACK)
-            nc.sync.dma_start(x_sb[s][t][:], rows[:, t, :])
+            queue.dma_start(x_sb[s][t][:], rows[:, t, :])
 
-        def load_scales(plane, scales, lo, hi):
+        def load_scales(queue, plane, scales, lo, hi):
             rows = scales.rearrange("e s q i -> q (e s) i")
             for quad in range(4):
-                nc.sync.dma_start(
+                queue.dma_start(
                     plane[32 * quad : 32 * quad + 4, lo:hi, :].bitcast(I32),
                     rows[4 * quad : 4 * quad + 4, lo:hi, :].bitcast(I32),
                 )
 
-        def load_up(e):
-            for m, words in enumerate((w1_words, w3_words)):
-                nc.sync.dma_start(up_words[m][e][:].bitcast(I32), words[e].rearrange("s p b -> p s b").bitcast(I32))
+        def load_up(queue, m, e):
+            words = (w1_words, w3_words)[m]
+            queue.dma_start(up_words[m][e][:].bitcast(I32), words[e].rearrange("s p b -> p s b").bitcast(I32))
 
         nc.sync.dma_start(offs_sb[:], offs)
-        load_gate(0, 384)
+        load_gate(nc.scalar, 0, 3 * P)
         for s in range(PASSES):
             for t in range(PACK):
-                load_x(s, t)
-        load_gate(384, S)
-        load_scales(up_scales[0], w1_scales, 0, 4)
-        load_scales(up_scales[1], w3_scales, 0, 4)
-        load_up(0)
-        load_up(1)
-        load_scales(down_scales, w2_scales, 0, 4)
-        load_scales(up_scales[0], w1_scales, 4, 8)
-        load_scales(up_scales[1], w3_scales, 4, 8)
+                load_x((nc.sync, nc.scalar)[t % 2], s, t)
+        load_scales(nc.sync, up_scales[0], w1_scales, 0, 4)
+        load_scales(nc.scalar, up_scales[1], w3_scales, 0, 4)
+        load_gate(nc.sync, 3 * P, S)
+        load_up(nc.sync, 0, 0)
+        load_up(nc.scalar, 1, 0)
+        load_up(nc.sync, 0, 1)
+        load_up(nc.sync, 1, 1)
+        load_scales(nc.sync, down_scales, w2_scales, 0, 4)
         nc.sync.dma_start(down_words[:].bitcast(I32), w2_words.rearrange("e s p b -> p (e s) b").bitcast(I32))
-        load_up(2)
-        load_up(3)
+        load_scales(nc.sync, up_scales[0], w1_scales, 4, 8)
+        load_scales(nc.sync, up_scales[1], w3_scales, 4, 8)
+        for e in (2, 3):
+            load_up(nc.sync, 0, e)
+            load_up(nc.sync, 1, e)
         nc.sync.dma_start(pos_sb[0][:], pos1)
         nc.sync.dma_start(pos_sb[1][:], pos2)
 
-        gathered = [[keep.tile([P, PACK, n], F32, name=f"gathered{s}{c}") for c, (a, n) in enumerate(GATHERS[s])] for s in range(PASSES)]
-        x_bf = [keep.tile([P, S * PACK], BF16, name=f"x_bf{s}", align_bytes=64) for s in range(PASSES)]
-        x_codes = [keep.tile([P, S], U32, name=f"x_codes{s}", align_bytes=64) for s in range(PASSES)]
-        x_scales = [keep.tile([P, S], U8, name=f"x_scales{s}", align_bytes=64) for s in range(PASSES)]
-        a1, a3, act, hid, h_bf, h_codes, h_scales = {}, {}, {}, {}, {}, {}, {}
-
-        def gather(s, c, planes):
-            a, n = GATHERS[s][c]
-            for t in planes:
+        def gather_and_quantize(s, j0, j1):
+            n = (j1 - j0) * P
+            slots = slice(j0 * P, j1 * P)
+            gathered = stage.tile([P, PACK, n], F32, name="gathered")
+            for t in range(PACK):
                 nc.vector.tensor_tensor(
-                    gathered[s][c][:, t, :],
-                    x_sb[s][t][:].indirect(offs_sb[:, a // 16 : (a + n) // 16]),
-                    gate_sb[:, a : a + n],
+                    gathered[:, t, :],
+                    x_sb[s][t][:].indirect(offs_sb[:, j0 * P // 16 : j1 * P // 16]),
+                    gate_sb[:, slots],
                     MULT,
                 )
+            for a in range(j0, j1, 2):
+                b = min(a + 2, j1)
+                rounded = x_bf[s][:, a * P * PACK : b * P * PACK]
+                copy = nc.vector.tensor_copy if (s, a) == (PASSES - 1, LAST) else nc.scalar.copy
+                copy(
+                    rounded.rearrange("p (c i t) -> p c t i", i=4, t=PACK),
+                    gathered[:, :, (a - j0) * P : (b - j0) * P].rearrange("p t (c i) -> p c t i", i=4),
+                )
+                nc.vector.quantize_mx(
+                    out=x_codes[s][:, a * P : b * P].bitcast(FP8X4), scales=x_scales[s][:, a * P : b * P], in_=rounded
+                )
 
-        def interleave(s, j0, j1, engine_copy):
-            c = max(i for i, (a, n) in enumerate(GATHERS[s]) if a <= j0 * P)
-            a = GATHERS[s][c][0]
-            engine_copy(
-                x_bf[s][:, j0 * P * PACK : j1 * P * PACK].rearrange("p (c i t) -> p c t i", i=4, t=PACK),
-                gathered[s][c][:, :, j0 * P - a : j1 * P - a].rearrange("p t (c i) -> p c t i", i=4),
-            )
+        def own_bank(j, shape, name):
+            return psum.tile(shape, F32, name=name, tag=f"bank{2 + j % 6}")
 
-        def quantize_x(s, j0, j1):
-            cols = slice(j0 * P, j1 * P)
-            nc.vector.quantize_mx(
-                out=x_codes[s][:, cols].bitcast(FP8X4),
-                scales=x_scales[s][:, cols],
-                in_=x_bf[s][:, j0 * P * PACK : j1 * P * PACK],
-            )
-
-        def up(j, m, s):
-            cols = slice(j * P, (j + 1) * P)
-            e = j * P // C
-            if s == 0 and m == 0:
-                a1[j] = ps_a1.tile([P, H], F32, name="a1")
-            if s == 0 and m == 1:
-                a3[j] = ps_a3.tile([P, H], F32, name="a3")
-            nc.tensor.matmul_mx(
-                out=(a1, a3)[m][j][:],
-                lhsT=x_codes[s][:, cols].bitcast(FP8X4),
-                lhsT_scale=x_scales[s][:, cols],
-                rhs=up_words[m][e][:, s, :].bitcast(FP4X4),
-                rhs_scale=up_scales[m][:, e * PASSES + s, :],
-                start=(s == 0),
-                stop=(s == PASSES - 1),
-            )
+        def halves(j):
+            return ((0, 1), (1, 2)) if j == LAST else ((0, 2),)
 
         def by_half(bank):
             return bank[:].rearrange("q (p u v) -> q u p v", u=2, v=2)
 
-        def gelu(j):
-            act[j] = ring.tile([P, H], F32, name="act")
-            nc.scalar.activation(act[j][:].rearrange("q (u p v) -> q u p v", u=2, v=2), by_half(a1[j]), GELU)
+        a3 = {}
 
-        def product(j):
-            hid[j] = ring.tile([P, H], BF16, name="hid", align_bytes=64)
-            nc.vector.tensor_tensor(
-                hid[j][:].rearrange("q (u p v) -> q u p v", u=2, v=2),
-                by_half(a3[j]),
-                act[j][:].rearrange("q (u p v) -> q u p v", u=2, v=2),
-                MULT,
-            )
+        def up(j):
+            cols = slice(j * P, (j + 1) * P)
+            e = j * P // C
+            a1 = psum.tile([P, H], F32, name="a1", tag=f"bank{j % 2}")
+            a3[j] = own_bank(j, [P, H], "a3")
+            for m, acc in enumerate((a1, a3[j])):
+                for s in range(PASSES):
+                    nc.tensor.matmul_mx(
+                        out=acc[:],
+                        lhsT=x_codes[s][:, cols].bitcast(FP8X4),
+                        lhsT_scale=x_scales[s][:, cols],
+                        rhs=up_words[m][e][:, s, :].bitcast(FP4X4),
+                        rhs_scale=up_scales[m][:, e * PASSES + s, :],
+                        start=(s == 0),
+                        stop=(s == PASSES - 1),
+                    )
+                if m == 0:
+                    for lo, hi in halves(j):
+                        nc.scalar.activation(act[j][:, lo:hi], by_half(a1)[:, lo:hi], GELU)
 
-        def turn(j):
-            turned = ps_h.tile([P, 2, P], F32, name="turned")
-            words = hid[j][:].bitcast(F32)
+        def product_and_turn(j):
+            for lo, hi in halves(j):
+                nc.vector.tensor_tensor(hid[j][:, lo:hi], by_half(a3[j])[:, lo:hi], act[j][:, lo:hi], MULT)
+            turned = own_bank(j, [P, 2, P], "turned")
+            words = hid[j][:].rearrange("q u p v -> q (u p v)").bitcast(F32)
             for u in range(2):
                 nc.tensor.transpose(turned[:, u, :], words[:, u * P : (u + 1) * P], ident[:])
-            h_bf[j] = ring.tile([P, P * PACK], BF16, name="h_bf", align_bytes=64)
             nc.scalar.copy(
                 h_bf[j][:].bitcast(F32).rearrange("p (r u) -> p r u", u=2), turned[:].rearrange("p u r -> p r u")
             )
 
-        def quantize_h(j):
-            h_codes[j] = ring.tile([P, P], U32, name="h_codes", align_bytes=64)
-            h_scales[j] = ring.tile([P, P], U8, name="h_scales", align_bytes=64)
-            nc.vector.quantize_mx(out=h_codes[j][:].bitcast(FP8X4), scales=h_scales[j][:], in_=h_bf[j][:])
-
         def down(j):
             e = j * P // C
-            y_ps = ps_y.tile([P, NT, P], F32, name="y_ps")
+            nc.vector.quantize_mx(out=h_codes[j][:].bitcast(FP8X4), scales=h_scales[j][:], in_=h_bf[j][:])
+            y_ps = own_bank(j, [P, NT, P], "y_ps")
             for m in range(NT):
                 nc.tensor.matmul_mx(
                     out=y_ps[:, m, :],
@@ -193,94 +186,36 @@ def tile_moe_pre_glu_gelu_kernel(
                     start=True,
                     stop=True,
                 )
-            nc.scalar.copy(y_sb[:, :, j * P : (j + 1) * P], y_ps[:])
+            if j == LAST:
+                nc.vector.tensor_copy(y_sb[:, :, j * P : (j + 1) * P], y_ps[:])
+            else:
+                nc.scalar.copy(y_sb[:, :, j * P : (j + 1) * P], y_ps[:])
 
-        def up_and_gelu(j):
-            up(j, 0, 0)
-            up(j, 0, 1)
-            gelu(j)
-            up(j, 1, 0)
-            up(j, 1, 1)
-
-        def product_and_turn(j):
-            product(j)
-            turn(j)
-
-        def finish(j):
-            quantize_h(j)
+        gather_and_quantize(0, 0, 3)
+        gather_and_quantize(1, 0, 3)
+        for j in range(0, 3):
+            up(j)
+        for j in range(0, 3):
+            product_and_turn(j)
+            down(j)
+        gather_and_quantize(0, 3, 6)
+        gather_and_quantize(1, 3, 6)
+        for j in range(3, 6):
+            up(j)
+        gather_and_quantize(0, 6, 8)
+        gather_and_quantize(1, 6, 7)
+        gather_and_quantize(1, 7, 8)
+        for j in range(6, 8):
+            up(j)
+        for j in range(3, 8):
+            product_and_turn(j)
+        for j in range(3, 8):
             down(j)
 
-        gather(0, 0, range(0, 4))
-        interleave(0, 0, 2, nc.scalar.copy)
-        interleave(0, 2, 3, nc.scalar.copy)
-        gather(1, 0, range(0, 2))
-        quantize_x(0, 0, 2)
-        gather(1, 0, range(2, 3))
-        quantize_x(0, 2, 3)
-        gather(1, 0, range(3, 4))
-        interleave(1, 0, 2, nc.scalar.copy)
-        interleave(1, 2, 3, nc.scalar.copy)
-        gather(0, 1, range(0, 2))
-        quantize_x(1, 0, 2)
-        up_and_gelu(0)
-        up_and_gelu(1)
-        gather(0, 1, range(2, 3))
-        quantize_x(1, 2, 3)
-        up_and_gelu(2)
-        gather(0, 1, range(3, 4))
-        interleave(0, 3, 5, nc.scalar.copy)
-        interleave(0, 5, 6, nc.scalar.copy)
-        gather(1, 1, range(0, 1))
-        product_and_turn(0)
-        gather(1, 1, range(1, 2))
-        quantize_x(0, 3, 5)
-        product_and_turn(1)
-        gather(1, 1, range(2, 3))
-        quantize_x(0, 5, 6)
-        finish(0)
-        gather(1, 1, range(3, 4))
-        interleave(1, 3, 5, nc.scalar.copy)
-        interleave(1, 5, 6, nc.scalar.copy)
-        product_and_turn(2)
-        finish(1)
-        gather(0, 2, range(0, 2))
-        quantize_x(1, 3, 5)
-        up_and_gelu(3)
-        up_and_gelu(4)
-        gather(0, 2, range(2, 3))
-        quantize_x(1, 5, 6)
-        up_and_gelu(5)
-        finish(2)
-        gather(0, 2, range(3, 4))
-        interleave(0, 6, 8, nc.scalar.copy)
-        gather(1, 2, range(0, 4))
-        interleave(1, 6, 7, nc.scalar.copy)
-        quantize_x(0, 6, 8)
-        gather(1, 3, range(0, 4))
-        interleave(1, 7, 8, nc.scalar.copy)
-        quantize_x(1, 6, 7)
-        up_and_gelu(6)
-        up(7, 0, 0)
-        up(7, 1, 0)
-        quantize_x(1, 7, 8)
-        up(7, 0, 1)
-        gelu(7)
-        up(7, 1, 1)
-        product_and_turn(3)
-        product_and_turn(4)
-        finish(3)
-        product_and_turn(5)
-        finish(4)
-        product_and_turn(6)
-        finish(5)
-        product_and_turn(7)
-        finish(6)
-        finish(7)
-
-        for m, lo, hi in ((0, 0, T), (1, 0, T), (2, 0, T // 2), (2, T // 2, T)):
-            first = ring.tile([P, hi - lo], F32, name="first")
-            second = ring.tile([P, hi - lo], F32, name="second")
-            total = ring.tile([P, hi - lo], F32, name="total")
+        for piece, (m, lo, hi) in enumerate(((0, 0, T), (1, 0, T), (2, 0, T // 2), (2, T // 2, T))):
+            first = keep.tile([P, hi - lo], F32, name=f"first{piece}")
+            second = keep.tile([P, hi - lo], F32, name=f"second{piece}")
+            total = keep.tile([P, hi - lo], F32, name=f"total{piece}")
             nc.vector.tensor_copy(first[:], y_sb[:, m, :].indirect(pos_sb[0][:, lo // 16 : hi // 16]))
             nc.vector.tensor_copy(second[:], y_sb[:, m, :].indirect(pos_sb[1][:, lo // 16 : hi // 16]))
             nc.vector.tensor_tensor(total[:], first[:], second[:], ADD)

@@ -218,5 +218,5 @@ def tile_moe_pre_glu_gelu_kernel(
             total = keep.tile([P, hi - lo], F32, name=f"total{piece}")
             nc.vector.tensor_copy(first[:], y_sb[:, m, :].indirect(pos_sb[0][:, lo // 16 : hi // 16]))
             nc.vector.tensor_copy(second[:], y_sb[:, m, :].indirect(pos_sb[1][:, lo // 16 : hi // 16]))
-            nc.vector.tensor_tensor(total[:], first[:], second[:], ADD)
+            (nc.vector if piece == 3 else nc.gpsimd).tensor_tensor(total[:], first[:], second[:], ADD)
             nc.sync.dma_start(out[m * P : (m + 1) * P, lo:hi], total[:])

@@ -9,11 +9,13 @@ P = 128
 PACK = 4
 PASSES = K // (P * PACK)
 TILES = S // P
-NT = N // P
+ROW_TILES = N // P
 LAST = TILES - 1
+LIST_ROWS = 16
 
+WEIGHTS = E * (2 * K * H + H * N)
 FLOPS = 2 * S * (2 * K * H + H * N)
-BYTES = 4 * K * T + E * (2 * K * H + H * N) // 2 + E * (2 * K * H + H * N) // 32 + 4 * S + 2 * P * (S + 2 * T) // 16 + 4 * N * T
+BYTES = 4 * K * T + WEIGHTS // 2 + WEIGHTS // 32 + 4 * S + 2 * P * (S + 2 * T) // LIST_ROWS + 4 * N * T
 
 F32 = mybir.dt.float32
 BF16 = mybir.dt.bfloat16
@@ -27,6 +29,16 @@ MULT = mybir.AluOpType.mult
 ADD = mybir.AluOpType.add
 GELU = mybir.ActivationFunctionType.Gelu_apprx_tanh
 
+W1, W3 = 0, 1
+
+W1_BANK = (0, 1, 3, 3, 7, 3, 0, 5)
+W3_BANK = (0, 3, 4, 1, 6, 4, 2, 3)
+TURNED_BANK = (2, 3, 4, 6, 7, 4, 2, 3)
+Y_BANK = (2, 7, 4, 5, 6, 7, 2, 3)
+Y_COPY_ON_VECTOR = (5, LAST)
+OUT_PIECES = ((0, 0, T), (1, 0, T), (2, 0, T // 2), (2, T // 2, T - P), (2, T - P, T))
+FIRST_GATE = 3 * P
+
 
 def tile_moe_pre_glu_gelu_kernel(
     tc, xT, w1_words, w1_scales, w3_words, w3_scales, w2_words, w2_scales, gate, offs, pos1, pos2, out
@@ -37,47 +49,51 @@ def tile_moe_pre_glu_gelu_kernel(
         stage = ctx.enter_context(tc.tile_pool(name="stage", bufs=2))
         psum = ctx.enter_context(tc.psum_pool(name="psum", bufs=1))
 
-        offs_sb = keep.tile([P, S // 16], U16, name="offs_sb")
-        pos_sb = [keep.tile([P, T // 16], U16, name=f"pos_sb{r}") for r in range(2)]
+        offs_sb = keep.tile([P, S // LIST_ROWS], U16, name="offs_sb")
+        pos_sb = [keep.tile([P, T // LIST_ROWS], U16, name=f"pos_sb{r}") for r in range(2)]
         gate_sb = keep.tile([P, S], F32, name="gate_sb")
-        x_sb = [[keep.tile([P, T], F32, name=f"x_sb{s}{t}") for t in range(PACK)] for s in range(PASSES)]
-        up_words = [[keep.tile([P, PASSES, 2 * H], U8, name=f"up_words{m}{e}", align_bytes=64) for e in range(E)] for m in range(2)]
-        up_scales = [keep.tile([P, E * PASSES, H], U8, name=f"up_scales{m}", align_bytes=64) for m in range(2)]
+        window = [[keep.tile([P, T], F32, name=f"window{s}{t}") for t in range(PACK)] for s in range(PASSES)]
+        up_words = [
+            [keep.tile([P, PASSES, 2 * H], U8, name=f"up_words{m}{e}", align_bytes=64) for e in range(E)]
+            for m in (W1, W3)
+        ]
+        up_scales = [keep.tile([P, E * PASSES, H], U8, name=f"up_scales{m}", align_bytes=64) for m in (W1, W3)]
         down_words = keep.tile([P, E, 2 * N], U8, name="down_words", align_bytes=64)
         down_scales = keep.tile([P, E, N], U8, name="down_scales", align_bytes=64)
         x_bf = [keep.tile([P, S * PACK], BF16, name=f"x_bf{s}", align_bytes=64) for s in range(PASSES)]
         x_codes = [keep.tile([P, S], U32, name=f"x_codes{s}", align_bytes=64) for s in range(PASSES)]
         x_scales = [keep.tile([P, S], U8, name=f"x_scales{s}", align_bytes=64) for s in range(PASSES)]
         act = [keep.tile([P, 2, P, 2], F32, name=f"act{j}") for j in range(TILES)]
-        hid = [keep.tile([P, 2, P, 2], BF16, name=f"hid{j}") for j in range(TILES)]
         h_bf = [keep.tile([P, P * PACK], BF16, name=f"h_bf{j}", align_bytes=64) for j in range(TILES)]
         h_codes = [keep.tile([P, P], U32, name=f"h_codes{j}", align_bytes=64) for j in range(TILES)]
         h_scales = [keep.tile([P, P], U8, name=f"h_scales{j}", align_bytes=64) for j in range(TILES)]
-        y_sb = keep.tile([P, NT, S], F32, name="y_sb", align_bytes=64)
+        y_sb = keep.tile([P, ROW_TILES, S], F32, name="y_sb", align_bytes=64)
         ident = keep.tile([P, P], F32, name="ident")
 
         zero = keep.tile([P, 1], F32, name="zero")
-        warm = keep.tile([P, 1], F32, name="warm")
+        no_bias = keep.tile([P, 1], F32, name="no_bias")
         nc.gpsimd.memset(zero[:], 0.0)
-        nc.scalar.activation(warm[:], zero[:], GELU)
-        for lo, hi in ((0, 4), (4, 8)):
-            for plane in up_scales:
-                nc.gpsimd.memset(plane[:, lo:hi, :].rearrange("p a b -> p (a b)").bitcast(U32), 0)
+        nc.scalar.activation(no_bias[:], zero[:], GELU)
+
+        early, late = (0, 2 * PASSES), (2 * PASSES, E * PASSES)
+        for lo, hi in (early, late):
+            for scales_sb in up_scales:
+                nc.gpsimd.memset(scales_sb[:, lo:hi, :].rearrange("p a b -> p (a b)").bitcast(U32), 0)
         nc.gpsimd.memset(down_scales[:].rearrange("p a b -> p (a b)").bitcast(U32), 0)
         make_identity(nc, ident[:])
 
-        def load_gate(queue, a, b):
-            queue.dma_start(gate_sb[:, a:b], gate[0:P, a:b])
+        def load_gate(queue, lo, hi):
+            queue.dma_start(gate_sb[:, lo:hi], gate[0:P, lo:hi])
 
-        def load_x(queue, s, t):
+        def load_window(queue, s, t):
             rows = xT[s * P * PACK : (s + 1) * P * PACK, :].rearrange("(p t) c -> p t c", t=PACK)
-            queue.dma_start(x_sb[s][t][:], rows[:, t, :])
+            queue.dma_start(window[s][t][:], rows[:, t, :])
 
-        def load_scales(queue, plane, scales, lo, hi):
+        def load_scales(queue, scales_sb, scales, lo, hi):
             rows = scales.rearrange("e s q i -> q (e s) i")
             for quad in range(4):
                 queue.dma_start(
-                    plane[32 * quad : 32 * quad + 4, lo:hi, :].bitcast(I32),
+                    scales_sb[32 * quad : 32 * quad + 4, lo:hi, :].bitcast(I32),
                     rows[4 * quad : 4 * quad + 4, lo:hi, :].bitcast(I32),
                 )
 
@@ -86,70 +102,77 @@ def tile_moe_pre_glu_gelu_kernel(
             queue.dma_start(up_words[m][e][:].bitcast(I32), words[e].rearrange("s p b -> p s b").bitcast(I32))
 
         nc.sync.dma_start(offs_sb[:], offs)
-        load_gate(nc.scalar, 0, 3 * P)
-        for s in range(PASSES):
-            for t in range(PACK):
-                load_x((nc.sync, nc.scalar)[t % 2], s, t)
-        load_scales(nc.sync, up_scales[0], w1_scales, 0, 4)
-        load_scales(nc.scalar, up_scales[1], w3_scales, 0, 4)
-        load_gate(nc.sync, 3 * P, S)
-        load_up(nc.sync, 0, 0)
-        load_up(nc.scalar, 1, 0)
-        load_up(nc.sync, 0, 1)
-        load_up(nc.sync, 1, 1)
-        load_scales(nc.sync, down_scales, w2_scales, 0, 4)
+        load_gate(nc.scalar, 0, FIRST_GATE)
+        load_window(nc.sync, 1, 0)
+        for t in (1, 2, 3):
+            load_window(nc.scalar, 0, t)
+        load_window(nc.sync, 0, 0)
+        for t in (2, 3):
+            load_window(nc.scalar, 1, t)
+        load_scales(nc.sync, up_scales[W1], w1_scales, *early)
+        load_window(nc.sync, 1, 1)
+        load_scales(nc.scalar, up_scales[W3], w3_scales, *early)
+        load_gate(nc.sync, FIRST_GATE, S)
+        load_up(nc.sync, W1, 0)
+        load_up(nc.scalar, W3, 0)
+        load_up(nc.sync, W1, 1)
+        load_up(nc.sync, W3, 1)
+        load_scales(nc.sync, down_scales, w2_scales, 0, E)
         nc.sync.dma_start(down_words[:].bitcast(I32), w2_words.rearrange("e s p b -> p (e s) b").bitcast(I32))
-        load_scales(nc.sync, up_scales[0], w1_scales, 4, 8)
-        load_scales(nc.sync, up_scales[1], w3_scales, 4, 8)
-        for e in (2, 3):
-            load_up(nc.sync, 0, e)
-            load_up(nc.sync, 1, e)
+        load_scales(nc.sync, up_scales[W3], w3_scales, *late)
+        load_up(nc.sync, W3, 2)
+        load_up(nc.sync, W1, 2)
+        load_up(nc.sync, W1, 3)
         nc.sync.dma_start(pos_sb[0][:], pos1)
+        load_scales(nc.sync, up_scales[W1], w1_scales, *late)
+        load_up(nc.sync, W3, 3)
         nc.sync.dma_start(pos_sb[1][:], pos2)
 
-        def gather_and_quantize(s, j0, j1):
-            n = (j1 - j0) * P
-            slots = slice(j0 * P, j1 * P)
-            gathered = stage.tile([P, PACK, n], F32, name="gathered")
+        gathered = {}
+        w3_sums = {}
+
+        def gather(s, j0, j1):
+            rows = stage.tile([P, PACK, (j1 - j0) * P], F32, name="gathered")
+            for j in range(j0, j1):
+                gathered[s, j] = (rows, j0)
             for t in range(PACK):
                 nc.vector.tensor_tensor(
-                    gathered[:, t, :],
-                    x_sb[s][t][:].indirect(offs_sb[:, j0 * P // 16 : j1 * P // 16]),
-                    gate_sb[:, slots],
+                    rows[:, t, :],
+                    window[s][t][:].indirect(offs_sb[:, j0 * P // LIST_ROWS : j1 * P // LIST_ROWS]),
+                    gate_sb[:, j0 * P : j1 * P],
                     MULT,
                 )
-            for a in range(j0, j1, 2):
-                b = min(a + 2, j1)
-                rounded = x_bf[s][:, a * P * PACK : b * P * PACK]
-                copy = nc.vector.tensor_copy if (s, a) == (PASSES - 1, LAST) else nc.scalar.copy
-                copy(
-                    rounded.rearrange("p (c i t) -> p c t i", i=4, t=PACK),
-                    gathered[:, :, (a - j0) * P : (b - j0) * P].rearrange("p t (c i) -> p c t i", i=4),
-                )
-                nc.vector.quantize_mx(
-                    out=x_codes[s][:, a * P : b * P].bitcast(FP8X4), scales=x_scales[s][:, a * P : b * P], in_=rounded
-                )
 
-        def own_bank(j, shape, name):
-            return psum.tile(shape, F32, name=name, tag=f"bank{2 + j % 6}")
+        def interleave(s, j0, j1):
+            rows, first = gathered[s, j0]
+            copy = nc.vector.tensor_copy if (s, j0) == (PASSES - 1, LAST) else nc.scalar.copy
+            copy(
+                x_bf[s][:, j0 * P * PACK : j1 * P * PACK].rearrange("p (c i t) -> p c t i", i=4, t=PACK),
+                rows[:, :, (j0 - first) * P : (j1 - first) * P].rearrange("p t (c i) -> p c t i", i=4),
+            )
 
-        def halves(j):
+        def quantize_x(s, j0, j1):
+            nc.vector.quantize_mx(
+                out=x_codes[s][:, j0 * P : j1 * P].bitcast(FP8X4),
+                scales=x_scales[s][:, j0 * P : j1 * P],
+                in_=x_bf[s][:, j0 * P * PACK : j1 * P * PACK],
+            )
+
+        def by_pair(sums):
+            return sums[:].rearrange("q (p u v) -> q u p v", u=2, v=2)
+
+        def u_ranges(j):
             return ((0, 1), (1, 2)) if j == LAST else ((0, 2),)
-
-        def by_half(bank):
-            return bank[:].rearrange("q (p u v) -> q u p v", u=2, v=2)
-
-        a3 = {}
 
         def up(j):
             cols = slice(j * P, (j + 1) * P)
             e = j * P // C
-            a1 = psum.tile([P, H], F32, name="a1", tag=f"bank{j % 2}")
-            a3[j] = own_bank(j, [P, H], "a3")
-            for m, acc in enumerate((a1, a3[j])):
+            w1_sums = psum.tile([P, H], F32, name="w1_sums", tag=f"bank{W1_BANK[j]}")
+            w3_sums[j] = psum.tile([P, H], F32, name="w3_sums", tag=f"bank{W3_BANK[j]}")
+            for m, sums in ((W1, w1_sums), (W3, w3_sums[j])):
                 for s in range(PASSES):
                     nc.tensor.matmul_mx(
-                        out=acc[:],
+                        out=sums[:],
                         lhsT=x_codes[s][:, cols].bitcast(FP8X4),
                         lhsT_scale=x_scales[s][:, cols],
                         rhs=up_words[m][e][:, s, :].bitcast(FP4X4),
@@ -157,17 +180,18 @@ def tile_moe_pre_glu_gelu_kernel(
                         start=(s == 0),
                         stop=(s == PASSES - 1),
                     )
-                if m == 0:
-                    for lo, hi in halves(j):
-                        nc.scalar.activation(act[j][:, lo:hi], by_half(a1)[:, lo:hi], GELU)
+                if m == W1:
+                    for lo, hi in u_ranges(j):
+                        nc.scalar.activation(act[j][:, lo:hi], by_pair(w1_sums)[:, lo:hi], GELU, bias=no_bias[:])
 
         def product_and_turn(j):
-            for lo, hi in halves(j):
-                nc.vector.tensor_tensor(hid[j][:, lo:hi], by_half(a3[j])[:, lo:hi], act[j][:, lo:hi], MULT)
-            turned = own_bank(j, [P, 2, P], "turned")
-            words = hid[j][:].rearrange("q u p v -> q (u p v)").bitcast(F32)
+            h_rows = keep.tile([P, 2, P, 2], BF16, name=f"h_rows{j}")
+            for lo, hi in u_ranges(j):
+                nc.vector.tensor_tensor(h_rows[:, lo:hi], by_pair(w3_sums[j])[:, lo:hi], act[j][:, lo:hi], MULT)
+            turned = psum.tile([P, 2, P], F32, name="turned", tag=f"bank{TURNED_BANK[j]}")
+            units = h_rows[:].rearrange("q u p v -> q (u p v)").bitcast(F32)
             for u in range(2):
-                nc.tensor.transpose(turned[:, u, :], words[:, u * P : (u + 1) * P], ident[:])
+                nc.tensor.transpose(turned[:, u, :], units[:, u * P : (u + 1) * P], ident[:])
             nc.scalar.copy(
                 h_bf[j][:].bitcast(F32).rearrange("p (r u) -> p r u", u=2), turned[:].rearrange("p u r -> p r u")
             )
@@ -175,48 +199,72 @@ def tile_moe_pre_glu_gelu_kernel(
         def down(j):
             e = j * P // C
             nc.vector.quantize_mx(out=h_codes[j][:].bitcast(FP8X4), scales=h_scales[j][:], in_=h_bf[j][:])
-            y_ps = own_bank(j, [P, NT, P], "y_ps")
-            for m in range(NT):
+            y_sums = psum.tile([P, ROW_TILES, P], F32, name="y_sums", tag=f"bank{Y_BANK[j]}")
+            for r in range(ROW_TILES):
                 nc.tensor.matmul_mx(
-                    out=y_ps[:, m, :],
-                    lhsT=down_words[:, e, 2 * m * P : 2 * (m + 1) * P].bitcast(FP4X4),
-                    lhsT_scale=down_scales[:, e, m * P : (m + 1) * P],
+                    out=y_sums[:, r, :],
+                    lhsT=down_words[:, e, 2 * r * P : 2 * (r + 1) * P].bitcast(FP4X4),
+                    lhsT_scale=down_scales[:, e, r * P : (r + 1) * P],
                     rhs=h_codes[j][:].bitcast(FP8X4),
                     rhs_scale=h_scales[j][:],
                     start=True,
                     stop=True,
                 )
-            if j == LAST:
-                nc.vector.tensor_copy(y_sb[:, :, j * P : (j + 1) * P], y_ps[:])
-            else:
-                nc.scalar.copy(y_sb[:, :, j * P : (j + 1) * P], y_ps[:])
+            copy = nc.vector.tensor_copy if j in Y_COPY_ON_VECTOR else nc.scalar.copy
+            copy(y_sb[:, :, j * P : (j + 1) * P], y_sums[:])
 
-        gather_and_quantize(0, 0, 3)
-        gather_and_quantize(1, 0, 3)
-        for j in range(0, 3):
+        gather(1, 0, 3)
+        gather(0, 0, 3)
+        interleave(0, 2, 3)
+        interleave(0, 0, 2)
+        quantize_x(0, 0, 2)
+        quantize_x(0, 2, 3)
+        for j0, j1 in ((0, 2), (2, 3)):
+            interleave(1, j0, j1)
+            quantize_x(1, j0, j1)
+        for j in (0, 2, 1):
             up(j)
-        for j in range(0, 3):
+        for j in range(3):
             product_and_turn(j)
             down(j)
-        gather_and_quantize(0, 3, 6)
-        gather_and_quantize(1, 3, 6)
-        for j in range(3, 6):
-            up(j)
-        gather_and_quantize(0, 6, 8)
-        gather_and_quantize(1, 6, 7)
-        gather_and_quantize(1, 7, 8)
-        for j in range(6, 8):
-            up(j)
-        for j in range(3, 8):
+
+        gather(0, 3, 6)
+        interleave(0, 3, 5)
+        interleave(0, 5, 6)
+        quantize_x(0, 5, 6)
+        gather(1, 3, 6)
+        quantize_x(0, 3, 5)
+        interleave(1, 3, 5)
+        interleave(1, 5, 6)
+        gather(0, 6, 8)
+        quantize_x(1, 3, 5)
+        up(4)
+        interleave(0, 6, 8)
+        quantize_x(0, 6, 8)
+        gather(1, 6, 7)
+        quantize_x(1, 5, 6)
+        interleave(1, 6, 7)
+        up(3)
+        up(5)
+        gather(1, 7, 8)
+        quantize_x(1, 6, 7)
+        interleave(1, 7, 8)
+        quantize_x(1, 7, 8)
+        up(6)
+        up(7)
+
+        for j in range(3, TILES):
             product_and_turn(j)
-        for j in range(3, 8):
+        for j in range(3, TILES):
             down(j)
 
-        for piece, (m, lo, hi) in enumerate(((0, 0, T), (1, 0, T), (2, 0, T // 2), (2, T // 2, T))):
+        for piece, (r, lo, hi) in enumerate(OUT_PIECES):
             first = keep.tile([P, hi - lo], F32, name=f"first{piece}")
             second = keep.tile([P, hi - lo], F32, name=f"second{piece}")
             total = keep.tile([P, hi - lo], F32, name=f"total{piece}")
-            nc.vector.tensor_copy(first[:], y_sb[:, m, :].indirect(pos_sb[0][:, lo // 16 : hi // 16]))
-            nc.vector.tensor_copy(second[:], y_sb[:, m, :].indirect(pos_sb[1][:, lo // 16 : hi // 16]))
-            (nc.vector if piece == 3 else nc.gpsimd).tensor_tensor(total[:], first[:], second[:], ADD)
-            nc.sync.dma_start(out[m * P : (m + 1) * P, lo:hi], total[:])
+            entries = slice(lo // LIST_ROWS, hi // LIST_ROWS)
+            nc.vector.tensor_copy(first[:], y_sb[:, r, :].indirect(pos_sb[0][:, entries]))
+            nc.vector.tensor_copy(second[:], y_sb[:, r, :].indirect(pos_sb[1][:, entries]))
+            adder = nc.vector if piece == len(OUT_PIECES) - 1 else nc.gpsimd
+            adder.tensor_tensor(total[:], first[:], second[:], ADD)
+            nc.sync.dma_start(out[r * P : (r + 1) * P, lo:hi], total[:])

@@ -35,7 +35,6 @@ W1_BANK = (0, 1, 3, 3, 7, 3, 0, 5)
 W3_BANK = (0, 3, 4, 1, 6, 4, 2, 3)
 TURNED_BANK = (2, 3, 4, 6, 7, 4, 2, 3)
 Y_BANK = (2, 7, 4, 5, 6, 7, 2, 3)
-Y_COPY_ON_VECTOR = (5, LAST)
 OUT_PIECES = ((0, 0, T), (1, 0, T), (2, 0, T // 2), (2, T // 2, T - P), (2, T - P, T))
 FIRST_GATE = 3 * P
 
@@ -129,7 +128,7 @@ def tile_moe_pre_glu_gelu_kernel(
         nc.sync.dma_start(pos_sb[1][:], pos2)
 
         gathered = {}
-        w3_sums = {}
+        w3_sums, y_sums = {}, {}
 
         def gather(s, j0, j1):
             rows = stage.tile([P, PACK, (j1 - j0) * P], F32, name="gathered")
@@ -196,13 +195,16 @@ def tile_moe_pre_glu_gelu_kernel(
                 h_bf[j][:].bitcast(F32).rearrange("p (r u) -> p r u", u=2), turned[:].rearrange("p u r -> p r u")
             )
 
-        def down(j):
-            e = j * P // C
+        def quantize_h(j):
             nc.vector.quantize_mx(out=h_codes[j][:].bitcast(FP8X4), scales=h_scales[j][:], in_=h_bf[j][:])
-            y_sums = psum.tile([P, ROW_TILES, P], F32, name="y_sums", tag=f"bank{Y_BANK[j]}")
-            for r in range(ROW_TILES):
+
+        def down(j, r0, r1):
+            e = j * P // C
+            if r0 == 0:
+                y_sums[j] = psum.tile([P, ROW_TILES, P], F32, name="y_sums", tag=f"bank{Y_BANK[j]}")
+            for r in range(r0, r1):
                 nc.tensor.matmul_mx(
-                    out=y_sums[:, r, :],
+                    out=y_sums[j][:, r, :],
                     lhsT=down_words[:, e, 2 * r * P : 2 * (r + 1) * P].bitcast(FP4X4),
                     lhsT_scale=down_scales[:, e, r * P : (r + 1) * P],
                     rhs=h_codes[j][:].bitcast(FP8X4),
@@ -210,8 +212,8 @@ def tile_moe_pre_glu_gelu_kernel(
                     start=True,
                     stop=True,
                 )
-            copy = nc.vector.tensor_copy if j in Y_COPY_ON_VECTOR else nc.scalar.copy
-            copy(y_sb[:, :, j * P : (j + 1) * P], y_sums[:])
+            copy = nc.vector.tensor_copy if (j, r0) == (LAST, 0) else nc.scalar.copy
+            copy(y_sb[:, r0:r1, j * P : (j + 1) * P], y_sums[j][:, r0:r1, :])
 
         gather(1, 0, 3)
         gather(0, 0, 3)
@@ -226,7 +228,8 @@ def tile_moe_pre_glu_gelu_kernel(
             up(j)
         for j in range(3):
             product_and_turn(j)
-            down(j)
+            quantize_h(j)
+            down(j, 0, ROW_TILES)
 
         gather(0, 3, 6)
         interleave(0, 3, 5)
@@ -256,7 +259,10 @@ def tile_moe_pre_glu_gelu_kernel(
         for j in range(3, TILES):
             product_and_turn(j)
         for j in range(3, TILES):
-            down(j)
+            quantize_h(j)
+            down(j, 0, 1)
+        for j in range(3, TILES):
+            down(j, 1, ROW_TILES)
 
         for piece, (r, lo, hi) in enumerate(OUT_PIECES):
             first = keep.tile([P, hi - lo], F32, name=f"first{piece}")

@@ -31,12 +31,12 @@ GELU = mybir.ActivationFunctionType.Gelu_apprx_tanh
 
 W1, W3 = 0, 1
 
-W1_BANK = (0, 1, 3, 3, 7, 3, 0, 5)
-W3_BANK = (0, 3, 4, 1, 6, 4, 2, 3)
-TURNED_BANK = (2, 3, 4, 6, 7, 4, 2, 3)
-Y_BANK = (2, 7, 4, 5, 6, 7, 2, 3)
-OUT_PIECES = ((0, 0, T), (1, 0, T), (2, 0, T // 2), (2, T // 2, T - P), (2, T - P, T))
+GROUPS = (((0, 3), (3, 6), (6, 8)), ((0, 3), (3, 6), (6, 7), (7, 8)))
+W1_BANKS = 2
+W3_BANKS = 6
+PARKED = TILES - W3_BANKS
 FIRST_GATE = 3 * P
+LAST_PIECE = P
 
 
 def tile_moe_pre_glu_gelu_kernel(
@@ -51,7 +51,10 @@ def tile_moe_pre_glu_gelu_kernel(
         offs_sb = keep.tile([P, S // LIST_ROWS], U16, name="offs_sb")
         pos_sb = [keep.tile([P, T // LIST_ROWS], U16, name=f"pos_sb{r}") for r in range(2)]
         gate_sb = keep.tile([P, S], F32, name="gate_sb")
-        window = [[keep.tile([P, T], F32, name=f"window{s}{t}") for t in range(PACK)] for s in range(PASSES)]
+        window = [
+            [keep.tile([P, T], F32, name=f"window{s}{t}", tag=f"window{s}{t}", align_bytes=64) for t in range(PACK)]
+            for s in range(PASSES)
+        ]
         up_words = [
             [keep.tile([P, PASSES, 2 * H], U8, name=f"up_words{m}{e}", align_bytes=64) for e in range(E)]
             for m in (W1, W3)
@@ -59,27 +62,25 @@ def tile_moe_pre_glu_gelu_kernel(
         up_scales = [keep.tile([P, E * PASSES, H], U8, name=f"up_scales{m}", align_bytes=64) for m in (W1, W3)]
         down_words = keep.tile([P, E, 2 * N], U8, name="down_words", align_bytes=64)
         down_scales = keep.tile([P, E, N], U8, name="down_scales", align_bytes=64)
-        x_bf = [keep.tile([P, S * PACK], BF16, name=f"x_bf{s}", align_bytes=64) for s in range(PASSES)]
-        x_codes = [keep.tile([P, S], U32, name=f"x_codes{s}", align_bytes=64) for s in range(PASSES)]
+        x_codes = {}
         x_scales = [keep.tile([P, S], U8, name=f"x_scales{s}", align_bytes=64) for s in range(PASSES)]
-        act = [keep.tile([P, 2, P, 2], F32, name=f"act{j}") for j in range(TILES)]
-        h_bf = [keep.tile([P, P * PACK], BF16, name=f"h_bf{j}", align_bytes=64) for j in range(TILES)]
-        h_codes = [keep.tile([P, P], U32, name=f"h_codes{j}", align_bytes=64) for j in range(TILES)]
-        h_scales = [keep.tile([P, P], U8, name=f"h_scales{j}", align_bytes=64) for j in range(TILES)]
-        y_sb = keep.tile([P, ROW_TILES, S], F32, name="y_sb", align_bytes=64)
+        act = [keep.tile([P, 2, P, 2], F32, name=f"act{j}", tag=f"act{j}", align_bytes=64) for j in range(TILES)]
+        parked = [keep.tile([P, 2, P, 2], F32, name=f"parked{j}") for j in range(PARKED)]
+        h_scales = keep.tile([P, S], U8, name="h_scales", align_bytes=64)
+        y_sb = [keep.tile([P, S], F32, name=f"y_sb{r}", align_bytes=64) for r in range(ROW_TILES)]
         ident = keep.tile([P, P], F32, name="ident")
 
         zero = keep.tile([P, 1], F32, name="zero")
         no_bias = keep.tile([P, 1], F32, name="no_bias")
         nc.gpsimd.memset(zero[:], 0.0)
         nc.scalar.activation(no_bias[:], zero[:], GELU)
+        make_identity(nc, ident[:])
 
         early, late = (0, 2 * PASSES), (2 * PASSES, E * PASSES)
         for lo, hi in (early, late):
             for scales_sb in up_scales:
                 nc.gpsimd.memset(scales_sb[:, lo:hi, :].rearrange("p a b -> p (a b)").bitcast(U32), 0)
         nc.gpsimd.memset(down_scales[:].rearrange("p a b -> p (a b)").bitcast(U32), 0)
-        make_identity(nc, ident[:])
 
         def load_gate(queue, lo, hi):
             queue.dma_start(gate_sb[:, lo:hi], gate[0:P, lo:hi])
@@ -101,39 +102,31 @@ def tile_moe_pre_glu_gelu_kernel(
             queue.dma_start(up_words[m][e][:].bitcast(I32), words[e].rearrange("s p b -> p s b").bitcast(I32))
 
         nc.sync.dma_start(offs_sb[:], offs)
-        load_gate(nc.scalar, 0, FIRST_GATE)
-        load_window(nc.sync, 1, 0)
-        for t in (1, 2, 3):
-            load_window(nc.scalar, 0, t)
-        load_window(nc.sync, 0, 0)
-        for t in (2, 3):
-            load_window(nc.scalar, 1, t)
-        load_scales(nc.sync, up_scales[W1], w1_scales, *early)
-        load_window(nc.sync, 1, 1)
-        load_scales(nc.scalar, up_scales[W3], w3_scales, *early)
+        load_gate(nc.sync, 0, FIRST_GATE)
+        for s in range(PASSES):
+            for t in range(PACK):
+                load_window(nc.sync, s, t)
         load_gate(nc.sync, FIRST_GATE, S)
-        load_up(nc.sync, W1, 0)
-        load_up(nc.scalar, W3, 0)
-        load_up(nc.sync, W1, 1)
-        load_up(nc.sync, W3, 1)
+        for queue, (lo, hi) in ((nc.scalar, early), (nc.sync, late)):
+            load_scales(queue, up_scales[W1], w1_scales, lo, hi)
+            load_scales(queue, up_scales[W3], w3_scales, lo, hi)
+            for e in range(lo // PASSES, hi // PASSES):
+                for m in (W1, W3):
+                    load_up(nc.sync, m, e)
         load_scales(nc.sync, down_scales, w2_scales, 0, E)
         nc.sync.dma_start(down_words[:].bitcast(I32), w2_words.rearrange("e s p b -> p (e s) b").bitcast(I32))
-        load_scales(nc.sync, up_scales[W3], w3_scales, *late)
-        load_up(nc.sync, W3, 2)
-        load_up(nc.sync, W1, 2)
-        load_up(nc.sync, W1, 3)
         nc.sync.dma_start(pos_sb[0][:], pos1)
-        load_scales(nc.sync, up_scales[W1], w1_scales, *late)
-        load_up(nc.sync, W3, 3)
         nc.sync.dma_start(pos_sb[1][:], pos2)
 
         gathered = {}
-        w3_sums, y_sums = {}, {}
+        w3_sums, h_rows, h_bf, h_codes = {}, {}, {}, {}
+
+        def bank(b, shape, name):
+            return psum.tile(shape, F32, name=name, tag=f"bank{b}")
 
         def gather(s, j0, j1):
             rows = stage.tile([P, PACK, (j1 - j0) * P], F32, name="gathered")
-            for j in range(j0, j1):
-                gathered[s, j] = (rows, j0)
+            gathered[s, j0] = rows
             for t in range(PACK):
                 nc.vector.tensor_tensor(
                     rows[:, t, :],
@@ -142,135 +135,151 @@ def tile_moe_pre_glu_gelu_kernel(
                     MULT,
                 )
 
-        def interleave(s, j0, j1):
-            rows, first = gathered[s, j0]
-            copy = nc.vector.tensor_copy if (s, j0) == (PASSES - 1, LAST) else nc.scalar.copy
-            copy(
-                x_bf[s][:, j0 * P * PACK : j1 * P * PACK].rearrange("p (c i t) -> p c t i", i=4, t=PACK),
-                rows[:, :, (j0 - first) * P : (j1 - first) * P].rearrange("p t (c i) -> p c t i", i=4),
-            )
-
-        def quantize_x(s, j0, j1):
-            nc.vector.quantize_mx(
-                out=x_codes[s][:, j0 * P : j1 * P].bitcast(FP8X4),
-                scales=x_scales[s][:, j0 * P : j1 * P],
-                in_=x_bf[s][:, j0 * P * PACK : j1 * P * PACK],
-            )
+        def pack_x(s, j0, j1):
+            rows = gathered[s, j0]
+            for a in range(j0, j1, 2):
+                b = min(a + 2, j1)
+                tag = f"x_bf{s}{a}"
+                x_bf = keep.tile([P, (b - a) * P * PACK], BF16, name=f"x_bf{s}{a}", tag=tag, align_bytes=64)
+                codes = keep.tile([P, (b - a) * P], U32, name=f"x_codes{s}{a}", tag=f"x_codes{s}{a}", align_bytes=64)
+                for j in range(a, b):
+                    x_codes[s, j] = codes[:, (j - a) * P : (j - a + 1) * P]
+                nc.scalar.copy(
+                    x_bf[:].rearrange("p (c i t) -> p c t i", i=4, t=PACK),
+                    rows[:, :, (a - j0) * P : (b - j0) * P].rearrange("p t (c i) -> p c t i", i=4),
+                )
+                nc.vector.quantize_mx(
+                    out=codes[:].bitcast(FP8X4),
+                    scales=x_scales[s][:, a * P : b * P],
+                    in_=x_bf[:],
+                )
 
         def by_pair(sums):
             return sums[:].rearrange("q (p u v) -> q u p v", u=2, v=2)
 
-        def u_ranges(j):
-            return ((0, 1), (1, 2)) if j == LAST else ((0, 2),)
-
         def up(j):
             cols = slice(j * P, (j + 1) * P)
             e = j * P // C
-            w1_sums = psum.tile([P, H], F32, name="w1_sums", tag=f"bank{W1_BANK[j]}")
-            w3_sums[j] = psum.tile([P, H], F32, name="w3_sums", tag=f"bank{W3_BANK[j]}")
-            for m, sums in ((W1, w1_sums), (W3, w3_sums[j])):
+            w1_sums = bank(j % W1_BANKS, [P, H], "w1_sums")
+            w3_bank = bank(W1_BANKS + (j - PARKED) % W3_BANKS, [P, H], "w3_sums")
+            for m, sums in ((W1, w1_sums), (W3, w3_bank)):
                 for s in range(PASSES):
                     nc.tensor.matmul_mx(
                         out=sums[:],
-                        lhsT=x_codes[s][:, cols].bitcast(FP8X4),
+                        lhsT=x_codes[s, j].bitcast(FP8X4),
                         lhsT_scale=x_scales[s][:, cols],
                         rhs=up_words[m][e][:, s, :].bitcast(FP4X4),
                         rhs_scale=up_scales[m][:, e * PASSES + s, :],
                         start=(s == 0),
                         stop=(s == PASSES - 1),
                     )
-                if m == W1:
-                    for lo, hi in u_ranges(j):
-                        nc.scalar.activation(act[j][:, lo:hi], by_pair(w1_sums)[:, lo:hi], GELU, bias=no_bias[:])
+            nc.scalar.activation(act[j][:], by_pair(w1_sums), GELU, bias=no_bias[:])
+            if j < PARKED:
+                nc.scalar.copy(parked[j][:], by_pair(w3_bank))
+                w3_sums[j] = parked[j][:]
+            else:
+                w3_sums[j] = by_pair(w3_bank)
 
-        def product_and_turn(j):
-            h_rows = keep.tile([P, 2, P, 2], BF16, name=f"h_rows{j}")
-            for lo, hi in u_ranges(j):
-                nc.vector.tensor_tensor(h_rows[:, lo:hi], by_pair(w3_sums[j])[:, lo:hi], act[j][:, lo:hi], MULT)
-            turned = psum.tile([P, 2, P], F32, name="turned", tag=f"bank{TURNED_BANK[j]}")
-            units = h_rows[:].rearrange("q u p v -> q (u p v)").bitcast(F32)
-            for u in range(2):
-                nc.tensor.transpose(turned[:, u, :], units[:, u * P : (u + 1) * P], ident[:])
+        def product(j):
+            if j % 2 == 0:
+                h_rows[j // 2] = keep.tile(
+                    [P, 2 * H], BF16, name=f"h_rows{j // 2}", tag=f"window{PASSES - 1}{j // 2}", align_bytes=64
+                )
+            rows = h_rows[j // 2][:, (j % 2) * H : (j % 2 + 1) * H]
+            nc.vector.tensor_tensor(rows.rearrange("q (u p v) -> q u p v", u=2, v=2), w3_sums[j], act[j][:], MULT)
+
+        def turn(j0, j1, b):
+            n = j1 - j0
+            turned = bank(b, [P, n, 2, P], "turned")
+            for j in range(j0, j1):
+                units = h_rows[j // 2][:].bitcast(F32)
+                for u in range(2):
+                    a = ((j % 2) * 2 + u) * P
+                    nc.tensor.transpose(turned[:, j - j0, u, :], units[:, a : a + P], ident[:])
+            h_bf[j0] = keep.tile([P, n * P * PACK], BF16, name=f"h_bf{j0}", align_bytes=64)
             nc.scalar.copy(
-                h_bf[j][:].bitcast(F32).rearrange("p (r u) -> p r u", u=2), turned[:].rearrange("p u r -> p r u")
+                h_bf[j0][:].bitcast(F32).rearrange("p (j r u) -> p j r u", j=n, u=2),
+                turned[:].rearrange("p j u r -> p j r u"),
             )
 
-        def quantize_h(j):
-            nc.vector.quantize_mx(out=h_codes[j][:].bitcast(FP8X4), scales=h_scales[j][:], in_=h_bf[j][:])
+        def quantize_h(j0, j1, codes):
+            h_codes[j0] = codes
+            nc.vector.quantize_mx(out=codes.bitcast(FP8X4), scales=h_scales[:, j0 * P : j1 * P], in_=h_bf[j0][:])
 
-        def down(j, r0, r1):
-            e = j * P // C
-            if r0 == 0:
-                y_sums[j] = psum.tile([P, ROW_TILES, P], F32, name="y_sums", tag=f"bank{Y_BANK[j]}")
-            for r in range(r0, r1):
+        def down(r, pieces, b, copy):
+            j0, j1 = pieces[0][0], pieces[-1][1]
+            sums = bank(b, [P, (j1 - j0) * P], "y_sums")
+            for a, z in pieces:
+                e = a * P // C
                 nc.tensor.matmul_mx(
-                    out=y_sums[j][:, r, :],
+                    out=sums[:, (a - j0) * P : (z - j0) * P],
                     lhsT=down_words[:, e, 2 * r * P : 2 * (r + 1) * P].bitcast(FP4X4),
                     lhsT_scale=down_scales[:, e, r * P : (r + 1) * P],
-                    rhs=h_codes[j][:].bitcast(FP8X4),
-                    rhs_scale=h_scales[j][:],
+                    rhs=h_codes[a].bitcast(FP8X4),
+                    rhs_scale=h_scales[:, a * P : z * P],
                     start=True,
                     stop=True,
                 )
-            copy = nc.vector.tensor_copy if (j, r0) == (LAST, 0) else nc.scalar.copy
-            copy(y_sb[:, r0:r1, j * P : (j + 1) * P], y_sums[j][:, r0:r1, :])
+            copy(y_sb[r][:, j0 * P : j1 * P], sums[:])
 
-        gather(1, 0, 3)
         gather(0, 0, 3)
-        interleave(0, 2, 3)
-        interleave(0, 0, 2)
-        quantize_x(0, 0, 2)
-        quantize_x(0, 2, 3)
-        for j0, j1 in ((0, 2), (2, 3)):
-            interleave(1, j0, j1)
-            quantize_x(1, j0, j1)
-        for j in (0, 2, 1):
-            up(j)
-        for j in range(3):
-            product_and_turn(j)
-            quantize_h(j)
-            down(j, 0, ROW_TILES)
-
-        gather(0, 3, 6)
-        interleave(0, 3, 5)
-        interleave(0, 5, 6)
-        quantize_x(0, 5, 6)
-        gather(1, 3, 6)
-        quantize_x(0, 3, 5)
-        interleave(1, 3, 5)
-        interleave(1, 5, 6)
-        gather(0, 6, 8)
-        quantize_x(1, 3, 5)
-        up(4)
-        interleave(0, 6, 8)
-        quantize_x(0, 6, 8)
+        gather(1, 0, 2)
+        pack_x(0, 0, 3)
+        gather(0, 3, 5)
+        pack_x(1, 0, 2)
+        gather(1, 2, 4)
+        pack_x(0, 3, 5)
+        up(0)
+        up(1)
+        gather(0, 5, 8)
+        pack_x(1, 2, 4)
+        gather(1, 4, 6)
+        pack_x(0, 5, 8)
+        up(2)
         gather(1, 6, 7)
-        quantize_x(1, 5, 6)
-        interleave(1, 6, 7)
+        pack_x(1, 4, 6)
         up(3)
-        up(5)
         gather(1, 7, 8)
-        quantize_x(1, 6, 7)
-        interleave(1, 7, 8)
-        quantize_x(1, 7, 8)
-        up(6)
-        up(7)
+        pack_x(1, 6, 7)
+        up(4)
+        pack_x(1, 7, 8)
+        for j in (5, 6, 7):
+            up(j)
 
-        for j in range(3, TILES):
-            product_and_turn(j)
-        for j in range(3, TILES):
-            quantize_h(j)
-            down(j, 0, 1)
-        for j in range(3, TILES):
-            down(j, 1, ROW_TILES)
+        pieces = ((0, 2), (2, 4), (4, 6), (6, 7), (7, 8))
+        for j in range(TILES):
+            product(j)
+        for (j0, j1), b in zip(pieces, (2, 3, 4, 5, 0)):
+            turn(j0, j1, b)
+        first_codes = keep.tile([P, C], U32, name="first_codes", tag=f"act{LAST - 1}", align_bytes=64)
+        later_codes = keep.tile([P, S - C], U32, name="later_codes", tag=f"act{LAST}", align_bytes=64)
+        for j0, j1 in pieces:
+            codes = first_codes[:] if j0 == 0 else later_codes[:, j0 * P - C : j1 * P - C]
+            quantize_h(j0, j1, codes)
+        for piece, b in zip(pieces[:-1], (6, 7, 2, 3)):
+            down(0, [piece], b, nc.scalar.copy)
+        down(0, pieces[-1:], 1, nc.vector.tensor_copy)
+        for r, banks in ((1, (4, 5)), (2, (0, 6))):
+            down(r, pieces[:2], banks[0], nc.scalar.copy)
+            down(r, pieces[2:], banks[1], nc.scalar.copy)
 
-        for piece, (r, lo, hi) in enumerate(OUT_PIECES):
-            first = keep.tile([P, hi - lo], F32, name=f"first{piece}")
-            second = keep.tile([P, hi - lo], F32, name=f"second{piece}")
-            total = keep.tile([P, hi - lo], F32, name=f"total{piece}")
-            entries = slice(lo // LIST_ROWS, hi // LIST_ROWS)
-            nc.vector.tensor_copy(first[:], y_sb[:, r, :].indirect(pos_sb[0][:, entries]))
-            nc.vector.tensor_copy(second[:], y_sb[:, r, :].indirect(pos_sb[1][:, entries]))
-            adder = nc.vector if piece == len(OUT_PIECES) - 1 else nc.gpsimd
-            adder.tensor_tensor(total[:], first[:], second[:], ADD)
+        def fetch_first(r, lo, hi):
+            first = keep.tile([P, hi - lo], F32, name=f"first{r}_{lo}")
+            nc.vector.tensor_copy(first[:], y_sb[r][:].indirect(pos_sb[0][:, lo // LIST_ROWS : hi // LIST_ROWS]))
+            return first
+
+        def add_second(r, first, start, lo, hi):
+            total = keep.tile([P, hi - lo], F32, name=f"total{r}_{lo}")
+            entries = pos_sb[1][:, lo // LIST_ROWS : hi // LIST_ROWS]
+            nc.vector.tensor_tensor(total[:], y_sb[r][:].indirect(entries), first[:, lo - start : hi - start], ADD)
             nc.sync.dma_start(out[r * P : (r + 1) * P, lo:hi], total[:])
+
+        half = T // 2
+        for r in range(ROW_TILES):
+            firsts = [fetch_first(r, lo, lo + half) for lo in (0, half)]
+            add_second(r, firsts[0], 0, 0, half)
+            if r < ROW_TILES - 1:
+                add_second(r, firsts[1], half, half, T)
+            else:
+                add_second(r, firsts[1], half, half, T - LAST_PIECE)
+                add_second(r, firsts[1], half, T - LAST_PIECE, T)

@@ -36,6 +36,7 @@ W1_BANKS = 2
 W3_BANKS = 6
 PARKED = TILES - W3_BANKS
 FIRST_GATE = 3 * P
+SECOND_GATE = 5 * P
 LAST_PIECE = P
 
 
@@ -106,13 +107,15 @@ def tile_moe_pre_glu_gelu_kernel(
         for s in range(PASSES):
             for t in range(PACK):
                 load_window(nc.sync, s, t)
-        load_gate(nc.sync, FIRST_GATE, S)
+        load_gate(nc.sync, FIRST_GATE, SECOND_GATE)
         for queue, (lo, hi) in ((nc.scalar, early), (nc.sync, late)):
             load_scales(queue, up_scales[W1], w1_scales, lo, hi)
             load_scales(queue, up_scales[W3], w3_scales, lo, hi)
             for e in range(lo // PASSES, hi // PASSES):
                 for m in (W1, W3):
                     load_up(nc.sync, m, e)
+                if e == 0:
+                    load_gate(nc.sync, SECOND_GATE, S)
         load_scales(nc.sync, down_scales, w2_scales, 0, E)
         nc.sync.dma_start(down_words[:].bitcast(I32), w2_words.rearrange("e s p b -> p (e s) b").bitcast(I32))
         nc.sync.dma_start(pos_sb[0][:], pos1)
@@ -263,23 +266,14 @@ def tile_moe_pre_glu_gelu_kernel(
             down(r, pieces[:2], banks[0], nc.scalar.copy)
             down(r, pieces[2:], banks[1], nc.scalar.copy)
 
-        def fetch_first(r, lo, hi):
-            first = keep.tile([P, hi - lo], F32, name=f"first{r}_{lo}")
-            nc.vector.tensor_copy(first[:], y_sb[r][:].indirect(pos_sb[0][:, lo // LIST_ROWS : hi // LIST_ROWS]))
-            return first
-
-        def add_second(r, first, start, lo, hi):
-            total = keep.tile([P, hi - lo], F32, name=f"total{r}_{lo}")
-            entries = pos_sb[1][:, lo // LIST_ROWS : hi // LIST_ROWS]
-            nc.vector.tensor_tensor(total[:], y_sb[r][:].indirect(entries), first[:, lo - start : hi - start], ADD)
+        out_pieces = ((0, 0, T), (1, 0, T), (2, 0, T // 2), (2, T // 2, T - P), (2, T - P, T))
+        for n, (r, lo, hi) in enumerate(out_pieces):
+            first = keep.tile([P, hi - lo], F32, name=f"first{n}")
+            second = keep.tile([P, hi - lo], F32, name=f"second{n}")
+            total = keep.tile([P, hi - lo], F32, name=f"total{n}")
+            entries = slice(lo // LIST_ROWS, hi // LIST_ROWS)
+            nc.vector.tensor_copy(first[:], y_sb[r][:].indirect(pos_sb[0][:, entries]))
+            nc.vector.tensor_copy(second[:], y_sb[r][:].indirect(pos_sb[1][:, entries]))
+            adder = nc.vector if n == len(out_pieces) - 1 else nc.gpsimd
+            adder.tensor_tensor(total[:], first[:], second[:], ADD)
             nc.sync.dma_start(out[r * P : (r + 1) * P, lo:hi], total[:])
-
-        half = T // 2
-        for r in range(ROW_TILES):
-            firsts = [fetch_first(r, lo, lo + half) for lo in (0, half)]
-            add_second(r, firsts[0], 0, 0, half)
-            if r < ROW_TILES - 1:
-                add_second(r, firsts[1], half, half, T)
-            else:
-                add_second(r, firsts[1], half, half, T - LAST_PIECE)
-                add_second(r, firsts[1], half, T - LAST_PIECE, T)

@@ -166,15 +166,16 @@ def tile_moe_pre_glu_gelu_kernel(
             w1_sums = bank(j % W1_BANKS, [P, H], "w1_sums")
             w3_bank = bank(W1_BANKS + (j - PARKED) % W3_BANKS, [P, H], "w3_sums")
             for m, sums in ((W1, w1_sums), (W3, w3_bank)):
-                for s in range(PASSES):
+                order = (1, 0) if j > 2 and j % 2 == 1 else (0, 1)
+                for s in order:
                     nc.tensor.matmul_mx(
                         out=sums[:],
                         lhsT=x_codes[s, j].bitcast(FP8X4),
                         lhsT_scale=x_scales[s][:, cols],
                         rhs=up_words[m][e][:, s, :].bitcast(FP4X4),
                         rhs_scale=up_scales[m][:, e * PASSES + s, :],
-                        start=(s == 0),
-                        stop=(s == PASSES - 1),
+                        start=(s == order[0]),
+                        stop=(s == order[-1]),
                     )
             nc.scalar.activation(act[j][:], by_pair(w1_sums), GELU, bias=no_bias[:])
             if j < PARKED:
@@ -184,20 +185,21 @@ def tile_moe_pre_glu_gelu_kernel(
                 w3_sums[j] = by_pair(w3_bank)
 
         def product(j):
-            if j % 2 == 0:
-                h_rows[j // 2] = keep.tile(
-                    [P, 2 * H], BF16, name=f"h_rows{j // 2}", tag=f"window{PASSES - 1}{j // 2}", align_bytes=64
-                )
-            rows = h_rows[j // 2][:, (j % 2) * H : (j % 2 + 1) * H]
+            if j == 0:
+                for name, tag, tiles in (("h_first", "window02", (0, 1)), ("h_rest", f"x_bf0{LAST}", range(2, TILES))):
+                    held = keep.tile([P, len(tiles) * H], BF16, name=name, tag=tag, align_bytes=64)
+                    for n, i in enumerate(tiles):
+                        h_rows[i] = held[:, n * H : (n + 1) * H]
+            rows = h_rows[j]
             nc.vector.tensor_tensor(rows.rearrange("q (u p v) -> q u p v", u=2, v=2), w3_sums[j], act[j][:], MULT)
 
         def turn(j0, j1, b):
             n = j1 - j0
             turned = bank(b, [P, n, 2, P], "turned")
             for j in range(j0, j1):
-                units = h_rows[j // 2][:].bitcast(F32)
+                units = h_rows[j].bitcast(F32)
                 for u in range(2):
-                    a = ((j % 2) * 2 + u) * P
+                    a = u * P
                     nc.tensor.transpose(turned[:, j - j0, u, :], units[:, a : a + P], ident[:])
             h_bf[j0] = keep.tile([P, n * P * PACK], BF16, name=f"h_bf{j0}", align_bytes=64)
             nc.scalar.copy(
@@ -228,26 +230,27 @@ def tile_moe_pre_glu_gelu_kernel(
         gather(0, 0, 3)
         gather(1, 0, 2)
         pack_x(0, 0, 3)
-        gather(0, 3, 5)
-        pack_x(1, 0, 2)
         gather(1, 2, 4)
-        pack_x(0, 3, 5)
+        pack_x(1, 0, 2)
+        gather(0, 3, 5)
+        pack_x(1, 2, 4)
         up(0)
         up(1)
-        gather(0, 5, 8)
-        pack_x(1, 2, 4)
         gather(1, 4, 6)
-        pack_x(0, 5, 8)
+        pack_x(0, 3, 5)
         up(2)
-        gather(1, 6, 7)
+        gather(0, 5, 7)
         pack_x(1, 4, 6)
         up(3)
-        gather(1, 7, 8)
-        pack_x(1, 6, 7)
+        gather(1, 6, 8)
+        pack_x(0, 5, 7)
         up(4)
-        pack_x(1, 7, 8)
-        for j in (5, 6, 7):
-            up(j)
+        gather(0, 7, 8)
+        pack_x(1, 6, 8)
+        up(5)
+        pack_x(0, 7, 8)
+        up(6)
+        up(7)
 
         pieces = ((0, 2), (2, 4), (4, 6), (6, 7), (7, 8))
         for j in range(TILES):
@@ -262,7 +265,7 @@ def tile_moe_pre_glu_gelu_kernel(
         for piece, b in zip(pieces[:-1], (6, 7, 2, 3)):
             down(0, [piece], b, nc.scalar.copy)
         down(0, pieces[-1:], 1, nc.vector.tensor_copy)
-        for r, banks in ((1, (4, 5)), (2, (0, 6))):
+        for r, banks in ((1, (4, 5)), (2, (1, 6))):
             down(r, pieces[:2], banks[0], nc.scalar.copy)
             down(r, pieces[2:], banks[1], nc.scalar.copy)
 

@@ -31,13 +31,11 @@ GELU = mybir.ActivationFunctionType.Gelu_apprx_tanh
 
 W1, W3 = 0, 1
 
-GROUPS = (((0, 3), (3, 6), (6, 8)), ((0, 3), (3, 6), (6, 7), (7, 8)))
 W1_BANKS = 2
 W3_BANKS = 6
 PARKED = TILES - W3_BANKS
-FIRST_GATE = 3 * P
-SECOND_GATE = 5 * P
-LAST_PIECE = P
+SPARE = 32
+FIRST_GATE = 4 * P
 
 
 def tile_moe_pre_glu_gelu_kernel(
@@ -51,9 +49,9 @@ def tile_moe_pre_glu_gelu_kernel(
 
         offs_sb = keep.tile([P, S // LIST_ROWS], U16, name="offs_sb")
         pos_sb = [keep.tile([P, T // LIST_ROWS], U16, name=f"pos_sb{r}") for r in range(2)]
-        gate_sb = keep.tile([P, S], F32, name="gate_sb")
+        gate_all = keep.tile([P, S], F32, name="gate_all")
         window = [
-            [keep.tile([P, T], F32, name=f"window{s}{t}", tag=f"window{s}{t}", align_bytes=64) for t in range(PACK)]
+            [keep.tile([P, T + SPARE], F32, name=f"window{s}{t}", tag=f"window{s}{t}", align_bytes=64) for t in range(PACK)]
             for s in range(PASSES)
         ]
         up_words = [
@@ -83,12 +81,19 @@ def tile_moe_pre_glu_gelu_kernel(
                 nc.gpsimd.memset(scales_sb[:, lo:hi, :].rearrange("p a b -> p (a b)").bitcast(U32), 0)
         nc.gpsimd.memset(down_scales[:].rearrange("p a b -> p (a b)").bitcast(U32), 0)
 
+        for planes in window:
+            for plane in planes:
+                nc.vector.memset(plane[:, T:], 0.0)
+
+        def gate_sb(lo, hi):
+            return gate_all[:, lo:hi]
+
         def load_gate(queue, lo, hi):
-            queue.dma_start(gate_sb[:, lo:hi], gate[0:P, lo:hi])
+            queue.dma_start(gate_sb(lo, hi), gate[0:P, lo:hi])
 
         def load_window(queue, s, t):
             rows = xT[s * P * PACK : (s + 1) * P * PACK, :].rearrange("(p t) c -> p t c", t=PACK)
-            queue.dma_start(window[s][t][:], rows[:, t, :])
+            queue.dma_start(window[s][t][:, :T], rows[:, t, :])
 
         def load_scales(queue, scales_sb, scales, lo, hi):
             rows = scales.rearrange("e s q i -> q (e s) i")
@@ -103,71 +108,86 @@ def tile_moe_pre_glu_gelu_kernel(
             queue.dma_start(up_words[m][e][:].bitcast(I32), words[e].rearrange("s p b -> p s b").bitcast(I32))
 
         nc.sync.dma_start(offs_sb[:], offs)
-        load_gate(nc.sync, 0, FIRST_GATE)
+        load_gate(nc.sync, 0, P)
         for s in range(PASSES):
             for t in range(PACK):
                 load_window(nc.sync, s, t)
-        load_gate(nc.sync, FIRST_GATE, SECOND_GATE)
+                if (s, t) == (0, 0):
+                    load_gate(nc.sync, P, FIRST_GATE)
+        load_gate(nc.sync, FIRST_GATE, S)
         for queue, (lo, hi) in ((nc.scalar, early), (nc.sync, late)):
             load_scales(queue, up_scales[W1], w1_scales, lo, hi)
             load_scales(queue, up_scales[W3], w3_scales, lo, hi)
             for e in range(lo // PASSES, hi // PASSES):
                 for m in (W1, W3):
                     load_up(nc.sync, m, e)
-                if e == 0:
-                    load_gate(nc.sync, SECOND_GATE, S)
         load_scales(nc.sync, down_scales, w2_scales, 0, E)
         nc.sync.dma_start(down_words[:].bitcast(I32), w2_words.rearrange("e s p b -> p (e s) b").bitcast(I32))
         nc.sync.dma_start(pos_sb[0][:], pos1)
         nc.sync.dma_start(pos_sb[1][:], pos2)
 
-        gathered = {}
+        gathered, woven = {}, {}
         w3_sums, h_rows, h_bf, h_codes = {}, {}, {}, {}
 
         def bank(b, shape, name):
             return psum.tile(shape, F32, name=name, tag=f"bank{b}")
 
-        def gather(s, j0, j1):
-            rows = stage.tile([P, PACK, (j1 - j0) * P], F32, name="gathered")
-            gathered[s, j0] = rows
-            for t in range(PACK):
-                nc.vector.tensor_tensor(
-                    rows[:, t, :],
-                    window[s][t][:].indirect(offs_sb[:, j0 * P // LIST_ROWS : j1 * P // LIST_ROWS]),
-                    gate_sb[:, j0 * P : j1 * P],
-                    MULT,
+        def staged(s, j0, j1, room=0):
+            if (s, j0) not in gathered:
+                gathered[s, j0] = stage.tile([P, PACK * (j1 - j0) * P + room], F32, name="gathered", align_bytes=64)
+            return gathered[s, j0][:]
+
+        def gather(s, j0, j1, planes=range(PACK)):
+            rows = staged(s, j0, j1)[:, : PACK * (j1 - j0) * P].rearrange("p (t c) -> p t c", t=PACK)
+            for t in planes:
+                cuts = (j0, j0 + 1, j1) if (s, j0, t) == (0, 0, 0) else (j0, j1)
+                for a, z in zip(cuts, cuts[1:]):
+                    nc.vector.tensor_tensor(
+                        rows[:, t, (a - j0) * P : (z - j0) * P],
+                        window[s][t][:].indirect(offs_sb[:, a * P // LIST_ROWS : z * P // LIST_ROWS]),
+                        gate_sb(a * P, z * P),
+                        MULT,
+                    )
+
+        def weave(s, j0, j1, a, z, tag=None, into=None):
+            rows = staged(s, j0, j1)[:, : PACK * (j1 - j0) * P].rearrange("p (t c) -> p t c", t=PACK)
+            if into is None:
+                tag = tag or f"x_bf{s}{a}"
+                held = keep.tile([P, (z - a) * P * PACK], BF16, name=f"x_bf{s}{a}", tag=tag, align_bytes=64)
+                into = held[:]
+            x_bf = into[:, : (z - a) * P * PACK]
+            woven[s, a] = x_bf
+            nc.scalar.copy(
+                x_bf.rearrange("p (c i t) -> p c t i", i=4, t=PACK),
+                rows[:, :, (a - j0) * P : (z - j0) * P].rearrange("p t (c i) -> p c t i", i=4),
+            )
+
+        def quantize_x(s, a, cuts, tag=None):
+            z = cuts[-1]
+            codes = keep.tile([P, (z - a) * P], U32, name=f"x_codes{s}{a}", tag=tag or f"x_codes{s}{a}", align_bytes=64)
+            for j in range(a, z):
+                x_codes[s, j] = codes[:, (j - a) * P : (j - a + 1) * P]
+            for lo, hi in zip((a,) + cuts, cuts):
+                nc.vector.quantize_mx(
+                    out=codes[:, (lo - a) * P : (hi - a) * P].bitcast(FP8X4),
+                    scales=x_scales[s][:, lo * P : hi * P],
+                    in_=woven[s, a][:, (lo - a) * P * PACK : (hi - a) * P * PACK],
                 )
 
-        def pack_x(s, j0, j1):
-            rows = gathered[s, j0]
-            for a in range(j0, j1, 2):
-                b = min(a + 2, j1)
-                tag = f"x_bf{s}{a}"
-                x_bf = keep.tile([P, (b - a) * P * PACK], BF16, name=f"x_bf{s}{a}", tag=tag, align_bytes=64)
-                codes = keep.tile([P, (b - a) * P], U32, name=f"x_codes{s}{a}", tag=f"x_codes{s}{a}", align_bytes=64)
-                for j in range(a, b):
-                    x_codes[s, j] = codes[:, (j - a) * P : (j - a + 1) * P]
-                nc.scalar.copy(
-                    x_bf[:].rearrange("p (c i t) -> p c t i", i=4, t=PACK),
-                    rows[:, :, (a - j0) * P : (b - j0) * P].rearrange("p t (c i) -> p c t i", i=4),
-                )
-                nc.vector.quantize_mx(
-                    out=codes[:].bitcast(FP8X4),
-                    scales=x_scales[s][:, a * P : b * P],
-                    in_=x_bf[:],
-                )
+        def pack_x(s, j0, j1, a, cuts, tag=None):
+            weave(s, j0, j1, a, cuts[-1], tag)
+            quantize_x(s, a, cuts)
 
         def by_pair(sums):
             return sums[:].rearrange("q (p u v) -> q u p v", u=2, v=2)
 
-        def up(j):
+        def up(j, order=(0, 1)):
             cols = slice(j * P, (j + 1) * P)
             e = j * P // C
             w1_sums = bank(j % W1_BANKS, [P, H], "w1_sums")
             w3_bank = bank(W1_BANKS + (j - PARKED) % W3_BANKS, [P, H], "w3_sums")
-            for m, sums in ((W1, w1_sums), (W3, w3_bank)):
-                order = (1, 0) if j > 2 and j % 2 == 1 else (0, 1)
-                for s in order:
+            for s in order:
+                for m, sums in ((W1, w1_sums), (W3, w3_bank)):
                     nc.tensor.matmul_mx(
                         out=sums[:],
                         lhsT=x_codes[s, j].bitcast(FP8X4),
@@ -186,7 +206,7 @@ def tile_moe_pre_glu_gelu_kernel(
 
         def product(j):
             if j == 0:
-                for name, tag, tiles in (("h_first", "window02", (0, 1)), ("h_rest", f"x_bf0{LAST}", range(2, TILES))):
+                for name, tag, tiles in (("h_first", "window02", (0, 1)), ("h_rest", "x_bf07", range(2, TILES))):
                     held = keep.tile([P, len(tiles) * H], BF16, name=name, tag=tag, align_bytes=64)
                     for n, i in enumerate(tiles):
                         h_rows[i] = held[:, n * H : (n + 1) * H]
@@ -206,6 +226,11 @@ def tile_moe_pre_glu_gelu_kernel(
                 h_bf[j0][:].bitcast(F32).rearrange("p (j r u) -> p j r u", j=n, u=2),
                 turned[:].rearrange("p j u r -> p j r u"),
             )
+
+        def finish(j0, j1, b):
+            for j in range(j0, j1):
+                product(j)
+            turn(j0, j1, b)
 
         def quantize_h(j0, j1, codes):
             h_codes[j0] = codes
@@ -227,30 +252,30 @@ def tile_moe_pre_glu_gelu_kernel(
                 )
             copy(y_sb[r][:, j0 * P : j1 * P], sums[:])
 
-        gather(0, 0, 3)
+        gather(0, 0, 4)
         gather(1, 0, 2)
-        pack_x(0, 0, 3)
-        gather(1, 2, 4)
-        pack_x(1, 0, 2)
-        gather(0, 3, 5)
-        pack_x(1, 2, 4)
+        pack_x(0, 0, 4, 0, (2,))
+        pack_x(0, 0, 4, 2, (4,))
+        pack_x(1, 0, 2, 0, (2,))
+        gather(1, 2, 6)
         up(0)
+        fourth = staged(0, 4, 7, room=5 * P)
+        gather(0, 4, 7, (0, 1, 2))
+        weave(1, 2, 6, 2, 6, into=fourth[:, 9 * P :].bitcast(BF16))
+        quantize_x(1, 2, (4, 6))
         up(1)
-        gather(1, 4, 6)
-        pack_x(0, 3, 5)
+        gather(0, 4, 7, (3,))
         up(2)
-        gather(0, 5, 7)
-        pack_x(1, 4, 6)
+        pack_x(0, 4, 7, 4, (6, 7))
         up(3)
         gather(1, 6, 8)
-        pack_x(0, 5, 7)
-        up(4)
+        pack_x(1, 6, 8, 6, (8,))
+        up(4, (1, 0))
         gather(0, 7, 8)
-        pack_x(1, 6, 8)
-        up(5)
-        pack_x(0, 7, 8)
+        pack_x(0, 7, 8, 7, (8,))
+        up(5, (1, 0))
         up(6)
-        up(7)
+        up(7, (1, 0))
 
         pieces = ((0, 2), (2, 4), (4, 6), (6, 7), (7, 8))
         for j in range(TILES):
@@ -262,21 +287,33 @@ def tile_moe_pre_glu_gelu_kernel(
         for j0, j1 in pieces:
             codes = first_codes[:] if j0 == 0 else later_codes[:, j0 * P - C : j1 * P - C]
             quantize_h(j0, j1, codes)
-        for piece, b in zip(pieces[:-1], (6, 7, 2, 3)):
+        for piece, b in zip(pieces[:3], (6, 7, 2)):
             down(0, [piece], b, nc.scalar.copy)
-        down(0, pieces[-1:], 1, nc.vector.tensor_copy)
-        for r, banks in ((1, (4, 5)), (2, (1, 6))):
+        for piece, b in zip(pieces[3:], (0, 1)):
+            down(0, [piece], b, nc.vector.tensor_copy)
+        for r, banks in ((1, (1, 0)), (2, (2, 7))):
             down(r, pieces[:2], banks[0], nc.scalar.copy)
             down(r, pieces[2:], banks[1], nc.scalar.copy)
 
-        out_pieces = ((0, 0, T), (1, 0, T), (2, 0, T // 2), (2, T // 2, T - P), (2, T - P, T))
-        for n, (r, lo, hi) in enumerate(out_pieces):
-            first = keep.tile([P, hi - lo], F32, name=f"first{n}")
-            second = keep.tile([P, hi - lo], F32, name=f"second{n}")
-            total = keep.tile([P, hi - lo], F32, name=f"total{n}")
-            entries = slice(lo // LIST_ROWS, hi // LIST_ROWS)
-            nc.vector.tensor_copy(first[:], y_sb[r][:].indirect(pos_sb[0][:, entries]))
-            nc.vector.tensor_copy(second[:], y_sb[r][:].indirect(pos_sb[1][:, entries]))
-            adder = nc.vector if n == len(out_pieces) - 1 else nc.gpsimd
-            adder.tensor_tensor(total[:], first[:], second[:], ADD)
+        def fetch(r, which, lo, hi):
+            return y_sb[r][:].indirect(pos_sb[which][:, lo // LIST_ROWS : hi // LIST_ROWS])
+
+        def store(r, lo, hi, total):
             nc.sync.dma_start(out[r * P : (r + 1) * P, lo:hi], total[:])
+
+        for r in range(ROW_TILES - 1):
+            first = keep.tile([P, T], F32, name=f"first{r}")
+            second = keep.tile([P, T], F32, name=f"second{r}")
+            total = keep.tile([P, T], F32, name=f"total{r}")
+            nc.vector.tensor_copy(first[:], fetch(r, 0, 0, T))
+            nc.vector.tensor_copy(second[:], fetch(r, 1, 0, T))
+            nc.gpsimd.tensor_tensor(total[:], first[:], second[:], ADD)
+            store(r, 0, T, total)
+        r = ROW_TILES - 1
+        first = keep.tile([P, T], F32, name="first_last")
+        for lo in (0, T // 2):
+            nc.vector.tensor_copy(first[:, lo : lo + T // 2], fetch(r, 0, lo, lo + T // 2))
+        for lo, hi in ((0, T // 2), (T // 2, T - P), (T - P, T)):
+            total = keep.tile([P, hi - lo], F32, name=f"total_last{lo}")
+            nc.vector.tensor_tensor(total[:], fetch(r, 1, lo, hi), first[:, lo:hi], ADD)
+            store(r, lo, hi, total)

@@ -127,7 +127,8 @@ def tile_moe_pre_glu_gelu_kernel(
         nc.sync.dma_start(pos_sb[1][:], pos2)
 
         gathered, woven = {}, {}
-        w3_sums, h_rows, h_bf, h_codes = {}, {}, {}, {}
+        up_sums, w3_sums, h_rows, h_codes = {}, {}, {}, {}
+        h_bf = keep.tile([P, TILES * H], BF16, name="h_bf", align_bytes=64)
 
         def bank(b, shape, name):
             return psum.tile(shape, F32, name=name, tag=f"bank{b}")
@@ -181,60 +182,62 @@ def tile_moe_pre_glu_gelu_kernel(
         def by_pair(sums):
             return sums[:].rearrange("q (p u v) -> q u p v", u=2, v=2)
 
-        def up(j, order=(0, 1)):
-            cols = slice(j * P, (j + 1) * P)
+        def up_pass(j, m, s, first):
+            if first:
+                b = j % W1_BANKS if m == W1 else W1_BANKS + (j - PARKED) % W3_BANKS
+                up_sums[j, m] = bank(b, [P, H], ("w1_sums", "w3_sums")[m])
             e = j * P // C
-            w1_sums = bank(j % W1_BANKS, [P, H], "w1_sums")
-            w3_bank = bank(W1_BANKS + (j - PARKED) % W3_BANKS, [P, H], "w3_sums")
-            for s in order:
-                for m, sums in ((W1, w1_sums), (W3, w3_bank)):
-                    nc.tensor.matmul_mx(
-                        out=sums[:],
-                        lhsT=x_codes[s, j].bitcast(FP8X4),
-                        lhsT_scale=x_scales[s][:, cols],
-                        rhs=up_words[m][e][:, s, :].bitcast(FP4X4),
-                        rhs_scale=up_scales[m][:, e * PASSES + s, :],
-                        start=(s == order[0]),
-                        stop=(s == order[-1]),
-                    )
-            nc.scalar.activation(act[j][:], by_pair(w1_sums), GELU, bias=no_bias[:])
+            nc.tensor.matmul_mx(
+                out=up_sums[j, m][:],
+                lhsT=x_codes[s, j].bitcast(FP8X4),
+                lhsT_scale=x_scales[s][:, j * P : (j + 1) * P],
+                rhs=up_words[m][e][:, s, :].bitcast(FP4X4),
+                rhs_scale=up_scales[m][:, e * PASSES + s, :],
+                start=first,
+                stop=not first,
+            )
+
+        def activate(j):
+            nc.scalar.activation(act[j][:], by_pair(up_sums[j, W1]), GELU, bias=no_bias[:])
             if j < PARKED:
-                nc.scalar.copy(parked[j][:], by_pair(w3_bank))
+                nc.scalar.copy(parked[j][:], by_pair(up_sums[j, W3]))
                 w3_sums[j] = parked[j][:]
             else:
-                w3_sums[j] = by_pair(w3_bank)
+                w3_sums[j] = by_pair(up_sums[j, W3])
+
+        def up(j, order=(0, 1)):
+            for s in order:
+                for m in (W1, W3):
+                    up_pass(j, m, s, s == order[0])
+            activate(j)
 
         def product(j):
             if j == 0:
-                for name, tag, tiles in (("h_first", "window02", (0, 1)), ("h_rest", "x_bf07", range(2, TILES))):
-                    held = keep.tile([P, len(tiles) * H], BF16, name=name, tag=tag, align_bytes=64)
+                h_rest = keep.tile([P, 6 * H], BF16, name="h_rest", tag="x_bf07", align_bytes=64)
+                for held, tiles in ((woven[1, 6], (0, 2)), (h_rest[:], (1, 3, 4, 5, 6, 7))):
                     for n, i in enumerate(tiles):
                         h_rows[i] = held[:, n * H : (n + 1) * H]
             rows = h_rows[j]
-            nc.vector.tensor_tensor(rows.rearrange("q (u p v) -> q u p v", u=2, v=2), w3_sums[j], act[j][:], MULT)
+            engine = nc.gpsimd if j == 1 else nc.vector
+            engine.tensor_tensor(rows.rearrange("q (u p v) -> q u p v", u=2, v=2), act[j][:], w3_sums[j], MULT)
 
-        def turn(j0, j1, b):
-            n = j1 - j0
+        def turn(tiles, b):
+            n = len(tiles)
             turned = bank(b, [P, n, 2, P], "turned")
-            for j in range(j0, j1):
+            for k, j in enumerate(tiles):
                 units = h_rows[j].bitcast(F32)
                 for u in range(2):
-                    a = u * P
-                    nc.tensor.transpose(turned[:, j - j0, u, :], units[:, a : a + P], ident[:])
-            h_bf[j0] = keep.tile([P, n * P * PACK], BF16, name=f"h_bf{j0}", align_bytes=64)
+                    nc.tensor.transpose(turned[:, k, u, :], units[:, u * P : (u + 1) * P], ident[:])
+            words = h_bf[:].bitcast(F32).rearrange("p (j r u) -> p j r u", j=TILES, u=2)
             nc.scalar.copy(
-                h_bf[j0][:].bitcast(F32).rearrange("p (j r u) -> p j r u", j=n, u=2),
-                turned[:].rearrange("p j u r -> p j r u"),
+                words[:, tiles.start : tiles.stop : tiles.step, :, :], turned[:].rearrange("p j u r -> p j r u")
             )
-
-        def finish(j0, j1, b):
-            for j in range(j0, j1):
-                product(j)
-            turn(j0, j1, b)
 
         def quantize_h(j0, j1, codes):
             h_codes[j0] = codes
-            nc.vector.quantize_mx(out=codes.bitcast(FP8X4), scales=h_scales[:, j0 * P : j1 * P], in_=h_bf[j0][:])
+            nc.vector.quantize_mx(
+                out=codes.bitcast(FP8X4), scales=h_scales[:, j0 * P : j1 * P], in_=h_bf[:, j0 * H : j1 * H]
+            )
 
         def down(r, pieces, b, copy):
             j0, j1 = pieces[0][0], pieces[-1][1]
@@ -269,19 +272,26 @@ def tile_moe_pre_glu_gelu_kernel(
         pack_x(0, 4, 7, 4, (6, 7))
         up(3)
         gather(1, 6, 8)
-        pack_x(1, 6, 8, 6, (8,))
+        pack_x(1, 6, 8, 6, (7, 8))
         up(4, (1, 0))
         gather(0, 7, 8)
         pack_x(0, 7, 8, 7, (8,))
         up(5, (1, 0))
         up(6)
-        up(7, (1, 0))
+        up_pass(7, W3, 1, True)
+        product(0)
+        product(2)
+        turn(range(0, 3, 2), 2)
+        up_pass(7, W1, 1, True)
+        up_pass(7, W1, 0, False)
+        up_pass(7, W3, 0, False)
+        activate(7)
 
         pieces = ((0, 2), (2, 4), (4, 6), (6, 7), (7, 8))
-        for j in range(TILES):
+        for j in (1, 3, 4, 5, 6, 7):
             product(j)
-        for (j0, j1), b in zip(pieces, (2, 3, 4, 5, 0)):
-            turn(j0, j1, b)
+        for tiles, b in ((range(1, 4, 2), 3), (range(4, 6), 4), (range(6, 7), 5), (range(7, 8), 0)):
+            turn(tiles, b)
         first_codes = keep.tile([P, C], U32, name="first_codes", tag=f"act{LAST - 1}", align_bytes=64)
         later_codes = keep.tile([P, S - C], U32, name="later_codes", tag=f"act{LAST}", align_bytes=64)
         for j0, j1 in pieces:

@@ -107,12 +107,12 @@ def tile_moe_pre_glu_gelu_kernel(
             words = (w1_words, w3_words)[m]
             queue.dma_start(up_words[m][e][:].bitcast(I32), words[e].rearrange("s p b -> p s b").bitcast(I32))
 
-        nc.sync.dma_start(offs_sb[:], offs)
-        load_gate(nc.sync, 0, P)
         for s in range(PASSES):
             for t in range(PACK):
                 load_window(nc.sync, s, t)
                 if (s, t) == (0, 0):
+                    nc.sync.dma_start(offs_sb[:], offs)
+                    load_gate(nc.sync, 0, P)
                     load_gate(nc.sync, P, FIRST_GATE)
         load_gate(nc.sync, FIRST_GATE, S)
         for queue, (lo, hi) in ((nc.scalar, early), (nc.sync, late)):
@@ -163,7 +163,8 @@ def tile_moe_pre_glu_gelu_kernel(
                 rows[:, :, (a - j0) * P : (z - j0) * P].rearrange("p t (c i) -> p c t i", i=4),
             )
 
-        def quantize_x(s, a, cuts, tag=None):
+        def quantize_x(s, a, cuts, tag=None, first=None):
+            first = a if first is None else first
             z = cuts[-1]
             codes = keep.tile([P, (z - a) * P], U32, name=f"x_codes{s}{a}", tag=tag or f"x_codes{s}{a}", align_bytes=64)
             for j in range(a, z):
@@ -172,11 +173,11 @@ def tile_moe_pre_glu_gelu_kernel(
                 nc.vector.quantize_mx(
                     out=codes[:, (lo - a) * P : (hi - a) * P].bitcast(FP8X4),
                     scales=x_scales[s][:, lo * P : hi * P],
-                    in_=woven[s, a][:, (lo - a) * P * PACK : (hi - a) * P * PACK],
+                    in_=woven[s, first][:, (lo - first) * P * PACK : (hi - first) * P * PACK],
                 )
 
-        def pack_x(s, j0, j1, a, cuts, tag=None):
-            weave(s, j0, j1, a, cuts[-1], tag)
+        def pack_x(s, j0, j1, a, cuts, tag=None, z=None):
+            weave(s, j0, j1, a, z or cuts[-1], tag)
             quantize_x(s, a, cuts)
 
         def by_pair(sums):
@@ -184,7 +185,8 @@ def tile_moe_pre_glu_gelu_kernel(
 
         def up_pass(j, m, s, first):
             if first:
-                b = j % W1_BANKS if m == W1 else W1_BANKS + (j - PARKED) % W3_BANKS
+                banks = (j % W1_BANKS, W1_BANKS + (j - PARKED) % W3_BANKS)
+                b = banks[1 - m] if j >= W3_BANKS else banks[m]
                 up_sums[j, m] = bank(b, [P, H], ("w1_sums", "w3_sums")[m])
             e = j * P // C
             nc.tensor.matmul_mx(
@@ -212,14 +214,9 @@ def tile_moe_pre_glu_gelu_kernel(
             activate(j)
 
         def product(j):
-            if j == 0:
-                h_rest = keep.tile([P, 6 * H], BF16, name="h_rest", tag="x_bf07", align_bytes=64)
-                for held, tiles in ((woven[1, 6], (0, 2)), (h_rest[:], (1, 3, 4, 5, 6, 7))):
-                    for n, i in enumerate(tiles):
-                        h_rows[i] = held[:, n * H : (n + 1) * H]
-            rows = h_rows[j]
-            engine = nc.gpsimd if j == 1 else nc.vector
-            engine.tensor_tensor(rows.rearrange("q (u p v) -> q u p v", u=2, v=2), act[j][:], w3_sums[j], MULT)
+            engine = nc.gpsimd if j < PARKED else nc.vector
+            rows = h_rows[j].rearrange("q (u p v) -> q u p v", u=2, v=2)
+            engine.tensor_tensor(rows, act[j][:], w3_sums[j], MULT)
 
         def turn(tiles, b):
             n = len(tiles)
@@ -259,49 +256,55 @@ def tile_moe_pre_glu_gelu_kernel(
         gather(1, 0, 2)
         pack_x(0, 0, 4, 0, (2,))
         pack_x(0, 0, 4, 2, (4,))
-        pack_x(1, 0, 2, 0, (2,))
-        gather(1, 2, 6)
+        gather(1, 2, 6, (0,))
+        weave(1, 0, 2, 0, 2, into=staged(1, 2, 6)[:, 6 * P :].bitcast(BF16))
+        quantize_x(1, 0, (1, 2))
+        gather(1, 2, 6, (1, 2, 3))
         up(0)
+        up(1)
         fourth = staged(0, 4, 7, room=5 * P)
         gather(0, 4, 7, (0, 1, 2))
         weave(1, 2, 6, 2, 6, into=fourth[:, 9 * P :].bitcast(BF16))
         quantize_x(1, 2, (4, 6))
-        up(1)
         gather(0, 4, 7, (3,))
         up(2)
-        pack_x(0, 4, 7, 4, (6, 7))
+        pack_x(0, 4, 7, 4, (6,), z=7)
+        quantize_x(0, 6, (7,), first=4)
         up(3)
         gather(1, 6, 8)
-        pack_x(1, 6, 8, 6, (7, 8))
+        fifth = keep.tile([P, 3 * H], BF16, name="fifth", align_bytes=64)
+        weave(1, 6, 8, 6, 8, into=fifth[:, H // 2 :])
+        quantize_x(1, 6, (7, 8))
         up(4, (1, 0))
         gather(0, 7, 8)
-        pack_x(0, 7, 8, 7, (8,))
         up(5, (1, 0))
+        pack_x(0, 7, 8, 7, (8,), "x_codes04")
         up(6)
-        up_pass(7, W3, 1, True)
-        product(0)
-        product(2)
-        turn(range(0, 3, 2), 2)
-        up_pass(7, W1, 1, True)
-        up_pass(7, W1, 0, False)
-        up_pass(7, W3, 0, False)
-        activate(7)
-
-        pieces = ((0, 2), (2, 4), (4, 6), (6, 7), (7, 8))
-        for j in (1, 3, 4, 5, 6, 7):
-            product(j)
-        for tiles, b in ((range(1, 4, 2), 3), (range(4, 6), 4), (range(6, 7), 5), (range(7, 8), 0)):
-            turn(tiles, b)
+        up(7, (1, 0))
+        h_rest = keep.tile([P, 5 * H], BF16, name="h_rest", tag="x_codes04", align_bytes=64)
+        for held, tiles in ((fifth[:], (2, 3, 0)), (h_rest[:], (1, 4, 5, 6, 7))):
+            for n, j in enumerate(tiles):
+                h_rows[j] = held[:, n * H : (n + 1) * H]
+        pieces = ((2, 4), (4, 6), (0, 2), (6, 7), (7, 8))
+        for (j0, j1), b in zip(pieces, (2, 3, 4, 5, 6)):
+            for j in range(j0, j1):
+                product(j)
+            turn(range(j0, j1), b)
         first_codes = keep.tile([P, C], U32, name="first_codes", tag=f"act{LAST - 1}", align_bytes=64)
         later_codes = keep.tile([P, S - C], U32, name="later_codes", tag=f"act{LAST}", align_bytes=64)
+        at = 0
         for j0, j1 in pieces:
-            codes = first_codes[:] if j0 == 0 else later_codes[:, j0 * P - C : j1 * P - C]
-            quantize_h(j0, j1, codes)
-        for piece, b in zip(pieces[:3], (6, 7, 2)):
+            if j0 == 2:
+                quantize_h(j0, j1, first_codes[:])
+            else:
+                quantize_h(j0, j1, later_codes[:, at : at + (j1 - j0) * P])
+                at += (j1 - j0) * P
+        for piece, b in zip(pieces[:3], (7, 2, 3)):
             down(0, [piece], b, nc.scalar.copy)
-        for piece, b in zip(pieces[3:], (0, 1)):
+        for piece, b in zip(pieces[3:], (6, 0)):
             down(0, [piece], b, nc.vector.tensor_copy)
-        for r, banks in ((1, (1, 0)), (2, (2, 7))):
+        pieces = sorted(pieces)
+        for r, banks in ((1, (0, 6)), (2, (0, 6))):
             down(r, pieces[:2], banks[0], nc.scalar.copy)
             down(r, pieces[2:], banks[1], nc.scalar.copy)
 

@@ -127,7 +127,7 @@ def tile_moe_pre_glu_gelu_kernel(
         nc.sync.dma_start(pos_sb[1][:], pos2)
 
         gathered, woven = {}, {}
-        up_sums, w3_sums, h_rows, h_codes = {}, {}, {}, {}
+        up_sums, w3_sums, h_rows, h_half, h_codes = {}, {}, {}, {}, {}
         h_bf = keep.tile([P, TILES * H], BF16, name="h_bf", align_bytes=64)
 
         def bank(b, shape, name):
@@ -215,16 +215,15 @@ def tile_moe_pre_glu_gelu_kernel(
 
         def product(j):
             engine = nc.gpsimd if j < PARKED else nc.vector
-            rows = h_rows[j].rearrange("q (u p v) -> q u p v", u=2, v=2)
-            engine.tensor_tensor(rows, act[j][:], w3_sums[j], MULT)
+            engine.tensor_tensor(h_rows[j], act[j][:], w3_sums[j], MULT)
 
         def turn(tiles, b):
             n = len(tiles)
             turned = bank(b, [P, n, 2, P], "turned")
             for k, j in enumerate(tiles):
-                units = h_rows[j].bitcast(F32)
                 for u in range(2):
-                    nc.tensor.transpose(turned[:, k, u, :], units[:, u * P : (u + 1) * P], ident[:])
+                    units = h_half[j, u].bitcast(F32)
+                    nc.tensor.transpose(turned[:, k, u, :], units, ident[:])
             words = h_bf[:].bitcast(F32).rearrange("p (j r u) -> p j r u", j=TILES, u=2)
             nc.scalar.copy(
                 words[:, tiles.start : tiles.stop : tiles.step, :, :], turned[:].rearrange("p j u r -> p j r u")
@@ -272,7 +271,7 @@ def tile_moe_pre_glu_gelu_kernel(
         quantize_x(0, 6, (7,), first=4)
         up(3)
         gather(1, 6, 8)
-        fifth = keep.tile([P, 3 * H], BF16, name="fifth", align_bytes=64)
+        fifth = keep.tile([P, 5 * H // 2], BF16, name="fifth", align_bytes=64)
         weave(1, 6, 8, 6, 8, into=fifth[:, H // 2 :])
         quantize_x(1, 6, (7, 8))
         up(4, (1, 0))
@@ -281,14 +280,23 @@ def tile_moe_pre_glu_gelu_kernel(
         pack_x(0, 7, 8, 7, (8,), "x_codes04")
         up(6)
         up(7, (1, 0))
-        h_rest = keep.tile([P, 5 * H], BF16, name="h_rest", tag="x_codes04", align_bytes=64)
-        for held, tiles in ((fifth[:], (2, 3, 0)), (h_rest[:], (1, 4, 5, 6, 7))):
+        h_rest = keep.tile([P, 11 * H // 2], BF16, name="h_rest", tag="x_codes04", align_bytes=64)
+        for held, tiles in ((fifth[:], (2, 3)), (h_rest[:], (1, 4, 5, 6, 7))):
             for n, j in enumerate(tiles):
-                h_rows[j] = held[:, n * H : (n + 1) * H]
-        pieces = ((2, 4), (4, 6), (0, 2), (6, 7), (7, 8))
-        for (j0, j1), b in zip(pieces, (2, 3, 4, 5, 6)):
+                h_rows[j] = held[:, n * H : (n + 1) * H].rearrange("q (u p v) -> q u p v", u=2, v=2)
+                for u in range(2):
+                    h_half[j, u] = held[:, n * H + u * H // 2 : n * H + (u + 1) * H // 2]
+        h_half[0, 0] = fifth[:, 2 * H :]
+        h_half[0, 1] = h_rest[:, 5 * H :]
+        pieces = ((2, 4), (4, 6), (6, 7), (0, 2), (7, 8))
+        for (j0, j1), b in zip(pieces, (2, 3, 5, 4, 6)):
             for j in range(j0, j1):
-                product(j)
+                if j == 0:
+                    for u in range(2):
+                        half = h_half[0, u].rearrange("q (p v) -> q p v", v=2)
+                        nc.gpsimd.tensor_tensor(half, act[0][:, u], w3_sums[0][:, u], MULT)
+                else:
+                    product(j)
             turn(range(j0, j1), b)
         first_codes = keep.tile([P, C], U32, name="first_codes", tag=f"act{LAST - 1}", align_bytes=64)
         later_codes = keep.tile([P, S - C], U32, name="later_codes", tag=f"act{LAST}", align_bytes=64)
@@ -299,9 +307,9 @@ def tile_moe_pre_glu_gelu_kernel(
             else:
                 quantize_h(j0, j1, later_codes[:, at : at + (j1 - j0) * P])
                 at += (j1 - j0) * P
-        for piece, b in zip(pieces[:3], (7, 2, 3)):
+        for piece, b in zip(((2, 4), (4, 6), (0, 2)), (7, 2, 3)):
             down(0, [piece], b, nc.scalar.copy)
-        for piece, b in zip(pieces[3:], (6, 0)):
+        for piece, b in zip(((6, 7), (7, 8)), (6, 0)):
             down(0, [piece], b, nc.vector.tensor_copy)
         pieces = sorted(pieces)
         for r, banks in ((1, (0, 6)), (2, (0, 6))):

@@ -159,8 +159,8 @@ def tile_moe_pre_glu_gelu_kernel(
             x_bf = into[:, : (z - a) * P * PACK]
             woven[s, a] = x_bf
             nc.scalar.copy(
-                x_bf.rearrange("p (c i t) -> p c t i", i=4, t=PACK),
-                rows[:, :, (a - j0) * P : (z - j0) * P].rearrange("p t (c i) -> p c t i", i=4),
+                x_bf.rearrange("p (c i t) -> p c t i", i=8, t=PACK),
+                rows[:, :, (a - j0) * P : (z - j0) * P].rearrange("p t (c i) -> p c t i", i=8),
             )
 
         def quantize_x(s, a, cuts, tag=None, first=None):

@@ -34,7 +34,7 @@ W1, W3 = 0, 1
 W1_BANKS = 2
 W3_BANKS = 6
 PARKED = TILES - W3_BANKS
-SPARE = 32
+SPARE = 1
 FIRST_GATE = 4 * P
 
 

@@ -66,7 +66,7 @@ def tile_moe_pre_glu_gelu_kernel(
         act = [keep.tile([P, 2, P, 2], F32, name=f"act{j}", tag=f"act{j}", align_bytes=64) for j in range(TILES)]
         parked = [keep.tile([P, 2, P, 2], F32, name=f"parked{j}") for j in range(PARKED)]
         h_scales = keep.tile([P, S], U8, name="h_scales", align_bytes=64)
-        y_sb = [keep.tile([P, S], F32, name=f"y_sb{r}", align_bytes=64) for r in range(ROW_TILES)]
+        y_sb = []
         ident = keep.tile([P, P], F32, name="ident")
 
         zero = keep.tile([P, 1], F32, name="zero")
@@ -307,8 +307,10 @@ def tile_moe_pre_glu_gelu_kernel(
             else:
                 quantize_h(j0, j1, later_codes[:, at : at + (j1 - j0) * P])
                 at += (j1 - j0) * P
-        for piece, b in zip(((2, 4), (4, 6), (0, 2)), (7, 2, 3)):
-            down(0, [piece], b, nc.scalar.copy)
+        y_sb.append(keep.tile([P, S], F32, name="y_sb0", tag="x_codes04", align_bytes=64))
+        y_sb.extend(keep.tile([P, S], F32, name=f"y_sb{r}", align_bytes=64) for r in range(1, ROW_TILES))
+        down(0, [(2, 4), (4, 6)], 7, nc.scalar.copy)
+        down(0, [(0, 2)], 3, nc.scalar.copy)
         for piece, b in zip(((6, 7), (7, 8)), (6, 0)):
             down(0, [piece], b, nc.vector.tensor_copy)
         pieces = sorted(pieces)

@@ -10,8 +10,10 @@ PACK = 4
 PASSES = K // (P * PACK)
 TILES = S // P
 ROW_TILES = N // P
-LAST = TILES - 1
 LIST_ROWS = 16
+RUN = 8
+SPARE = 1
+GATED = 5
 
 WEIGHTS = E * (2 * K * H + H * N)
 FLOPS = 2 * S * (2 * K * H + H * N)
@@ -28,14 +30,9 @@ FP4X4 = mybir.dt.float4_e2m1fn_x4
 MULT = mybir.AluOpType.mult
 ADD = mybir.AluOpType.add
 GELU = mybir.ActivationFunctionType.Gelu_apprx_tanh
+COPY = mybir.ActivationFunctionType.Copy
 
 W1, W3 = 0, 1
-
-W1_BANKS = 2
-W3_BANKS = 6
-PARKED = TILES - W3_BANKS
-SPARE = 1
-FIRST_GATE = 4 * P
 
 
 def tile_moe_pre_glu_gelu_kernel(
@@ -44,14 +41,14 @@ def tile_moe_pre_glu_gelu_kernel(
     nc = tc.nc
     with ExitStack() as ctx:
         keep = ctx.enter_context(tc.tile_pool(name="keep", bufs=1))
-        stage = ctx.enter_context(tc.tile_pool(name="stage", bufs=2))
         psum = ctx.enter_context(tc.psum_pool(name="psum", bufs=1))
 
         offs_sb = keep.tile([P, S // LIST_ROWS], U16, name="offs_sb")
         pos_sb = [keep.tile([P, T // LIST_ROWS], U16, name=f"pos_sb{r}") for r in range(2)]
-        gate_all = keep.tile([P, S], F32, name="gate_all")
+        gate_cuts = (0, 2 * P, GATED * P, S)
+        gate_sb = [keep.tile([P, hi - lo], F32, name=f"gate_sb{lo}", align_bytes=64) for lo, hi in zip(gate_cuts, gate_cuts[1:])]
         window = [
-            [keep.tile([P, T + SPARE], F32, name=f"window{s}{t}", tag=f"window{s}{t}", align_bytes=64) for t in range(PACK)]
+            [keep.tile([P, T + SPARE], F32, name=f"window{s}{t}", align_bytes=64) for t in range(PACK)]
             for s in range(PASSES)
         ]
         up_words = [
@@ -61,178 +58,158 @@ def tile_moe_pre_glu_gelu_kernel(
         up_scales = [keep.tile([P, E * PASSES, H], U8, name=f"up_scales{m}", align_bytes=64) for m in (W1, W3)]
         down_words = keep.tile([P, E, 2 * N], U8, name="down_words", align_bytes=64)
         down_scales = keep.tile([P, E, N], U8, name="down_scales", align_bytes=64)
-        x_codes = {}
         x_scales = [keep.tile([P, S], U8, name=f"x_scales{s}", align_bytes=64) for s in range(PASSES)]
-        act = [keep.tile([P, 2, P, 2], F32, name=f"act{j}", tag=f"act{j}", align_bytes=64) for j in range(TILES)]
-        parked = [keep.tile([P, 2, P, 2], F32, name=f"parked{j}") for j in range(PARKED)]
         h_scales = keep.tile([P, S], U8, name="h_scales", align_bytes=64)
-        y_sb = []
+        y_sb = [keep.tile([P, S], F32, name=f"y_sb{r}", align_bytes=64) for r in range(ROW_TILES)]
         ident = keep.tile([P, P], F32, name="ident")
 
         zero = keep.tile([P, 1], F32, name="zero")
         no_bias = keep.tile([P, 1], F32, name="no_bias")
         nc.gpsimd.memset(zero[:], 0.0)
         nc.scalar.activation(no_bias[:], zero[:], GELU)
-        make_identity(nc, ident[:])
-
         early, late = (0, 2 * PASSES), (2 * PASSES, E * PASSES)
-        for lo, hi in (early, late):
+        for engine, (lo, hi) in ((nc.vector, early), (nc.gpsimd, late)):
             for scales_sb in up_scales:
-                nc.gpsimd.memset(scales_sb[:, lo:hi, :].rearrange("p a b -> p (a b)").bitcast(U32), 0)
-        nc.gpsimd.memset(down_scales[:].rearrange("p a b -> p (a b)").bitcast(U32), 0)
-
+                engine.memset(scales_sb[:, lo:hi, :].rearrange("p a b -> p (a b)").bitcast(U32), 0)
         for planes in window:
             for plane in planes:
-                nc.vector.memset(plane[:, T:], 0.0)
+                nc.gpsimd.memset(plane[:, T:], 0.0)
+        nc.gpsimd.memset(down_scales[:].rearrange("p a b -> p (a b)").bitcast(U32), 0)
+        make_identity(nc, ident[:])
 
-        def gate_sb(lo, hi):
-            return gate_all[:, lo:hi]
+        def load_gate(half):
+            nc.sync.dma_start(gate_sb[half][:], gate[0:P, gate_cuts[half] : gate_cuts[half + 1]])
 
-        def load_gate(queue, lo, hi):
-            queue.dma_start(gate_sb(lo, hi), gate[0:P, lo:hi])
-
-        def load_window(queue, s, t):
+        def load_window(s, t):
             rows = xT[s * P * PACK : (s + 1) * P * PACK, :].rearrange("(p t) c -> p t c", t=PACK)
-            queue.dma_start(window[s][t][:, :T], rows[:, t, :])
+            nc.sync.dma_start(window[s][t][:, :T], rows[:, t, :])
 
-        def load_scales(queue, scales_sb, scales, lo, hi):
+        def load_scales(scales_sb, scales, lo, hi, quad):
             rows = scales.rearrange("e s q i -> q (e s) i")
-            for quad in range(4):
-                queue.dma_start(
-                    scales_sb[32 * quad : 32 * quad + 4, lo:hi, :].bitcast(I32),
-                    rows[4 * quad : 4 * quad + 4, lo:hi, :].bitcast(I32),
-                )
+            nc.sync.dma_start(
+                scales_sb[32 * quad : 32 * quad + 4, lo:hi, :].bitcast(I32),
+                rows[4 * quad : 4 * quad + 4, lo:hi, :].bitcast(I32),
+            )
 
-        def load_up(queue, m, e):
+        def load_up(m, e):
             words = (w1_words, w3_words)[m]
-            queue.dma_start(up_words[m][e][:].bitcast(I32), words[e].rearrange("s p b -> p s b").bitcast(I32))
+            nc.sync.dma_start(up_words[m][e][:].bitcast(I32), words[e].rearrange("s p b -> p s b").bitcast(I32))
 
-        for s in range(PASSES):
-            for t in range(PACK):
-                load_window(nc.sync, s, t)
-                if (s, t) == (0, 0):
-                    nc.sync.dma_start(offs_sb[:], offs)
-                    load_gate(nc.sync, 0, P)
-                    load_gate(nc.sync, P, FIRST_GATE)
-        load_gate(nc.sync, FIRST_GATE, S)
-        for queue, (lo, hi) in ((nc.scalar, early), (nc.sync, late)):
-            load_scales(queue, up_scales[W1], w1_scales, lo, hi)
-            load_scales(queue, up_scales[W3], w3_scales, lo, hi)
-            for e in range(lo // PASSES, hi // PASSES):
-                for m in (W1, W3):
-                    load_up(nc.sync, m, e)
-        load_scales(nc.sync, down_scales, w2_scales, 0, E)
-        nc.sync.dma_start(down_words[:].bitcast(I32), w2_words.rearrange("e s p b -> p (e s) b").bitcast(I32))
+        load_window(1, 0)
+        nc.sync.dma_start(offs_sb[:], offs)
+        load_gate(0)
+        load_window(0, 0)
+        load_gate(1)
+        for t in range(1, PACK):
+            load_window(0, t)
+            load_window(1, t)
+        load_gate(2)
+        for m in (W1, W3):
+            load_up(m, 0)
+        for quad in range(4):
+            load_scales(up_scales[W1], w1_scales, *early, quad)
+            load_scales(up_scales[W3], w3_scales, *early, quad)
+        for e in range(1, E):
+            for m in (W3, W1):
+                load_up(m, e)
         nc.sync.dma_start(pos_sb[0][:], pos1)
         nc.sync.dma_start(pos_sb[1][:], pos2)
+        for quad in range(4):
+            load_scales(down_scales, w2_scales, 0, E, quad)
+        for quad in range(4):
+            load_scales(up_scales[W1], w1_scales, *late, quad)
+            load_scales(up_scales[W3], w3_scales, *late, quad)
+        nc.sync.dma_start(down_words[:].bitcast(I32), w2_words.rearrange("e s p b -> p (e s) b").bitcast(I32))
 
-        gathered, woven = {}, {}
-        up_sums, w3_sums, h_rows, h_half, h_codes = {}, {}, {}, {}, {}
-        h_bf = keep.tile([P, TILES * H], BF16, name="h_bf", align_bytes=64)
+        gathered, x_bf, x_codes, up_sums, act, h_rows, h_bf, h_codes = {}, {}, {}, {}, {}, {}, {}, {}
 
         def bank(b, shape, name):
             return psum.tile(shape, F32, name=name, tag=f"bank{b}")
 
-        def staged(s, j0, j1, room=0):
-            if (s, j0) not in gathered:
-                gathered[s, j0] = stage.tile([P, PACK * (j1 - j0) * P + room], F32, name="gathered", align_bytes=64)
-            return gathered[s, j0][:]
+        def gate_of(a, z):
+            half = (a >= 2) + (a >= GATED)
+            return gate_sb[half][:, a * P - gate_cuts[half] : z * P - gate_cuts[half]]
 
-        def gather(s, j0, j1, planes=range(PACK)):
-            rows = staged(s, j0, j1)[:, : PACK * (j1 - j0) * P].rearrange("p (t c) -> p t c", t=PACK)
-            for t in planes:
-                cuts = (j0, j0 + 1, j1) if (s, j0, t) == (0, 0, 0) else (j0, j1)
-                for a, z in zip(cuts, cuts[1:]):
-                    nc.vector.tensor_tensor(
-                        rows[:, t, (a - j0) * P : (z - j0) * P],
-                        window[s][t][:].indirect(offs_sb[:, a * P // LIST_ROWS : z * P // LIST_ROWS]),
-                        gate_sb(a * P, z * P),
-                        MULT,
-                    )
+        def gather(s, a, z, gated, tag=None, onto=None):
+            if onto is None:
+                name = f"gathered{s}{a}"
+                held = keep.tile([P, PACK * (z - a) * P], F32, name=name, tag=tag or name, align_bytes=64)
+                rows = held[:].rearrange("p (t c) -> p t c", t=PACK)
+            else:
+                earlier, first, was_gated = gathered[onto]
+                rows = earlier[:, :, (onto[1] - first) * P : (onto[1] - first + z - a) * P]
+            for j in range(a, z):
+                gathered[s, j] = (rows, a, gated)
+            for t in range(PACK):
+                source = window[s][t][:].indirect(offs_sb[:, a * P // LIST_ROWS : z * P // LIST_ROWS])
+                if gated:
+                    nc.vector.tensor_tensor(rows[:, t, :], source, gate_of(a, z), MULT)
+                else:
+                    nc.scalar.activation(rows[:, t, :], source, COPY)
 
-        def weave(s, j0, j1, a, z, tag=None, into=None):
-            rows = staged(s, j0, j1)[:, : PACK * (j1 - j0) * P].rearrange("p (t c) -> p t c", t=PACK)
-            if into is None:
-                tag = tag or f"x_bf{s}{a}"
-                held = keep.tile([P, (z - a) * P * PACK], BF16, name=f"x_bf{s}{a}", tag=tag, align_bytes=64)
-                into = held[:]
-            x_bf = into[:, : (z - a) * P * PACK]
-            woven[s, a] = x_bf
-            nc.scalar.copy(
-                x_bf.rearrange("p (c i t) -> p c t i", i=8, t=PACK),
-                rows[:, :, (a - j0) * P : (z - j0) * P].rearrange("p t (c i) -> p c t i", i=8),
-            )
+        def weave(s, a, z, tag=None):
+            rows, first, gated = gathered[s, a]
+            name = f"x_bf{s}{a}"
+            woven = keep.tile([P, (z - a) * P * PACK], BF16, name=name, tag=tag or name, align_bytes=64)
+            x_bf[s, a] = woven
+            target = woven[:].rearrange("p (c i t) -> p c t i", i=RUN, t=PACK)
+            source = rows[:, :, (a - first) * P : (z - first) * P].rearrange("p t (c i) -> p c t i", i=RUN)
+            if gated:
+                nc.vector.tensor_copy(target, source)
+            else:
+                weight = gate_of(a, z).rearrange("p (c i) -> p c i", i=RUN).unsqueeze(2)
+                nc.vector.tensor_tensor(target, source, weight.to_broadcast([P, (z - a) * P // RUN, PACK, RUN]), MULT)
 
-        def quantize_x(s, a, cuts, tag=None, first=None):
-            first = a if first is None else first
-            z = cuts[-1]
-            codes = keep.tile([P, (z - a) * P], U32, name=f"x_codes{s}{a}", tag=tag or f"x_codes{s}{a}", align_bytes=64)
+        def quantize_x(s, a, z):
+            name = f"x_codes{s}{a}"
+            codes = keep.tile([P, (z - a) * P], U32, name=name, tag=name, align_bytes=64)
             for j in range(a, z):
                 x_codes[s, j] = codes[:, (j - a) * P : (j - a + 1) * P]
-            for lo, hi in zip((a,) + cuts, cuts):
-                nc.vector.quantize_mx(
-                    out=codes[:, (lo - a) * P : (hi - a) * P].bitcast(FP8X4),
-                    scales=x_scales[s][:, lo * P : hi * P],
-                    in_=woven[s, first][:, (lo - first) * P * PACK : (hi - first) * P * PACK],
-                )
-
-        def pack_x(s, j0, j1, a, cuts, tag=None, z=None):
-            weave(s, j0, j1, a, z or cuts[-1], tag)
-            quantize_x(s, a, cuts)
+            nc.vector.quantize_mx(
+                out=codes[:].bitcast(FP8X4), scales=x_scales[s][:, a * P : z * P], in_=x_bf[s, a][:]
+            )
 
         def by_pair(sums):
             return sums[:].rearrange("q (p u v) -> q u p v", u=2, v=2)
 
-        def up_pass(j, m, s, first):
-            if first:
-                banks = (j % W1_BANKS, W1_BANKS + (j - PARKED) % W3_BANKS)
-                b = banks[1 - m] if j >= W3_BANKS else banks[m]
-                up_sums[j, m] = bank(b, [P, H], ("w1_sums", "w3_sums")[m])
+        def up(j, s, banks=None):
             e = j * P // C
-            nc.tensor.matmul_mx(
-                out=up_sums[j, m][:],
-                lhsT=x_codes[s, j].bitcast(FP8X4),
-                lhsT_scale=x_scales[s][:, j * P : (j + 1) * P],
-                rhs=up_words[m][e][:, s, :].bitcast(FP4X4),
-                rhs_scale=up_scales[m][:, e * PASSES + s, :],
-                start=first,
-                stop=not first,
-            )
+            for m in (W1, W3):
+                if banks:
+                    up_sums[j, m] = bank(banks[m], [P, H], ("w1_sums", "w3_sums")[m])
+                nc.tensor.matmul_mx(
+                    out=up_sums[j, m][:],
+                    lhsT=x_codes[s, j].bitcast(FP8X4),
+                    lhsT_scale=x_scales[s][:, j * P : (j + 1) * P],
+                    rhs=up_words[m][e][:, s, :].bitcast(FP4X4),
+                    rhs_scale=up_scales[m][:, e * PASSES + s, :],
+                    start=banks is not None,
+                    stop=banks is None,
+                )
 
-        def activate(j):
+        def gelu(j):
+            act[j] = keep.tile([P, 2, P, 2], F32, name=f"act{j}", tag=f"act{j}", align_bytes=64)
             nc.scalar.activation(act[j][:], by_pair(up_sums[j, W1]), GELU, bias=no_bias[:])
-            if j < PARKED:
-                nc.scalar.copy(parked[j][:], by_pair(up_sums[j, W3]))
-                w3_sums[j] = parked[j][:]
-            else:
-                w3_sums[j] = by_pair(up_sums[j, W3])
-
-        def up(j, order=(0, 1)):
-            for s in order:
-                for m in (W1, W3):
-                    up_pass(j, m, s, s == order[0])
-            activate(j)
 
         def product(j):
-            engine = nc.gpsimd if j < PARKED else nc.vector
-            engine.tensor_tensor(h_rows[j], act[j][:], w3_sums[j], MULT)
+            h_rows[j] = keep.tile([P, H], BF16, name=f"h_rows{j}", align_bytes=64)
+            target = h_rows[j][:].rearrange("q (u p v) -> q u p v", u=2, v=2)
+            nc.vector.tensor_tensor(target, act[j][:], by_pair(up_sums[j, W3]), MULT)
 
-        def turn(tiles, b):
-            n = len(tiles)
-            turned = bank(b, [P, n, 2, P], "turned")
-            for k, j in enumerate(tiles):
+        def turn(a, z, b, copy):
+            turned = bank(b, [P, z - a, 2, P], "turned")
+            for j in range(a, z):
+                words = h_rows[j][:].bitcast(F32)
                 for u in range(2):
-                    units = h_half[j, u].bitcast(F32)
-                    nc.tensor.transpose(turned[:, k, u, :], units, ident[:])
-            words = h_bf[:].bitcast(F32).rearrange("p (j r u) -> p j r u", j=TILES, u=2)
-            nc.scalar.copy(
-                words[:, tiles.start : tiles.stop : tiles.step, :, :], turned[:].rearrange("p j u r -> p j r u")
-            )
+                    nc.tensor.transpose(turned[:, j - a, u, :], words[:, u * P : (u + 1) * P], ident[:])
+            h_bf[a] = keep.tile([P, (z - a) * H], BF16, name=f"h_bf{a}", align_bytes=64)
+            words = h_bf[a][:].bitcast(F32).rearrange("p (j r u) -> p j r u", j=z - a, u=2)
+            copy(words, turned[:].rearrange("p j u r -> p j r u"))
 
-        def quantize_h(j0, j1, codes):
-            h_codes[j0] = codes
+        def quantize_h(a, z):
+            h_codes[a] = keep.tile([P, (z - a) * P], U32, name=f"h_codes{a}", align_bytes=64)
             nc.vector.quantize_mx(
-                out=codes.bitcast(FP8X4), scales=h_scales[:, j0 * P : j1 * P], in_=h_bf[:, j0 * H : j1 * H]
+                out=h_codes[a][:].bitcast(FP8X4), scales=h_scales[:, a * P : z * P], in_=h_bf[a][:]
             )
 
         def down(r, pieces, b, copy):
@@ -244,99 +221,111 @@ def tile_moe_pre_glu_gelu_kernel(
                     out=sums[:, (a - j0) * P : (z - j0) * P],
                     lhsT=down_words[:, e, 2 * r * P : 2 * (r + 1) * P].bitcast(FP4X4),
                     lhsT_scale=down_scales[:, e, r * P : (r + 1) * P],
-                    rhs=h_codes[a].bitcast(FP8X4),
+                    rhs=h_codes[a][:].bitcast(FP8X4),
                     rhs_scale=h_scales[:, a * P : z * P],
                     start=True,
                     stop=True,
                 )
             copy(y_sb[r][:, j0 * P : j1 * P], sums[:])
 
-        gather(0, 0, 4)
-        gather(1, 0, 2)
-        pack_x(0, 0, 4, 0, (2,))
-        pack_x(0, 0, 4, 2, (4,))
-        gather(1, 2, 6, (0,))
-        weave(1, 0, 2, 0, 2, into=staged(1, 2, 6)[:, 6 * P :].bitcast(BF16))
-        quantize_x(1, 0, (1, 2))
-        gather(1, 2, 6, (1, 2, 3))
-        up(0)
-        up(1)
-        fourth = staged(0, 4, 7, room=5 * P)
-        gather(0, 4, 7, (0, 1, 2))
-        weave(1, 2, 6, 2, 6, into=fourth[:, 9 * P :].bitcast(BF16))
-        quantize_x(1, 2, (4, 6))
-        gather(0, 4, 7, (3,))
-        up(2)
-        pack_x(0, 4, 7, 4, (6,), z=7)
-        quantize_x(0, 6, (7,), first=4)
-        up(3)
-        gather(1, 6, 8)
-        fifth = keep.tile([P, 5 * H // 2], BF16, name="fifth", align_bytes=64)
-        weave(1, 6, 8, 6, 8, into=fifth[:, H // 2 :])
-        quantize_x(1, 6, (7, 8))
-        up(4, (1, 0))
-        gather(0, 7, 8)
-        up(5, (1, 0))
-        pack_x(0, 7, 8, 7, (8,), "x_codes04")
-        up(6)
-        up(7, (1, 0))
-        h_rest = keep.tile([P, 11 * H // 2], BF16, name="h_rest", tag="x_codes04", align_bytes=64)
-        for held, tiles in ((fifth[:], (2, 3)), (h_rest[:], (1, 4, 5, 6, 7))):
-            for n, j in enumerate(tiles):
-                h_rows[j] = held[:, n * H : (n + 1) * H].rearrange("q (u p v) -> q u p v", u=2, v=2)
-                for u in range(2):
-                    h_half[j, u] = held[:, n * H + u * H // 2 : n * H + (u + 1) * H // 2]
-        h_half[0, 0] = fifth[:, 2 * H :]
-        h_half[0, 1] = h_rest[:, 5 * H :]
-        pieces = ((2, 4), (4, 6), (6, 7), (0, 2), (7, 8))
-        for (j0, j1), b in zip(pieces, (2, 3, 5, 4, 6)):
-            for j in range(j0, j1):
-                if j == 0:
-                    for u in range(2):
-                        half = h_half[0, u].rearrange("q (p v) -> q p v", v=2)
-                        nc.gpsimd.tensor_tensor(half, act[0][:, u], w3_sums[0][:, u], MULT)
-                else:
-                    product(j)
-            turn(range(j0, j1), b)
-        first_codes = keep.tile([P, C], U32, name="first_codes", tag=f"act{LAST - 1}", align_bytes=64)
-        later_codes = keep.tile([P, S - C], U32, name="later_codes", tag=f"act{LAST}", align_bytes=64)
-        at = 0
-        for j0, j1 in pieces:
-            if j0 == 2:
-                quantize_h(j0, j1, first_codes[:])
-            else:
-                quantize_h(j0, j1, later_codes[:, at : at + (j1 - j0) * P])
-                at += (j1 - j0) * P
-        y_sb.append(keep.tile([P, S], F32, name="y_sb0", tag="x_codes04", align_bytes=64))
-        y_sb.extend(keep.tile([P, S], F32, name=f"y_sb{r}", align_bytes=64) for r in range(1, ROW_TILES))
-        down(0, [(2, 4), (4, 6)], 7, nc.scalar.copy)
-        down(0, [(0, 2)], 3, nc.scalar.copy)
-        for piece, b in zip(((6, 7), (7, 8)), (6, 0)):
-            down(0, [piece], b, nc.vector.tensor_copy)
-        pieces = sorted(pieces)
-        for r, banks in ((1, (0, 6)), (2, (0, 6))):
-            down(r, pieces[:2], banks[0], nc.scalar.copy)
-            down(r, pieces[2:], banks[1], nc.scalar.copy)
+        on_scalar, on_vector = nc.scalar.copy, nc.vector.tensor_copy
+
+        gather(1, 0, 4, False)
+        gather(1, 4, 8, False)
+        gather(0, 0, 2, True)
+        gather(0, 2, 5, True)
+        weave(0, 0, 2)
+        weave(1, 0, 1)
+        quantize_x(0, 0, 2)
+        weave(1, 1, 2)
+        quantize_x(1, 0, 1)
+        gather(0, 5, 6, False, "x_bf10")
+        up(0, 0, (0, 1))
+        up(0, 1)
+        gelu(0)
+        weave(0, 2, 4)
+        quantize_x(1, 1, 2)
+        up(1, 0, (2, 3))
+        up(1, 1)
+        gelu(1)
+        gather(0, 6, 8, False, "x_codes11")
+        weave(1, 2, 3)
+        quantize_x(0, 2, 4)
+        weave(1, 3, 4)
+        quantize_x(1, 2, 3)
+        up(2, 0, (4, 5))
+        up(2, 1)
+        gelu(2)
+        weave(0, 4, 5)
+        quantize_x(1, 3, 4)
+        up(3, 0, (6, 7))
+        up(3, 1)
+        gelu(3)
+        weave(1, 4, 5)
+        quantize_x(0, 4, 5)
+        weave(0, 5, 6)
+        quantize_x(1, 4, 5)
+        up(4, 0, (0, 2))
+        up(4, 1)
+        weave(1, 5, 6)
+        quantize_x(0, 5, 6)
+        product(0)
+        quantize_x(1, 5, 6)
+        product(1)
+        up(5, 0, (4, 6))
+        up(5, 1)
+        gelu(4)
+        turn(0, 2, 0, on_scalar)
+        gelu(5)
+        weave(1, 6, 8, "act1")
+        weave(0, 6, 7)
+        quantize_x(1, 6, 8)
+        up(6, 1, (1, 3))
+        weave(0, 7, 8)
+        quantize_x(0, 6, 7)
+        up(6, 0)
+        up(7, 1, (4, 0))
+        gelu(6)
+        product(2)
+        quantize_x(0, 7, 8)
+        up(7, 0)
+        product(3)
+        quantize_h(0, 2)
+        turn(2, 4, 1, on_scalar)
+        gelu(7)
+        product(4)
+        down(0, [(0, 2)], 5, on_scalar)
+        product(5)
+        turn(4, 6, 6, on_scalar)
+        quantize_h(2, 4)
+        product(6)
+        turn(6, 7, 3, on_scalar)
+        product(7)
+        turn(7, 8, 0, on_scalar)
+        quantize_h(4, 6)
+        down(0, [(2, 4), (4, 6)], 7, on_vector)
+        quantize_h(6, 7)
+        quantize_h(7, 8)
+        down(0, [(6, 7), (7, 8)], 4, on_vector)
+        down(1, [(0, 2), (2, 4)], 5, on_scalar)
+        down(1, [(4, 6), (6, 7), (7, 8)], 2, on_scalar)
+        down(2, [(0, 2), (2, 4)], 1, on_scalar)
+        down(2, [(4, 6), (6, 7), (7, 8)], 6, on_scalar)
 
         def fetch(r, which, lo, hi):
             return y_sb[r][:].indirect(pos_sb[which][:, lo // LIST_ROWS : hi // LIST_ROWS])
 
-        def store(r, lo, hi, total):
-            nc.sync.dma_start(out[r * P : (r + 1) * P, lo:hi], total[:])
-
-        for r in range(ROW_TILES - 1):
-            first = keep.tile([P, T], F32, name=f"first{r}")
-            second = keep.tile([P, T], F32, name=f"second{r}")
-            total = keep.tile([P, T], F32, name=f"total{r}")
-            nc.vector.tensor_copy(first[:], fetch(r, 0, 0, T))
-            nc.vector.tensor_copy(second[:], fetch(r, 1, 0, T))
-            nc.gpsimd.tensor_tensor(total[:], first[:], second[:], ADD)
-            store(r, 0, T, total)
-        r = ROW_TILES - 1
-        first = keep.tile([P, T], F32, name="first_last")
-        for lo in (0, T // 2):
-            nc.vector.tensor_copy(first[:, lo : lo + T // 2], fetch(r, 0, lo, lo + T // 2))
-        for lo, hi in ((0, T // 2), (T // 2, T - P), (T - P, T)):
-            total = keep.tile([P, hi - lo], F32, name=f"total_last{lo}")
-            nc.vector.tensor_tensor(total[:], fetch(r, 1, lo, hi), first[:, lo:hi], ADD)
-            store(r, lo, hi, total)
+        half = T // 2
+        for r in range(ROW_TILES):
+            first = [keep.tile([P, half], F32, name=f"first{r}{n}", align_bytes=64) for n in range(2)]
+            for n in range(2):
+                if (r, n) == (0, 1):
+                    nc.vector.tensor_copy(first[n][:], fetch(r, 0, n * half, (n + 1) * half))
+                else:
+                    nc.scalar.activation(first[n][:], fetch(r, 0, n * half, (n + 1) * half), COPY)
+            cuts = (0, half, T - P, T) if r == ROW_TILES - 1 else (0, half, T)
+            for lo, hi in zip(cuts, cuts[1:]):
+                total = keep.tile([P, hi - lo], F32, name=f"total{r}{lo}", align_bytes=64)
+                n = lo // half
+                nc.vector.tensor_tensor(total[:], fetch(r, 1, lo, hi), first[n][:, lo - n * half : hi - n * half], ADD)
+                nc.sync.dma_start(out[r * P : (r + 1) * P, lo:hi], total[:])

@@ -13,7 +13,7 @@ ROW_TILES = N // P
 LIST_ROWS = 16
 RUN = 8
 SPARE = 1
-GATED = 5
+GATED = 2
 
 WEIGHTS = E * (2 * K * H + H * N)
 FLOPS = 2 * S * (2 * K * H + H * N)
@@ -45,7 +45,7 @@ def tile_moe_pre_glu_gelu_kernel(
 
         offs_sb = keep.tile([P, S // LIST_ROWS], U16, name="offs_sb")
         pos_sb = [keep.tile([P, T // LIST_ROWS], U16, name=f"pos_sb{r}") for r in range(2)]
-        gate_cuts = (0, 2 * P, GATED * P, S)
+        gate_cuts = (0, GATED * P, S)
         gate_sb = [keep.tile([P, hi - lo], F32, name=f"gate_sb{lo}", align_bytes=64) for lo, hi in zip(gate_cuts, gate_cuts[1:])]
         window = [
             [keep.tile([P, T + SPARE], F32, name=f"window{s}{t}", align_bytes=64) for t in range(PACK)]
@@ -67,10 +67,8 @@ def tile_moe_pre_glu_gelu_kernel(
         no_bias = keep.tile([P, 1], F32, name="no_bias")
         nc.gpsimd.memset(zero[:], 0.0)
         nc.scalar.activation(no_bias[:], zero[:], GELU)
-        early, late = (0, 2 * PASSES), (2 * PASSES, E * PASSES)
-        for engine, (lo, hi) in ((nc.vector, early), (nc.gpsimd, late)):
-            for scales_sb in up_scales:
-                engine.memset(scales_sb[:, lo:hi, :].rearrange("p a b -> p (a b)").bitcast(U32), 0)
+        for scales_sb in up_scales:
+            nc.vector.memset(scales_sb[:].rearrange("p a b -> p (a b)").bitcast(U32), 0)
         for planes in window:
             for plane in planes:
                 nc.gpsimd.memset(plane[:, T:], 0.0)
@@ -84,41 +82,37 @@ def tile_moe_pre_glu_gelu_kernel(
             rows = xT[s * P * PACK : (s + 1) * P * PACK, :].rearrange("(p t) c -> p t c", t=PACK)
             nc.sync.dma_start(window[s][t][:, :T], rows[:, t, :])
 
-        def load_scales(scales_sb, scales, lo, hi, quad):
+        def load_scales(scales_sb, scales, quad):
             rows = scales.rearrange("e s q i -> q (e s) i")
             nc.sync.dma_start(
-                scales_sb[32 * quad : 32 * quad + 4, lo:hi, :].bitcast(I32),
-                rows[4 * quad : 4 * quad + 4, lo:hi, :].bitcast(I32),
+                scales_sb[32 * quad : 32 * quad + 4].bitcast(I32), rows[4 * quad : 4 * quad + 4].bitcast(I32)
             )
 
-        def load_up(m, e):
-            words = (w1_words, w3_words)[m]
-            nc.sync.dma_start(up_words[m][e][:].bitcast(I32), words[e].rearrange("s p b -> p s b").bitcast(I32))
+        def load_up(m, e, lo=0, hi=PASSES):
+            words = (w1_words, w3_words)[m][e, lo:hi].rearrange("s p b -> p s b")
+            nc.sync.dma_start(up_words[m][e][:, lo:hi, :].bitcast(I32), words.bitcast(I32))
 
         load_window(1, 0)
         nc.sync.dma_start(offs_sb[:], offs)
         load_gate(0)
-        load_window(0, 0)
-        load_gate(1)
         for t in range(1, PACK):
-            load_window(0, t)
             load_window(1, t)
-        load_gate(2)
-        for m in (W1, W3):
+        for t in range(PACK):
+            load_window(0, t)
+        for m, scales in ((W1, w1_scales), (W3, w3_scales)):
             load_up(m, 0)
-        for quad in range(4):
-            load_scales(up_scales[W1], w1_scales, *early, quad)
-            load_scales(up_scales[W3], w3_scales, *early, quad)
+            for quad in range(4):
+                load_scales(up_scales[m], scales, quad)
+            if m == W1:
+                load_gate(1)
         for e in range(1, E):
-            for m in (W3, W1):
-                load_up(m, e)
+            for lo, hi in ((0, PASSES),) if e < 2 else ((1, 2), (0, 1)):
+                for m in (W3, W1) if (e, lo) == (E - 1, 1) else (W1, W3):
+                    load_up(m, e, lo, hi)
         nc.sync.dma_start(pos_sb[0][:], pos1)
         nc.sync.dma_start(pos_sb[1][:], pos2)
         for quad in range(4):
-            load_scales(down_scales, w2_scales, 0, E, quad)
-        for quad in range(4):
-            load_scales(up_scales[W1], w1_scales, *late, quad)
-            load_scales(up_scales[W3], w3_scales, *late, quad)
+            load_scales(down_scales, w2_scales, quad)
         nc.sync.dma_start(down_words[:].bitcast(I32), w2_words.rearrange("e s p b -> p (e s) b").bitcast(I32))
 
         gathered, x_bf, x_codes, up_sums, act, h_rows, h_bf, h_codes = {}, {}, {}, {}, {}, {}, {}, {}
@@ -127,7 +121,7 @@ def tile_moe_pre_glu_gelu_kernel(
             return psum.tile(shape, F32, name=name, tag=f"bank{b}")
 
         def gate_of(a, z):
-            half = (a >= 2) + (a >= GATED)
+            half = int(a >= GATED)
             return gate_sb[half][:, a * P - gate_cuts[half] : z * P - gate_cuts[half]]
 
         def gather(s, a, z, gated, tag=None, onto=None):
@@ -160,6 +154,26 @@ def tile_moe_pre_glu_gelu_kernel(
                 weight = gate_of(a, z).rearrange("p (c i) -> p c i", i=RUN).unsqueeze(2)
                 nc.vector.tensor_tensor(target, source, weight.to_broadcast([P, (z - a) * P // RUN, PACK, RUN]), MULT)
 
+        def first_tiles():
+            width = GATED * P
+            held = keep.tile([P, PASSES * PACK * width], F32, name="gathered_first", align_bytes=64)
+            rows = held[:].rearrange("p (s t c) -> p s t c", s=PASSES, t=PACK)
+            for s in (1, 0):
+                for t in range(PACK):
+                    cuts = range(GATED + 1) if (s, t) == (0, PACK - 1) else (0, GATED)
+                    for a, z in zip(cuts, cuts[1:]):
+                        source = window[s][t][:].indirect(offs_sb[:, a * P // LIST_ROWS : z * P // LIST_ROWS])
+                        nc.vector.tensor_tensor(rows[:, s, t, a * P : z * P], source, gate_of(a, z), MULT)
+            for j in range(GATED):
+                name = f"x_bf_first{j}"
+                woven = keep.tile([P, PASSES * P * PACK], BF16, name=name, tag=name, align_bytes=64)
+                nc.vector.tensor_copy(
+                    woven[:].rearrange("p (s c i t) -> p s c t i", s=PASSES, i=RUN, t=PACK),
+                    rows[:, :, :, j * P : (j + 1) * P].rearrange("p s t (c i) -> p s c t i", i=RUN),
+                )
+                for s in range(PASSES):
+                    x_bf[s, j] = woven[:, s * P * PACK : (s + 1) * P * PACK]
+
         def quantize_x(s, a, z):
             name = f"x_codes{s}{a}"
             codes = keep.tile([P, (z - a) * P], U32, name=name, tag=name, align_bytes=64)
@@ -191,8 +205,9 @@ def tile_moe_pre_glu_gelu_kernel(
             act[j] = keep.tile([P, 2, P, 2], F32, name=f"act{j}", tag=f"act{j}", align_bytes=64)
             nc.scalar.activation(act[j][:], by_pair(up_sums[j, W1]), GELU, bias=no_bias[:])
 
-        def product(j):
-            h_rows[j] = keep.tile([P, H], BF16, name=f"h_rows{j}", align_bytes=64)
+        def product(j, tag=None):
+            name = f"h_rows{j}"
+            h_rows[j] = keep.tile([P, H], BF16, name=name, tag=tag or name, align_bytes=64)
             target = h_rows[j][:].rearrange("q (u p v) -> q u p v", u=2, v=2)
             nc.vector.tensor_tensor(target, act[j][:], by_pair(up_sums[j, W3]), MULT)
 
@@ -230,87 +245,82 @@ def tile_moe_pre_glu_gelu_kernel(
 
         on_scalar, on_vector = nc.scalar.copy, nc.vector.tensor_copy
 
-        gather(1, 0, 4, False)
-        gather(1, 4, 8, False)
-        gather(0, 0, 2, True)
-        gather(0, 2, 5, True)
-        weave(0, 0, 2)
-        weave(1, 0, 1)
-        quantize_x(0, 0, 2)
-        weave(1, 1, 2)
-        quantize_x(1, 0, 1)
-        gather(0, 5, 6, False, "x_bf10")
-        up(0, 0, (0, 1))
-        up(0, 1)
-        gelu(0)
-        weave(0, 2, 4)
-        quantize_x(1, 1, 2)
-        up(1, 0, (2, 3))
-        up(1, 1)
-        gelu(1)
-        gather(0, 6, 8, False, "x_codes11")
-        weave(1, 2, 3)
-        quantize_x(0, 2, 4)
-        weave(1, 3, 4)
-        quantize_x(1, 2, 3)
-        up(2, 0, (4, 5))
-        up(2, 1)
-        gelu(2)
-        weave(0, 4, 5)
-        quantize_x(1, 3, 4)
-        up(3, 0, (6, 7))
-        up(3, 1)
-        gelu(3)
+        gather(1, 2, 5, False)
+        gather(1, 5, 8, False)
+        gather(0, 2, 4, False)
+        first_tiles()
+        for j in range(2):
+            quantize_x(1, j, j + 1)
+            quantize_x(0, j, j + 1)
+        weave(1, 2, 4)
+        for j in range(2):
+            up(j, 1, (2 * j, 2 * j + 1))
+            up(j, 0)
+            gelu(j)
+        gather(0, 4, 6, False, "x_codes01")
         weave(1, 4, 5)
-        quantize_x(0, 4, 5)
-        weave(0, 5, 6)
-        quantize_x(1, 4, 5)
-        up(4, 0, (0, 2))
-        up(4, 1)
+        quantize_x(1, 2, 4)
         weave(1, 5, 6)
-        quantize_x(0, 5, 6)
-        product(0)
+        quantize_x(1, 4, 5)
+        weave(0, 2, 3)
         quantize_x(1, 5, 6)
+        weave(0, 3, 4)
+        quantize_x(0, 2, 3)
+        weave(1, 6, 7)
+        quantize_x(0, 3, 4)
+        for j in range(2, 4):
+            up(j, 1, (2 * j, 2 * j + 1))
+            up(j, 0)
+            gelu(j)
+        gather(0, 6, 7, False, "x_codes02")
+        weave(1, 7, 8)
+        quantize_x(1, 6, 7)
+        product(0)
+        quantize_x(1, 7, 8)
         product(1)
-        up(5, 0, (4, 6))
-        up(5, 1)
-        gelu(4)
-        turn(0, 2, 0, on_scalar)
-        gelu(5)
-        weave(1, 6, 8, "act1")
-        weave(0, 6, 7)
-        quantize_x(1, 6, 8)
-        up(6, 1, (1, 3))
-        weave(0, 7, 8)
-        quantize_x(0, 6, 7)
-        up(6, 0)
-        up(7, 1, (4, 0))
-        gelu(6)
+        gather(0, 7, 8, False, "x_codes03")
+        weave(0, 4, 5)
+        weave(0, 5, 6)
+        quantize_x(0, 4, 5)
+        up(4, 1, (0, 2))
+        up(4, 0)
         product(2)
+        quantize_x(0, 5, 6)
+        up(5, 1, (1, 3))
+        up(5, 0)
+        weave(0, 6, 7)
+        product(3)
+        quantize_x(0, 6, 7)
+        gelu(4)
+        gelu(5)
+        turn(0, 2, 6, on_scalar)
+        up(6, 1, (0, 4))
+        up(7, 1, (1, 5))
+        up(6, 0)
+        weave(0, 7, 8)
+        quantize_h(0, 2)
         quantize_x(0, 7, 8)
         up(7, 0)
-        product(3)
-        quantize_h(0, 2)
-        turn(2, 4, 1, on_scalar)
-        gelu(7)
+        gelu(6)
         product(4)
-        down(0, [(0, 2)], 5, on_scalar)
+        gelu(7)
+        turn(2, 4, 0, on_scalar)
         product(5)
-        turn(4, 6, 6, on_scalar)
-        quantize_h(2, 4)
+        turn(4, 6, 1, on_scalar)
         product(6)
-        turn(6, 7, 3, on_scalar)
         product(7)
-        turn(7, 8, 0, on_scalar)
+        turn(6, 7, 4, on_scalar)
+        turn(7, 8, 5, on_scalar)
+        quantize_h(2, 4)
+        down(0, [(0, 2), (2, 4)], 7, on_scalar)
+        down(1, [(0, 2), (2, 4)], 6, on_scalar)
         quantize_h(4, 6)
-        down(0, [(2, 4), (4, 6)], 7, on_vector)
+        down(0, [(4, 6)], 2, on_vector)
         quantize_h(6, 7)
         quantize_h(7, 8)
-        down(0, [(6, 7), (7, 8)], 4, on_vector)
-        down(1, [(0, 2), (2, 4)], 5, on_scalar)
-        down(1, [(4, 6), (6, 7), (7, 8)], 2, on_scalar)
-        down(2, [(0, 2), (2, 4)], 1, on_scalar)
-        down(2, [(4, 6), (6, 7), (7, 8)], 6, on_scalar)
+        down(0, [(6, 7), (7, 8)], 3, on_vector)
+        down(2, [(0, 2), (2, 4)], 0, on_vector)
+        down(1, [(4, 6), (6, 7), (7, 8)], 1, on_scalar)
 
         def fetch(r, which, lo, hi):
             return y_sb[r][:].indirect(pos_sb[which][:, lo // LIST_ROWS : hi // LIST_ROWS])
@@ -323,6 +333,8 @@ def tile_moe_pre_glu_gelu_kernel(
                     nc.vector.tensor_copy(first[n][:], fetch(r, 0, n * half, (n + 1) * half))
                 else:
                     nc.scalar.activation(first[n][:], fetch(r, 0, n * half, (n + 1) * half), COPY)
+                if (r, n) == (0, 0):
+                    down(2, [(4, 6), (6, 7), (7, 8)], 4, on_scalar)
             cuts = (0, half, T - P, T) if r == ROW_TILES - 1 else (0, half, T)
             for lo, hi in zip(cuts, cuts[1:]):
                 total = keep.tile([P, hi - lo], F32, name=f"total{r}{lo}", align_bytes=64)

@@ -99,12 +99,11 @@ def tile_moe_pre_glu_gelu_kernel(
             load_window(1, t)
         for t in range(PACK):
             load_window(0, t)
+        load_gate(1)
         for m, scales in ((W1, w1_scales), (W3, w3_scales)):
             load_up(m, 0)
             for quad in range(4):
                 load_scales(up_scales[m], scales, quad)
-            if m == W1:
-                load_gate(1)
         for e in range(1, E):
             for lo, hi in ((0, PASSES),) if e < 2 else ((1, 2), (0, 1)):
                 for m in (W3, W1) if (e, lo) == (E - 1, 1) else (W1, W3):

@@ -116,6 +116,8 @@ def tile_moe_pre_glu_gelu_kernel(
 
         gathered, x_bf, x_codes, up_sums, act, h_rows, h_bf, h_codes = {}, {}, {}, {}, {}, {}, {}, {}
 
+        first_bf, x_plane = {}, {}
+
         def bank(b, shape, name):
             return psum.tile(shape, F32, name=name, tag=f"bank{b}")
 
@@ -170,14 +172,23 @@ def tile_moe_pre_glu_gelu_kernel(
                     woven[:].rearrange("p (s c i t) -> p s c t i", s=PASSES, i=RUN, t=PACK),
                     rows[:, :, :, j * P : (j + 1) * P].rearrange("p s t (c i) -> p s c t i", i=RUN),
                 )
-                for s in range(PASSES):
-                    x_bf[s, j] = woven[:, s * P * PACK : (s + 1) * P * PACK]
+                first_bf[j] = woven
+
+        def quantize_first(j):
+            name = f"x_codes_first{j}"
+            codes = keep.tile([P, PASSES * P], U32, name=name, tag=name, align_bytes=64)
+            scales = keep.tile([P, PASSES * P], U8, name=f"x_scales_first{j}", align_bytes=64)
+            for s in range(PASSES):
+                x_codes[s, j] = codes[:, s * P : (s + 1) * P]
+                x_plane[s, j] = scales[:, s * P : (s + 1) * P]
+            nc.vector.quantize_mx(out=codes[:].bitcast(FP8X4), scales=scales[:], in_=first_bf[j][:])
 
         def quantize_x(s, a, z):
             name = f"x_codes{s}{a}"
             codes = keep.tile([P, (z - a) * P], U32, name=name, tag=name, align_bytes=64)
             for j in range(a, z):
                 x_codes[s, j] = codes[:, (j - a) * P : (j - a + 1) * P]
+                x_plane[s, j] = x_scales[s][:, j * P : (j + 1) * P]
             nc.vector.quantize_mx(
                 out=codes[:].bitcast(FP8X4), scales=x_scales[s][:, a * P : z * P], in_=x_bf[s, a][:]
             )
@@ -193,7 +204,7 @@ def tile_moe_pre_glu_gelu_kernel(
                 nc.tensor.matmul_mx(
                     out=up_sums[j, m][:],
                     lhsT=x_codes[s, j].bitcast(FP8X4),
-                    lhsT_scale=x_scales[s][:, j * P : (j + 1) * P],
+                    lhsT_scale=x_plane[s, j],
                     rhs=up_words[m][e][:, s, :].bitcast(FP4X4),
                     rhs_scale=up_scales[m][:, e * PASSES + s, :],
                     start=banks is not None,
@@ -220,8 +231,9 @@ def tile_moe_pre_glu_gelu_kernel(
             words = h_bf[a][:].bitcast(F32).rearrange("p (j r u) -> p j r u", j=z - a, u=2)
             copy(words, turned[:].rearrange("p j u r -> p j r u"))
 
-        def quantize_h(a, z):
-            h_codes[a] = keep.tile([P, (z - a) * P], U32, name=f"h_codes{a}", align_bytes=64)
+        def quantize_h(a, z, tag=None):
+            name = f"h_codes{a}"
+            h_codes[a] = keep.tile([P, (z - a) * P], U32, name=name, tag=tag or name, align_bytes=64)
             nc.vector.quantize_mx(
                 out=h_codes[a][:].bitcast(FP8X4), scales=h_scales[:, a * P : z * P], in_=h_bf[a][:]
             )
@@ -244,52 +256,47 @@ def tile_moe_pre_glu_gelu_kernel(
 
         on_scalar, on_vector = nc.scalar.copy, nc.vector.tensor_copy
 
-        gather(1, 2, 5, False)
-        gather(1, 5, 8, False)
+        gather(1, 2, 6, False)
+        gather(1, 6, 8, False)
         gather(0, 2, 4, False)
         first_tiles()
-        for j in range(2):
-            quantize_x(1, j, j + 1)
-            quantize_x(0, j, j + 1)
+        quantize_first(0)
+        quantize_first(1)
         weave(1, 2, 4)
+        gather(0, 4, 6, False, "x_bf_first0")
         for j in range(2):
             up(j, 1, (2 * j, 2 * j + 1))
             up(j, 0)
             gelu(j)
-        gather(0, 4, 6, False, "x_codes01")
-        weave(1, 4, 5)
+        gather(0, 6, 7, False, "x_codes_first1")
+        weave(1, 4, 6)
         quantize_x(1, 2, 4)
-        weave(1, 5, 6)
-        quantize_x(1, 4, 5)
         weave(0, 2, 3)
-        quantize_x(1, 5, 6)
+        quantize_x(1, 4, 6)
         weave(0, 3, 4)
         quantize_x(0, 2, 3)
-        weave(1, 6, 7)
+        weave(1, 6, 8)
         quantize_x(0, 3, 4)
         for j in range(2, 4):
             up(j, 1, (2 * j, 2 * j + 1))
             up(j, 0)
             gelu(j)
-        gather(0, 6, 7, False, "x_codes02")
-        weave(1, 7, 8)
-        quantize_x(1, 6, 7)
-        product(0)
-        quantize_x(1, 7, 8)
-        product(1)
         gather(0, 7, 8, False, "x_codes03")
         weave(0, 4, 5)
+        quantize_x(1, 6, 8)
         weave(0, 5, 6)
         quantize_x(0, 4, 5)
         up(4, 1, (0, 2))
         up(4, 0)
-        product(2)
+        product(0)
         quantize_x(0, 5, 6)
+        product(1)
         up(5, 1, (1, 3))
         up(5, 0)
         weave(0, 6, 7)
-        product(3)
+        product(2)
         quantize_x(0, 6, 7)
+        product(3)
         gelu(4)
         gelu(5)
         turn(0, 2, 6, on_scalar)
@@ -297,11 +304,11 @@ def tile_moe_pre_glu_gelu_kernel(
         up(7, 1, (1, 5))
         up(6, 0)
         weave(0, 7, 8)
-        quantize_h(0, 2)
         quantize_x(0, 7, 8)
         up(7, 0)
         gelu(6)
         product(4)
+        quantize_h(0, 2, "x_bf07")
         gelu(7)
         turn(2, 4, 0, on_scalar)
         product(5)
@@ -314,29 +321,30 @@ def tile_moe_pre_glu_gelu_kernel(
         down(0, [(0, 2), (2, 4)], 7, on_scalar)
         down(1, [(0, 2), (2, 4)], 6, on_scalar)
         quantize_h(4, 6)
-        down(0, [(4, 6)], 2, on_vector)
         quantize_h(6, 7)
+        down(0, [(4, 6), (6, 7)], 2, on_vector)
         quantize_h(7, 8)
-        down(0, [(6, 7), (7, 8)], 3, on_vector)
+        down(0, [(7, 8)], 3, on_vector)
+        down(1, [(4, 6), (6, 7)], 1, on_scalar)
+        down(1, [(7, 8)], 4, on_scalar)
         down(2, [(0, 2), (2, 4)], 0, on_vector)
-        down(1, [(4, 6), (6, 7), (7, 8)], 1, on_scalar)
 
         def fetch(r, which, lo, hi):
             return y_sb[r][:].indirect(pos_sb[which][:, lo // LIST_ROWS : hi // LIST_ROWS])
 
         half = T // 2
+        first = {(r, lo): keep.tile([P, half], F32, name=f"first{r}{lo}", align_bytes=64) for r in range(ROW_TILES) for lo in (0, half)}
+        for r, lo in first:
+            if (r, lo) == (0, half):
+                nc.vector.tensor_copy(first[r, lo][:], fetch(r, 0, lo, lo + half))
+            else:
+                nc.scalar.activation(first[r, lo][:], fetch(r, 0, lo, lo + half), COPY)
+            if (r, lo) == (1, 0):
+                down(2, [(4, 6), (6, 7), (7, 8)], 5, on_scalar)
         for r in range(ROW_TILES):
-            first = [keep.tile([P, half], F32, name=f"first{r}{n}", align_bytes=64) for n in range(2)]
-            for n in range(2):
-                if (r, n) == (0, 1):
-                    nc.vector.tensor_copy(first[n][:], fetch(r, 0, n * half, (n + 1) * half))
-                else:
-                    nc.scalar.activation(first[n][:], fetch(r, 0, n * half, (n + 1) * half), COPY)
-                if (r, n) == (0, 0):
-                    down(2, [(4, 6), (6, 7), (7, 8)], 4, on_scalar)
             cuts = (0, half, T - P, T) if r == ROW_TILES - 1 else (0, half, T)
             for lo, hi in zip(cuts, cuts[1:]):
                 total = keep.tile([P, hi - lo], F32, name=f"total{r}{lo}", align_bytes=64)
-                n = lo // half
-                nc.vector.tensor_tensor(total[:], fetch(r, 1, lo, hi), first[n][:, lo - n * half : hi - n * half], ADD)
+                start = lo // half * half
+                nc.vector.tensor_tensor(total[:], fetch(r, 1, lo, hi), first[r, start][:, lo - start : hi - start], ADD)
                 nc.sync.dma_start(out[r * P : (r + 1) * P, lo:hi], total[:])

@@ -8,12 +8,12 @@ S = E * C
 P = 128
 PACK = 4
 PASSES = K // (P * PACK)
-TILES = S // P
 ROW_TILES = N // P
 LIST_ROWS = 16
 RUN = 8
 SPARE = 1
 GATED = 2
+SHARED = 2
 
 WEIGHTS = E * (2 * K * H + H * N)
 FLOPS = 2 * S * (2 * K * H + H * N)
@@ -46,7 +46,10 @@ def tile_moe_pre_glu_gelu_kernel(
         offs_sb = keep.tile([P, S // LIST_ROWS], U16, name="offs_sb")
         pos_sb = [keep.tile([P, T // LIST_ROWS], U16, name=f"pos_sb{r}") for r in range(2)]
         gate_cuts = (0, GATED * P, S)
-        gate_sb = [keep.tile([P, hi - lo], F32, name=f"gate_sb{lo}", align_bytes=64) for lo, hi in zip(gate_cuts, gate_cuts[1:])]
+        gate_sb = [
+            keep.tile([P, hi - lo], F32, name=f"gate_sb{lo}", align_bytes=64)
+            for lo, hi in zip(gate_cuts, gate_cuts[1:])
+        ]
         window = [
             [keep.tile([P, T + SPARE], F32, name=f"window{s}{t}", align_bytes=64) for t in range(PACK)]
             for s in range(PASSES)
@@ -69,14 +72,14 @@ def tile_moe_pre_glu_gelu_kernel(
         nc.scalar.activation(no_bias[:], zero[:], GELU)
         for scales_sb in up_scales:
             nc.vector.memset(scales_sb[:].rearrange("p a b -> p (a b)").bitcast(U32), 0)
-        for planes in window:
-            for plane in planes:
-                nc.gpsimd.memset(plane[:, T:], 0.0)
+        for pass_windows in window:
+            for one in pass_windows:
+                nc.gpsimd.memset(one[:, T:], 0.0)
         nc.gpsimd.memset(down_scales[:].rearrange("p a b -> p (a b)").bitcast(U32), 0)
         make_identity(nc, ident[:])
 
-        def load_gate(half):
-            nc.sync.dma_start(gate_sb[half][:], gate[0:P, gate_cuts[half] : gate_cuts[half + 1]])
+        def load_gate(piece):
+            nc.sync.dma_start(gate_sb[piece][:], gate[0:P, gate_cuts[piece] : gate_cuts[piece + 1]])
 
         def load_window(s, t):
             rows = xT[s * P * PACK : (s + 1) * P * PACK, :].rearrange("(p t) c -> p t c", t=PACK)
@@ -104,56 +107,53 @@ def tile_moe_pre_glu_gelu_kernel(
             load_up(m, 0)
             for quad in range(4):
                 load_scales(up_scales[m], scales, quad)
-        for e in range(1, E):
-            for lo, hi in ((0, PASSES),) if e < 2 else ((1, 2), (0, 1)):
-                for m in (W3, W1) if (e, lo) == (E - 1, 1) else (W1, W3):
-                    load_up(m, e, lo, hi)
+        for m in (W1, W3):
+            load_up(m, 1)
+        for e, s, order in ((2, 1, (W1, W3)), (2, 0, (W1, W3)), (3, 1, (W3, W1)), (3, 0, (W1, W3))):
+            for m in order:
+                load_up(m, e, s, s + 1)
         nc.sync.dma_start(pos_sb[0][:], pos1)
         nc.sync.dma_start(pos_sb[1][:], pos2)
         for quad in range(4):
             load_scales(down_scales, w2_scales, quad)
         nc.sync.dma_start(down_words[:].bitcast(I32), w2_words.rearrange("e s p b -> p (e s) b").bitcast(I32))
 
-        gathered, x_bf, x_codes, up_sums, act, h_rows, h_bf, h_codes = {}, {}, {}, {}, {}, {}, {}, {}
-
-        first_bf, x_plane = {}, {}
+        gathered, first_bf, x_bf, x_codes, x_plane = {}, {}, {}, {}, {}
+        up_sums, act, h_rows, h_bf, h_codes = {}, {}, {}, {}, {}
 
         def bank(b, shape, name):
             return psum.tile(shape, F32, name=name, tag=f"bank{b}")
 
         def gate_of(a, z):
-            half = int(a >= GATED)
-            return gate_sb[half][:, a * P - gate_cuts[half] : z * P - gate_cuts[half]]
+            piece = int(a >= GATED)
+            return gate_sb[piece][:, a * P - gate_cuts[piece] : z * P - gate_cuts[piece]]
 
-        def gather(s, a, z, gated, tag=None, onto=None):
-            if onto is None:
-                name = f"gathered{s}{a}"
-                held = keep.tile([P, PACK * (z - a) * P], F32, name=name, tag=tag or name, align_bytes=64)
-                rows = held[:].rearrange("p (t c) -> p t c", t=PACK)
-            else:
-                earlier, first, was_gated = gathered[onto]
-                rows = earlier[:, :, (onto[1] - first) * P : (onto[1] - first + z - a) * P]
+        def look_up(s, t, a, z):
+            return window[s][t][:].indirect(offs_sb[:, a * P // LIST_ROWS : z * P // LIST_ROWS])
+
+        def gather(s, a, z, on=None, shared=0):
+            name = f"gathered{s}{a}"
+            held = keep.tile([P, PACK * (z - a) * P], F32, name=name, tag=on or name, align_bytes=64)
+            rows = held[:].rearrange("p (t c) -> p t c", t=PACK)
             for j in range(a, z):
-                gathered[s, j] = (rows, a, gated)
+                gathered[s, j] = (rows, a)
             for t in range(PACK):
-                source = window[s][t][:].indirect(offs_sb[:, a * P // LIST_ROWS : z * P // LIST_ROWS])
-                if gated:
-                    nc.vector.tensor_tensor(rows[:, t, :], source, gate_of(a, z), MULT)
+                if t < PACK - shared:
+                    nc.scalar.activation(rows[:, t, :], look_up(s, t, a, z), COPY)
                 else:
-                    nc.scalar.activation(rows[:, t, :], source, COPY)
+                    nc.vector.tensor_copy(rows[:, t, :], look_up(s, t, a, z))
 
-        def weave(s, a, z, tag=None):
-            rows, first, gated = gathered[s, a]
+        def weave(s, a, z):
+            rows, start = gathered[s, a]
             name = f"x_bf{s}{a}"
-            woven = keep.tile([P, (z - a) * P * PACK], BF16, name=name, tag=tag or name, align_bytes=64)
-            x_bf[s, a] = woven
-            target = woven[:].rearrange("p (c i t) -> p c t i", i=RUN, t=PACK)
-            source = rows[:, :, (a - first) * P : (z - first) * P].rearrange("p t (c i) -> p c t i", i=RUN)
-            if gated:
-                nc.vector.tensor_copy(target, source)
-            else:
-                weight = gate_of(a, z).rearrange("p (c i) -> p c i", i=RUN).unsqueeze(2)
-                nc.vector.tensor_tensor(target, source, weight.to_broadcast([P, (z - a) * P // RUN, PACK, RUN]), MULT)
+            x_bf[s, a] = keep.tile([P, (z - a) * P * PACK], BF16, name=name, tag=name, align_bytes=64)
+            weight = gate_of(a, z).rearrange("p (c i) -> p c i", i=RUN).unsqueeze(2)
+            nc.vector.tensor_tensor(
+                x_bf[s, a][:].rearrange("p (c i t) -> p c t i", i=RUN, t=PACK),
+                rows[:, :, (a - start) * P : (z - start) * P].rearrange("p t (c i) -> p c t i", i=RUN),
+                weight.to_broadcast([P, (z - a) * P // RUN, PACK, RUN]),
+                MULT,
+            )
 
         def first_tiles():
             width = GATED * P
@@ -163,8 +163,7 @@ def tile_moe_pre_glu_gelu_kernel(
                 for t in range(PACK):
                     cuts = range(GATED + 1) if (s, t) == (0, PACK - 1) else (0, GATED)
                     for a, z in zip(cuts, cuts[1:]):
-                        source = window[s][t][:].indirect(offs_sb[:, a * P // LIST_ROWS : z * P // LIST_ROWS])
-                        nc.vector.tensor_tensor(rows[:, s, t, a * P : z * P], source, gate_of(a, z), MULT)
+                        nc.vector.tensor_tensor(rows[:, s, t, a * P : z * P], look_up(s, t, a, z), gate_of(a, z), MULT)
             for j in range(GATED):
                 name = f"x_bf_first{j}"
                 woven = keep.tile([P, PASSES * P * PACK], BF16, name=name, tag=name, align_bytes=64)
@@ -212,16 +211,15 @@ def tile_moe_pre_glu_gelu_kernel(
                 )
 
         def gelu(j):
-            act[j] = keep.tile([P, 2, P, 2], F32, name=f"act{j}", tag=f"act{j}", align_bytes=64)
+            act[j] = keep.tile([P, 2, P, 2], F32, name=f"act{j}", align_bytes=64)
             nc.scalar.activation(act[j][:], by_pair(up_sums[j, W1]), GELU, bias=no_bias[:])
 
-        def product(j, tag=None):
-            name = f"h_rows{j}"
-            h_rows[j] = keep.tile([P, H], BF16, name=name, tag=tag or name, align_bytes=64)
+        def product(j):
+            h_rows[j] = keep.tile([P, H], BF16, name=f"h_rows{j}", align_bytes=64)
             target = h_rows[j][:].rearrange("q (u p v) -> q u p v", u=2, v=2)
             nc.vector.tensor_tensor(target, act[j][:], by_pair(up_sums[j, W3]), MULT)
 
-        def turn(a, z, b, copy):
+        def turn(a, z, b):
             turned = bank(b, [P, z - a, 2, P], "turned")
             for j in range(a, z):
                 words = h_rows[j][:].bitcast(F32)
@@ -229,11 +227,11 @@ def tile_moe_pre_glu_gelu_kernel(
                     nc.tensor.transpose(turned[:, j - a, u, :], words[:, u * P : (u + 1) * P], ident[:])
             h_bf[a] = keep.tile([P, (z - a) * H], BF16, name=f"h_bf{a}", align_bytes=64)
             words = h_bf[a][:].bitcast(F32).rearrange("p (j r u) -> p j r u", j=z - a, u=2)
-            copy(words, turned[:].rearrange("p j u r -> p j r u"))
+            nc.scalar.copy(words, turned[:].rearrange("p j u r -> p j r u"))
 
-        def quantize_h(a, z, tag=None):
+        def quantize_h(a, z, on=None):
             name = f"h_codes{a}"
-            h_codes[a] = keep.tile([P, (z - a) * P], U32, name=name, tag=tag or name, align_bytes=64)
+            h_codes[a] = keep.tile([P, (z - a) * P], U32, name=name, tag=on or name, align_bytes=64)
             nc.vector.quantize_mx(
                 out=h_codes[a][:].bitcast(FP8X4), scales=h_scales[:, a * P : z * P], in_=h_bf[a][:]
             )
@@ -256,19 +254,19 @@ def tile_moe_pre_glu_gelu_kernel(
 
         on_scalar, on_vector = nc.scalar.copy, nc.vector.tensor_copy
 
-        gather(1, 2, 6, False)
-        gather(1, 6, 8, False)
-        gather(0, 2, 4, False)
+        gather(1, 2, 6)
+        gather(1, 6, 8)
+        gather(0, 2, 4)
         first_tiles()
         quantize_first(0)
         quantize_first(1)
         weave(1, 2, 4)
-        gather(0, 4, 6, False, "x_bf_first0")
+        gather(0, 4, 6, on="x_bf_first0")
         for j in range(2):
             up(j, 1, (2 * j, 2 * j + 1))
             up(j, 0)
             gelu(j)
-        gather(0, 6, 7, False, "x_codes_first1")
+        gather(0, 6, 7, on="x_codes_first1")
         weave(1, 4, 6)
         quantize_x(1, 2, 4)
         weave(0, 2, 3)
@@ -281,42 +279,42 @@ def tile_moe_pre_glu_gelu_kernel(
             up(j, 1, (2 * j, 2 * j + 1))
             up(j, 0)
             gelu(j)
-        gather(0, 7, 8, False, "x_codes03")
-        weave(0, 4, 5)
+
         quantize_x(1, 6, 8)
-        weave(0, 5, 6)
-        quantize_x(0, 4, 5)
+        weave(0, 4, 6)
+        product(0)
+        quantize_x(0, 4, 6)
         up(4, 1, (0, 2))
         up(4, 0)
-        product(0)
-        quantize_x(0, 5, 6)
         product(1)
         up(5, 1, (1, 3))
         up(5, 0)
         weave(0, 6, 7)
         product(2)
+        gather(0, 7, 8, on="x_codes03", shared=SHARED)
         quantize_x(0, 6, 7)
         product(3)
         gelu(4)
         gelu(5)
-        turn(0, 2, 6, on_scalar)
+        turn(0, 2, 6)
         up(6, 1, (0, 4))
         up(7, 1, (1, 5))
         up(6, 0)
         weave(0, 7, 8)
         quantize_x(0, 7, 8)
         up(7, 0)
+
         gelu(6)
         product(4)
-        quantize_h(0, 2, "x_bf07")
+        quantize_h(0, 2, on="x_bf07")
         gelu(7)
-        turn(2, 4, 0, on_scalar)
+        turn(2, 4, 0)
         product(5)
-        turn(4, 6, 1, on_scalar)
+        turn(4, 6, 1)
         product(6)
         product(7)
-        turn(6, 7, 4, on_scalar)
-        turn(7, 8, 5, on_scalar)
+        turn(6, 7, 4)
+        turn(7, 8, 5)
         quantize_h(2, 4)
         down(0, [(0, 2), (2, 4)], 7, on_scalar)
         down(1, [(0, 2), (2, 4)], 6, on_scalar)
@@ -333,7 +331,11 @@ def tile_moe_pre_glu_gelu_kernel(
             return y_sb[r][:].indirect(pos_sb[which][:, lo // LIST_ROWS : hi // LIST_ROWS])
 
         half = T // 2
-        first = {(r, lo): keep.tile([P, half], F32, name=f"first{r}{lo}", align_bytes=64) for r in range(ROW_TILES) for lo in (0, half)}
+        first = {
+            (r, lo): keep.tile([P, half], F32, name=f"first{r}{lo}", align_bytes=64)
+            for r in range(ROW_TILES)
+            for lo in (0, half)
+        }
         for r, lo in first:
             if (r, lo) == (0, half):
                 nc.vector.tensor_copy(first[r, lo][:], fetch(r, 0, lo, lo + half))
@@ -345,6 +347,6 @@ def tile_moe_pre_glu_gelu_kernel(
             cuts = (0, half, T - P, T) if r == ROW_TILES - 1 else (0, half, T)
             for lo, hi in zip(cuts, cuts[1:]):
                 total = keep.tile([P, hi - lo], F32, name=f"total{r}{lo}", align_bytes=64)
-                start = lo // half * half
-                nc.vector.tensor_tensor(total[:], fetch(r, 1, lo, hi), first[r, start][:, lo - start : hi - start], ADD)
+                base = lo // half * half
+                nc.vector.tensor_tensor(total[:], fetch(r, 1, lo, hi), first[r, base][:, lo - base : hi - base], ADD)
                 nc.sync.dma_start(out[r * P : (r + 1) * P, lo:hi], total[:])

@@ -13,7 +13,6 @@ LIST_ROWS = 16
 RUN = 8
 SPARE = 1
 GATED = 2
-SHARED = 2
 
 WEIGHTS = E * (2 * K * H + H * N)
 FLOPS = 2 * S * (2 * K * H + H * N)
@@ -138,7 +137,7 @@ def tile_moe_pre_glu_gelu_kernel(
             for j in range(a, z):
                 gathered[s, j] = (rows, a)
             for t in range(PACK):
-                if t < PACK - shared:
+                if t >= shared:
                     nc.scalar.activation(rows[:, t, :], look_up(s, t, a, z), COPY)
                 else:
                     nc.vector.tensor_copy(rows[:, t, :], look_up(s, t, a, z))
@@ -255,7 +254,7 @@ def tile_moe_pre_glu_gelu_kernel(
         on_scalar, on_vector = nc.scalar.copy, nc.vector.tensor_copy
 
         gather(1, 2, 6)
-        gather(1, 6, 8)
+        gather(1, 6, 8, shared=1)
         gather(0, 2, 4)
         first_tiles()
         quantize_first(0)
@@ -266,7 +265,7 @@ def tile_moe_pre_glu_gelu_kernel(
             up(j, 1, (2 * j, 2 * j + 1))
             up(j, 0)
             gelu(j)
-        gather(0, 6, 7, on="x_codes_first1")
+        gather(0, 6, 8, on="x_codes_first1")
         weave(1, 4, 6)
         quantize_x(1, 2, 4)
         weave(0, 2, 3)
@@ -290,9 +289,10 @@ def tile_moe_pre_glu_gelu_kernel(
         up(5, 1, (1, 3))
         up(5, 0)
         weave(0, 6, 7)
-        product(2)
-        gather(0, 7, 8, on="x_codes03", shared=SHARED)
+        weave(0, 7, 8)
         quantize_x(0, 6, 7)
+        product(2)
+        quantize_x(0, 7, 8)
         product(3)
         gelu(4)
         gelu(5)
@@ -300,8 +300,6 @@ def tile_moe_pre_glu_gelu_kernel(
         up(6, 1, (0, 4))
         up(7, 1, (1, 5))
         up(6, 0)
-        weave(0, 7, 8)
-        quantize_x(0, 7, 8)
         up(7, 0)
 
         gelu(6)

@@ -268,12 +268,10 @@ def tile_moe_pre_glu_gelu_kernel(
         gather(0, 6, 8, on="x_codes_first1")
         weave(1, 4, 6)
         quantize_x(1, 2, 4)
-        weave(0, 2, 3)
+        weave(0, 2, 4)
         quantize_x(1, 4, 6)
-        weave(0, 3, 4)
-        quantize_x(0, 2, 3)
         weave(1, 6, 8)
-        quantize_x(0, 3, 4)
+        quantize_x(0, 2, 4)
         for j in range(2, 4):
             up(j, 1, (2 * j, 2 * j + 1))
             up(j, 0)
@@ -288,11 +286,9 @@ def tile_moe_pre_glu_gelu_kernel(
         product(1)
         up(5, 1, (1, 3))
         up(5, 0)
-        weave(0, 6, 7)
-        weave(0, 7, 8)
-        quantize_x(0, 6, 7)
+        weave(0, 6, 8)
         product(2)
-        quantize_x(0, 7, 8)
+        quantize_x(0, 6, 8)
         product(3)
         gelu(4)
         gelu(5)
@@ -304,7 +300,7 @@ def tile_moe_pre_glu_gelu_kernel(
 
         gelu(6)
         product(4)
-        quantize_h(0, 2, on="x_bf07")
+        quantize_h(0, 2, on="x_bf06")
         gelu(7)
         turn(2, 4, 0)
         product(5)

@@ -84,11 +84,9 @@ def tile_moe_pre_glu_gelu_kernel(
             rows = xT[s * P * PACK : (s + 1) * P * PACK, :].rearrange("(p t) c -> p t c", t=PACK)
             nc.sync.dma_start(window[s][t][:, :T], rows[:, t, :])
 
-        def load_scales(scales_sb, scales, quad):
+        def load_scales(scales_sb, scales, first):
             rows = scales.rearrange("e s q i -> q (e s) i")
-            nc.sync.dma_start(
-                scales_sb[32 * quad : 32 * quad + 4].bitcast(I32), rows[4 * quad : 4 * quad + 4].bitcast(I32)
-            )
+            nc.sync.dma_start(scales_sb[first:P:32].bitcast(I32), rows[first:16:4].bitcast(I32))
 
         def load_up(m, e, lo=0, hi=PASSES):
             words = (w1_words, w3_words)[m][e, lo:hi].rearrange("s p b -> p s b")

from contextlib import ExitStack

import concourse.mybir as mybir
from concourse.masks import make_identity

K, T, E, C, H, N = 1024, 512, 4, 256, 512, 384
S = E * C
P = 128
PACK = 4
PASSES = K // (P * PACK)
ROW_TILES = N // P
LIST_ROWS = 16
RUN = 8
SPARE = 1
GATED = 2

WEIGHTS = E * (2 * K * H + H * N)
FLOPS = 2 * S * (2 * K * H + H * N)
BYTES = 4 * K * T + WEIGHTS // 2 + WEIGHTS // 32 + 4 * S + 2 * P * (S + 2 * T) // LIST_ROWS + 4 * N * T

F32 = mybir.dt.float32
BF16 = mybir.dt.bfloat16
I32 = mybir.dt.int32
U32 = mybir.dt.uint32
U16 = mybir.dt.uint16
U8 = mybir.dt.uint8
FP8X4 = mybir.dt.float8_e4m3fn_x4
FP4X4 = mybir.dt.float4_e2m1fn_x4
MULT = mybir.AluOpType.mult
ADD = mybir.AluOpType.add
GELU = mybir.ActivationFunctionType.Gelu_apprx_tanh
COPY = mybir.ActivationFunctionType.Copy

W1, W3 = 0, 1


def tile_moe_pre_glu_gelu_kernel(
    tc, xT, w1_words, w1_scales, w3_words, w3_scales, w2_words, w2_scales, gate, offs, pos1, pos2, out
):
    nc = tc.nc
    with ExitStack() as ctx:
        keep = ctx.enter_context(tc.tile_pool(name="keep", bufs=1))
        psum = ctx.enter_context(tc.psum_pool(name="psum", bufs=1))

        offs_sb = keep.tile([P, S // LIST_ROWS], U16, name="offs_sb")
        pos_sb = [keep.tile([P, T // LIST_ROWS], U16, name=f"pos_sb{r}") for r in range(2)]
        gate_cuts = (0, GATED * P, S)
        gate_sb = [
            keep.tile([P, hi - lo], F32, name=f"gate_sb{lo}", align_bytes=64)
            for lo, hi in zip(gate_cuts, gate_cuts[1:])
        ]
        window = [
            [keep.tile([P, T + SPARE], F32, name=f"window{s}{t}", align_bytes=64) for t in range(PACK)]
            for s in range(PASSES)
        ]
        up_words = [
            [keep.tile([P, PASSES, 2 * H], U8, name=f"up_words{m}{e}", align_bytes=64) for e in range(E)]
            for m in (W1, W3)
        ]
        up_scales = [keep.tile([P, E * PASSES, H], U8, name=f"up_scales{m}", align_bytes=64) for m in (W1, W3)]
        down_words = keep.tile([P, E, 2 * N], U8, name="down_words", align_bytes=64)
        down_scales = keep.tile([P, E, N], U8, name="down_scales", align_bytes=64)
        x_scales = [keep.tile([P, S], U8, name=f"x_scales{s}", align_bytes=64) for s in range(PASSES)]
        h_scales = keep.tile([P, S], U8, name="h_scales", align_bytes=64)
        y_sb = [keep.tile([P, S], F32, name=f"y_sb{r}", align_bytes=64) for r in range(ROW_TILES)]
        ident = keep.tile([P, P], F32, name="ident")

        zero = keep.tile([P, 1], F32, name="zero")
        no_bias = keep.tile([P, 1], F32, name="no_bias")
        nc.gpsimd.memset(zero[:], 0.0)
        nc.scalar.activation(no_bias[:], zero[:], GELU)
        for scales_sb in up_scales:
            nc.vector.memset(scales_sb[:].rearrange("p a b -> p (a b)").bitcast(U32), 0)
        for pass_windows in window:
            for one in pass_windows:
                nc.gpsimd.memset(one[:, T:], 0.0)
        nc.gpsimd.memset(down_scales[:].rearrange("p a b -> p (a b)").bitcast(U32), 0)
        make_identity(nc, ident[:])

        def load_gate(piece):
            nc.sync.dma_start(gate_sb[piece][:], gate[0:P, gate_cuts[piece] : gate_cuts[piece + 1]])

        def load_window(s, t):
            rows = xT[s * P * PACK : (s + 1) * P * PACK, :].rearrange("(p t) c -> p t c", t=PACK)
            nc.sync.dma_start(window[s][t][:, :T], rows[:, t, :])

        def load_scales(scales_sb, scales, first):
            rows = scales.rearrange("e s q i -> q (e s) i")
            nc.sync.dma_start(scales_sb[first:P:32].bitcast(I32), rows[first:16:4].bitcast(I32))

        def load_up(m, e, lo=0, hi=PASSES):
            words = (w1_words, w3_words)[m][e, lo:hi].rearrange("s p b -> p s b")
            nc.sync.dma_start(up_words[m][e][:, lo:hi, :].bitcast(I32), words.bitcast(I32))

        load_window(1, 0)
        nc.sync.dma_start(offs_sb[:], offs)
        load_gate(0)
        for t in range(1, PACK):
            load_window(1, t)
        for t in range(PACK):
            load_window(0, t)
        load_gate(1)
        for m, scales in ((W1, w1_scales), (W3, w3_scales)):
            load_up(m, 0)
            for quad in range(4):
                load_scales(up_scales[m], scales, quad)
        for m in (W1, W3):
            load_up(m, 1)
        for e, s, order in ((2, 1, (W1, W3)), (2, 0, (W1, W3)), (3, 1, (W3, W1)), (3, 0, (W1, W3))):
            for m in order:
                load_up(m, e, s, s + 1)
        nc.sync.dma_start(pos_sb[0][:], pos1)
        nc.sync.dma_start(pos_sb[1][:], pos2)
        for quad in range(4):
            load_scales(down_scales, w2_scales, quad)
        nc.sync.dma_start(down_words[:].bitcast(I32), w2_words.rearrange("e s p b -> p (e s) b").bitcast(I32))

        gathered, first_bf, x_bf, x_codes, x_plane = {}, {}, {}, {}, {}
        up_sums, act, h_rows, h_bf, h_codes = {}, {}, {}, {}, {}

        def bank(b, shape, name):
            return psum.tile(shape, F32, name=name, tag=f"bank{b}")

        def gate_of(a, z):
            piece = int(a >= GATED)
            return gate_sb[piece][:, a * P - gate_cuts[piece] : z * P - gate_cuts[piece]]

        def look_up(s, t, a, z):
            return window[s][t][:].indirect(offs_sb[:, a * P // LIST_ROWS : z * P // LIST_ROWS])

        def gather(s, a, z, on=None, shared=0):
            name = f"gathered{s}{a}"
            held = keep.tile([P, PACK * (z - a) * P], F32, name=name, tag=on or name, align_bytes=64)
            rows = held[:].rearrange("p (t c) -> p t c", t=PACK)
            for j in range(a, z):
                gathered[s, j] = (rows, a)
            for t in range(PACK):
                if t >= shared:
                    nc.scalar.activation(rows[:, t, :], look_up(s, t, a, z), COPY)
                else:
                    nc.vector.tensor_copy(rows[:, t, :], look_up(s, t, a, z))

        def weave(s, a, z):
            rows, start = gathered[s, a]
            name = f"x_bf{s}{a}"
            x_bf[s, a] = keep.tile([P, (z - a) * P * PACK], BF16, name=name, tag=name, align_bytes=64)
            weight = gate_of(a, z).rearrange("p (c i) -> p c i", i=RUN).unsqueeze(2)
            nc.vector.tensor_tensor(
                x_bf[s, a][:].rearrange("p (c i t) -> p c t i", i=RUN, t=PACK),
                rows[:, :, (a - start) * P : (z - start) * P].rearrange("p t (c i) -> p c t i", i=RUN),
                weight.to_broadcast([P, (z - a) * P // RUN, PACK, RUN]),
                MULT,
            )

        def first_tiles():
            width = GATED * P
            held = keep.tile([P, PASSES * PACK * width], F32, name="gathered_first", align_bytes=64)
            rows = held[:].rearrange("p (s t c) -> p s t c", s=PASSES, t=PACK)
            for s in (1, 0):
                for t in range(PACK):
                    cuts = range(GATED + 1) if (s, t) == (0, PACK - 1) else (0, GATED)
                    for a, z in zip(cuts, cuts[1:]):
                        nc.vector.tensor_tensor(rows[:, s, t, a * P : z * P], look_up(s, t, a, z), gate_of(a, z), MULT)
            for j in range(GATED):
                name = f"x_bf_first{j}"
                woven = keep.tile([P, PASSES * P * PACK], BF16, name=name, tag=name, align_bytes=64)
                nc.vector.tensor_copy(
                    woven[:].rearrange("p (s c i t) -> p s c t i", s=PASSES, i=RUN, t=PACK),
                    rows[:, :, :, j * P : (j + 1) * P].rearrange("p s t (c i) -> p s c t i", i=RUN),
                )
                first_bf[j] = woven

        def quantize_first(j):
            name = f"x_codes_first{j}"
            codes = keep.tile([P, PASSES * P], U32, name=name, tag=name, align_bytes=64)
            scales = keep.tile([P, PASSES * P], U8, name=f"x_scales_first{j}", align_bytes=64)
            for s in range(PASSES):
                x_codes[s, j] = codes[:, s * P : (s + 1) * P]
                x_plane[s, j] = scales[:, s * P : (s + 1) * P]
            nc.vector.quantize_mx(out=codes[:].bitcast(FP8X4), scales=scales[:], in_=first_bf[j][:])

        def quantize_x(s, a, z):
            name = f"x_codes{s}{a}"
            codes = keep.tile([P, (z - a) * P], U32, name=name, tag=name, align_bytes=64)
            for j in range(a, z):
                x_codes[s, j] = codes[:, (j - a) * P : (j - a + 1) * P]
                x_plane[s, j] = x_scales[s][:, j * P : (j + 1) * P]
            nc.vector.quantize_mx(
                out=codes[:].bitcast(FP8X4), scales=x_scales[s][:, a * P : z * P], in_=x_bf[s, a][:]
            )

        def by_pair(sums):
            return sums[:].rearrange("q (p u v) -> q u p v", u=2, v=2)

        def up(j, s, banks=None):
            e = j * P // C
            for m in (W1, W3):
                if banks:
                    up_sums[j, m] = bank(banks[m], [P, H], ("w1_sums", "w3_sums")[m])
                nc.tensor.matmul_mx(
                    out=up_sums[j, m][:],
                    lhsT=x_codes[s, j].bitcast(FP8X4),
                    lhsT_scale=x_plane[s, j],
                    rhs=up_words[m][e][:, s, :].bitcast(FP4X4),
                    rhs_scale=up_scales[m][:, e * PASSES + s, :],
                    start=banks is not None,
                    stop=banks is None,
                )

        def gelu(j):
            act[j] = keep.tile([P, 2, P, 2], F32, name=f"act{j}", align_bytes=64)
            nc.scalar.activation(act[j][:], by_pair(up_sums[j, W1]), GELU, bias=no_bias[:])

        def product(j):
            h_rows[j] = keep.tile([P, H], BF16, name=f"h_rows{j}", align_bytes=64)
            target = h_rows[j][:].rearrange("q (u p v) -> q u p v", u=2, v=2)
            nc.vector.tensor_tensor(target, act[j][:], by_pair(up_sums[j, W3]), MULT)

        def turn(a, z, b):
            turned = bank(b, [P, z - a, 2, P], "turned")
            for j in range(a, z):
                words = h_rows[j][:].bitcast(F32)
                for u in range(2):
                    nc.tensor.transpose(turned[:, j - a, u, :], words[:, u * P : (u + 1) * P], ident[:])
            h_bf[a] = keep.tile([P, (z - a) * H], BF16, name=f"h_bf{a}", align_bytes=64)
            words = h_bf[a][:].bitcast(F32).rearrange("p (j r u) -> p j r u", j=z - a, u=2)
            nc.scalar.copy(words, turned[:].rearrange("p j u r -> p j r u"))

        def quantize_h(a, z, on=None):
            name = f"h_codes{a}"
            h_codes[a] = keep.tile([P, (z - a) * P], U32, name=name, tag=on or name, align_bytes=64)
            nc.vector.quantize_mx(
                out=h_codes[a][:].bitcast(FP8X4), scales=h_scales[:, a * P : z * P], in_=h_bf[a][:]
            )

        def down(r, pieces, b, copy):
            j0, j1 = pieces[0][0], pieces[-1][1]
            sums = bank(b, [P, (j1 - j0) * P], "y_sums")
            for a, z in pieces:
                e = a * P // C
                nc.tensor.matmul_mx(
                    out=sums[:, (a - j0) * P : (z - j0) * P],
                    lhsT=down_words[:, e, 2 * r * P : 2 * (r + 1) * P].bitcast(FP4X4),
                    lhsT_scale=down_scales[:, e, r * P : (r + 1) * P],
                    rhs=h_codes[a][:].bitcast(FP8X4),
                    rhs_scale=h_scales[:, a * P : z * P],
                    start=True,
                    stop=True,
                )
            copy(y_sb[r][:, j0 * P : j1 * P], sums[:])

        on_scalar, on_vector = nc.scalar.copy, nc.vector.tensor_copy

        gather(1, 2, 6)
        gather(1, 6, 8, shared=1)
        gather(0, 2, 4)
        first_tiles()
        quantize_first(0)
        quantize_first(1)
        weave(1, 2, 4)
        gather(0, 4, 6, on="x_bf_first0")
        for j in range(2):
            up(j, 1, (2 * j, 2 * j + 1))
            up(j, 0)
            gelu(j)
        gather(0, 6, 8, on="x_codes_first1")
        weave(1, 4, 6)
        quantize_x(1, 2, 4)
        weave(0, 2, 4)
        quantize_x(1, 4, 6)
        weave(1, 6, 8)
        quantize_x(0, 2, 4)
        for j in range(2, 4):
            up(j, 1, (2 * j, 2 * j + 1))
            up(j, 0)
            gelu(j)

        quantize_x(1, 6, 8)
        weave(0, 4, 6)
        product(0)
        quantize_x(0, 4, 6)
        up(4, 1, (0, 2))
        up(4, 0)
        product(1)
        up(5, 1, (1, 3))
        up(5, 0)
        weave(0, 6, 8)
        product(2)
        quantize_x(0, 6, 8)
        product(3)
        gelu(4)
        gelu(5)
        turn(0, 2, 6)
        up(6, 1, (0, 4))
        up(7, 1, (1, 5))
        up(6, 0)
        up(7, 0)

        gelu(6)
        product(4)
        quantize_h(0, 2, on="x_bf06")
        gelu(7)
        turn(2, 4, 0)
        product(5)
        turn(4, 6, 1)
        product(6)
        product(7)
        turn(6, 7, 4)
        turn(7, 8, 5)
        quantize_h(2, 4)
        down(0, [(0, 2), (2, 4)], 7, on_scalar)
        down(1, [(0, 2), (2, 4)], 6, on_scalar)
        quantize_h(4, 6)
        quantize_h(6, 7)
        down(0, [(4, 6), (6, 7)], 2, on_vector)
        quantize_h(7, 8)
        down(0, [(7, 8)], 3, on_vector)
        down(1, [(4, 6), (6, 7)], 1, on_scalar)
        down(1, [(7, 8)], 4, on_scalar)
        down(2, [(0, 2), (2, 4)], 0, on_vector)

        def fetch(r, which, lo, hi):
            return y_sb[r][:].indirect(pos_sb[which][:, lo // LIST_ROWS : hi // LIST_ROWS])

        half = T // 2
        first = {
            (r, lo): keep.tile([P, half], F32, name=f"first{r}{lo}", align_bytes=64)
            for r in range(ROW_TILES)
            for lo in (0, half)
        }
        for r, lo in first:
            if (r, lo) == (0, half):
                nc.vector.tensor_copy(first[r, lo][:], fetch(r, 0, lo, lo + half))
            else:
                nc.scalar.activation(first[r, lo][:], fetch(r, 0, lo, lo + half), COPY)
            if (r, lo) == (1, 0):
                down(2, [(4, 6), (6, 7), (7, 8)], 5, on_scalar)
        for r in range(ROW_TILES):
            cuts = (0, half, T - P, T) if r == ROW_TILES - 1 else (0, half, T)
            for lo, hi in zip(cuts, cuts[1:]):
                total = keep.tile([P, hi - lo], F32, name=f"total{r}{lo}", align_bytes=64)
                base = lo // half * half
                nc.vector.tensor_tensor(total[:], fetch(r, 1, lo, hi), first[r, base][:, lo - base : hi - base], ADD)
                nc.sync.dma_start(out[r * P : (r + 1) * P, lo:hi], total[:])
